import numpy as np
import ml_dtypes


def mxq(x, axis, fmt="e4m3"):
    dtype, down = {"e4m3": (ml_dtypes.float8_e4m3fn, 7), "e5m2": (ml_dtypes.float8_e5m2, 14)}[fmt]
    v = np.moveaxis(np.asarray(x, np.float32).astype(ml_dtypes.bfloat16).astype(np.float64), axis, -1)
    blocks = v.reshape(v.shape[:-1] + (-1, 32))
    amax = np.abs(blocks).max(-1, keepdims=True)
    byte = np.maximum(np.where(amax > 0, np.frexp(amax)[1] - 1 + 127, 0) - down, 1)
    scale = np.exp2(byte - 127.0)
    codes = (blocks / scale).astype(np.float32).astype(dtype).astype(np.float64)
    return np.moveaxis((codes * scale).reshape(v.shape), -1, axis)


WIDE = False


def mx_kscale(k):
    if not WIDE:
        return np.ones(k)
    levels = np.array([10, -10, 5, -5, 0])
    if k % 512:
        return np.exp2(np.random.permutation(np.resize(levels, k // 32))).repeat(32)
    a = np.empty((k // 512, 16))
    for p in range(k // 512):
        a[p, :8] = np.random.permutation(np.resize(levels, 8))
        for g in range(8):
            far = levels[np.abs(levels - a[p, g]) >= 10]
            a[p, g + 8] = far[np.random.randint(len(far))]
    return np.exp2(a.ravel()).repeat(32)


def f64(x):
    return np.asarray(x).astype(np.float64)


def striped(idx):
    return np.tile(idx.reshape(-1, 16).T, (8, 1)).astype(np.uint16)


def unstriped(offs):
    return offs[:16].T.reshape(-1).astype(np.int64)


K, T, E, C, N = 512, 512, 4, 256, 1536


def by_expert(wq, xq):
    return np.concatenate([wq[e].T @ xq[:, e * C:(e + 1) * C] for e in range(E)], axis=1)


def setup_inputs():
    n = np.random.standard_normal
    s = mx_kscale(N)[:, None]
    first = np.random.permutation(np.repeat(np.arange(E), T // E))
    second = (first + 1 + np.random.permutation(np.repeat(np.arange(E - 1), -(-T // (E - 1)))[:T])) % E
    while np.bincount(second, minlength=E).max() != T // E:
        load = np.bincount(second, minlength=E); hi, lo = int(load.argmax()), int(load.argmin())
        t = np.flatnonzero((second == hi) & (first != lo))[0]; second[t] = lo
    slot_token = np.empty(E * C, np.int64); pos = np.empty((2, T), np.int64); fill = np.zeros(E, np.int64)
    place = np.stack([np.random.permutation(C) for _ in range(E)])
    for r, deal in enumerate((first, second)):
        for t in np.random.permutation(T):
            e = deal[t]; j = e * C + place[e, fill[e]]; fill[e] += 1; slot_token[j] = t; pos[r, t] = j
    g = np.random.uniform(0.2, 0.8, T)
    w_slot = np.empty(E * C); w_slot[pos[0]] = g; w_slot[pos[1]] = 1.0 - g
    return {
        "dyT": (n((N, T)) * s).astype(np.float32),
        "w": (n((E, N, K)) / np.sqrt(N) / s[None]).astype(np.float32),
        "gate": np.tile(w_slot, (N, 1)).astype(np.float32),
        "offs": striped(slot_token),
        "pos1": striped(pos[0]),
        "pos2": striped(pos[1]),
    }


def reference(dyT, w, gate, offs, pos1, pos2):
    idx = unstriped(offs)
    gq = mxq(f64(gate) * f64(dyT)[:, idx], 0, "e4m3")
    dx = by_expert(mxq(f64(w), 1, "e4m3"), gq)
    return dx[:, unstriped(pos1)] + dx[:, unstriped(pos2)]

@@ -1,0 +1,257 @@
+from contextlib import ExitStack
+
+import concourse.mybir as mybir
+
+K, T, E, C, N = 512, 512, 4, 256, 1536
+S = E * C
+P = 128
+PACK = 4
+PASS = P * PACK
+NPASS = N // PASS
+HALF = 512
+COLS = 256
+
+F32 = mybir.dt.float32
+BF16 = mybir.dt.bfloat16
+U32 = mybir.dt.uint32
+U16 = mybir.dt.uint16
+U8 = mybir.dt.uint8
+FP8X4 = mybir.dt.float8_e4m3fn_x4
+ADD = mybir.AluOpType.add
+MULT = mybir.AluOpType.mult
+
+FLOPS = 2 * K * N * S
+BYTES = 4 * (N * T + E * N * K + S + K * T) + 2 * 128 * (64 + 32 + 32)
+
+UNITS = ((0, 0, 2), (1, 0, 2), (2, 0, 2))
+NFULL = 6
+
+
+def tile_moe_bdx_lin_none_kernel(tc, dyT, w, gate, offs, pos1, pos2, out):
+    nc = tc.nc
+    with ExitStack() as ctx:
+        held = ctx.enter_context(tc.tile_pool(name="held", bufs=1))
+        wraws = ctx.enter_context(tc.tile_pool(name="wraws", bufs=7))
+        wbfs = ctx.enter_context(tc.tile_pool(name="wbfs", bufs=6))
+        gs = ctx.enter_context(tc.tile_pool(name="gs", bufs=2))
+        psum = ctx.enter_context(tc.psum_pool(name="psum", bufs=8))
+
+        offs_sb = held.tile([P, S // 16], U16, name="offs_sb")
+        pos1_sb = held.tile([P, T // 16], U16, name="pos1_sb")
+        pos2_sb = held.tile([P, T // 16], U16, name="pos2_sb")
+        gate_sb = held.tile([P, S], F32, name="gate_sb")
+        gcodes = [[held.tile([P, HALF], U32, name=f"gcodes{c}_{h}", align_bytes=64) for h in range(2)] for c in range(NPASS)]
+        gscales = [[held.tile([P, HALF], U8, name=f"gscales{c}_{h}", align_bytes=64) for h in range(2)] for c in range(NPASS)]
+        wins = {}
+
+        def load_win(c, j):
+            wins[c, j] = gs.tile([P, S + 8], F32, name=f"win{j}")
+            nc.gpsimd.memset(wins[c, j][:, T : S + 8], 0.0)
+            rows = dyT[c * PASS : (c + 1) * PASS, :].rearrange("(p j) t -> p j t", j=PACK)
+            nc.sync.dma_start(wins[c, j][:, 0:T], rows[:, j, :])
+
+        def load_gate(h):
+            nc.sync.dma_start(gate_sb[:, h * HALF : (h + 1) * HALF], gate[0:P, h * HALF : (h + 1) * HALF])
+
+        wlist = [(e, c) for e in range(E) for c in range(NPASS)]
+        wraw = {}
+
+        def load_w(i, half=None):
+            e, c = wlist[i]
+            if i not in wraw:
+                wraw[i] = wraws.tile([P, PACK, K], F32, name="wraw")
+            rows = w[e, c * PASS : (c + 1) * PASS, :].rearrange("(p j) k -> p j k", j=PACK)
+            cols = slice(0, K) if half is None else slice(half * COLS, (half + 1) * COLS)
+            nc.sync.dma_start(wraw[i][:, :, cols], rows[:, :, cols])
+
+        def interleave(copy, dst, src):
+            copy(
+                dst.rearrange("p (c i t) -> p c t i", i=4, t=PACK),
+                src.rearrange("p t (c i) -> p c t i", i=4),
+            )
+
+        gfs, gbs, wbs, accs, dxs, rs, codes, scales = {}, {}, {}, {}, {}, {}, {}, {}
+        scopy, vcopy = nc.scalar.copy, nc.vector.tensor_copy
+
+        def G(u, j, h=None):
+            if u not in gfs:
+                gfs[u] = gs.tile([P, PACK, S], F32, name="gf")
+            lo, hi = (0, S) if h is None else (h * HALF, (h + 1) * HALF)
+            nc.vector.tensor_tensor(gfs[u][:, j, lo:hi], wins[u, j][:].indirect(offs_sb[:, lo // 16 : hi // 16]), gate_sb[:, lo:hi], MULT)
+
+        def GI(u, p=0):
+            gbs[u, p] = wbfs.tile([P, PACK * HALF], BF16, name="wb", align_bytes=64)
+            interleave(scopy, gbs[u, p][:], gfs[u][:, :, p * HALF : (p + 1) * HALF])
+
+        def GQ(u, p=0):
+            c, h, n = UNITS[u]
+            nc.vector.quantize_mx(out=gcodes[c][h + p][:].bitcast(FP8X4), scales=gscales[c][h + p][:], in_=gbs[u, p][:])
+
+        def new_wb(key):
+            wbs[key] = wbfs.tile([P, PACK * 2 * COLS], BF16, name="wb", align_bytes=64)
+            codes[key] = held.tile([P, 2 * COLS], U32, name=f"codes_{key}", align_bytes=64)
+            scales[key] = held.tile([P, 2 * COLS], U8, name=f"scales_{key}", align_bytes=64)
+
+        def F(i, copy=scopy, halves=False):
+            new_wb(f"F{i}")
+            wb = wbs[f"F{i}"]
+            if halves:
+                for h in range(2):
+                    interleave(copy, wb[:, h * PACK * COLS : (h + 1) * PACK * COLS], wraw[i][:, :, h * COLS : (h + 1) * COLS])
+            else:
+                interleave(copy, wb[:], wraw[i][:])
+
+        def AB(half, i, copy=scopy):
+            r = i % 2
+            key = f"{'AB'[half]}{i - r}"
+            if key not in wbs:
+                new_wb(key)
+            interleave(copy, wbs[key][:, r * PACK * COLS : (r + 1) * PACK * COLS], wraw[i][:, :, half * COLS : (half + 1) * COLS])
+
+        def WQ(key):
+            nc.vector.quantize_mx(out=codes[key][:].bitcast(FP8X4), scales=scales[key][:], in_=wbs[key][:])
+
+        def MM(kt, h, lo=0, hi=6):
+            if lo == 0:
+                accs[kt, h] = psum.tile([P, HALF], F32, name="acc")
+            for p in range(lo, hi):
+                u, c = divmod(p, NPASS)
+                scols = slice(u * C, (u + 1) * C)
+                i = 2 * h * NPASS + p
+                half, inner = divmod(kt, 2)
+                if i < NFULL:
+                    key, k0 = f"F{i}", kt * P
+                else:
+                    key, k0 = f"{'AB'[half]}{i - i % 2}", (i % 2) * COLS + inner * P
+                nc.tensor.matmul_mx(
+                    out=accs[kt, h][:, scols],
+                    lhsT=codes[key][:, k0 : k0 + P].bitcast(FP8X4),
+                    lhsT_scale=scales[key][:, k0 : k0 + P],
+                    rhs=gcodes[c][h][:, scols].bitcast(FP8X4),
+                    rhs_scale=gscales[c][h][:, scols],
+                    start=(c == 0),
+                    stop=(c == NPASS - 1),
+                )
+
+        def PC(kt, h):
+            if kt not in dxs:
+                dxs[kt] = held.tile([P, S], F32, name=f"dx{kt}")
+            scopy(dxs[kt][:, h * HALF : (h + 1) * HALF], accs[kt, h][:])
+
+        def PO(kt, r):
+            rs[kt, r] = gs.tile([P, T], F32, name=f"r{r}")
+            vcopy(rs[kt, r][:], dxs[kt][:].indirect((pos1_sb, pos2_sb)[r][:]))
+
+        def AD(kt, engine):
+            res = gs.tile([P, T], F32, name="res")
+            engine.tensor_tensor(res[:], rs[kt, 0][:], rs[kt, 1][:], ADD)
+            nc.sync.dma_start(out[kt * P : (kt + 1) * P, :], res[:])
+
+        nc.sync.dma_start(offs_sb[:], offs)
+        load_win(0, 0)
+        load_gate(0)
+        load_gate(1)
+        load_win(0, 1)
+        load_w(0, 0)
+        load_win(0, 2)
+        load_w(0, 1)
+        load_win(0, 3)
+        load_w(1)
+        load_win(1, 0)
+        load_w(2)
+        load_win(1, 1)
+        load_w(3)
+        load_win(1, 2)
+        load_w(4)
+        load_win(1, 3)
+        load_w(5)
+        nc.sync.dma_start(pos1_sb[:], pos1)
+        nc.sync.dma_start(pos2_sb[:], pos2)
+        load_win(2, 0)
+        load_w(6)
+        load_win(2, 1)
+        load_w(7)
+        load_win(2, 2)
+        load_w(8)
+        load_win(2, 3)
+        for i in range(9, 12): load_w(i)
+        G(0, 0, 0)
+        G(0, 0, 1)
+        G(0, 1)
+        F(0, halves=True)
+        F(1)
+        G(0, 2)
+        G(0, 3)
+        GI(0, 0)
+        F(2)
+        F(3)
+        G(1, 0)
+        WQ("F0")
+        F(4)
+        G(1, 1)
+        WQ("F1")
+        F(5)
+        G(1, 2)
+        GQ(0, 0)
+        WQ("F2")
+        GI(0, 1)
+        G(1, 3)
+        WQ("F3")
+        AB(0, 6)
+        AB(0, 7)
+        G(2, 0)
+        WQ("F4")
+        GI(1, 0)
+        GI(1, 1)
+        G(2, 1)
+        WQ("F5")
+        GQ(0, 1)
+        AB(0, 8)
+        AB(0, 9)
+        G(2, 2)
+        WQ("A6")
+        GQ(1, 0)
+        AB(0, 10)
+        AB(0, 11)
+        G(2, 3)
+        GQ(1, 1)
+        GI(2, 0)
+        WQ("A8")
+        WQ("A10")
+        GI(2, 1)
+        GQ(2, 0)
+        for kt in range(4): MM(kt, 0)
+        AB(1, 10, vcopy)
+        AB(1, 11, vcopy)
+        AB(1, 8)
+        AB(1, 6, vcopy)
+        PC(0, 0)
+        GQ(2, 1)
+        AB(1, 9)
+        WQ("B10")
+        AB(1, 7, vcopy)
+        WQ("B6")
+        MM(0, 1)
+        MM(1, 1)
+        PC(1, 0)
+        PC(0, 1)
+        PC(1, 1)
+        WQ("B8")
+        PO(0, 0)
+        PO(0, 1)
+        MM(2, 1)
+        MM(3, 1)
+        PC(2, 0)
+        PC(3, 0)
+        PO(1, 0)
+        PC(2, 1)
+        PC(3, 1)
+        PO(1, 1)
+        AD(0, nc.gpsimd)
+        PO(2, 0)
+        AD(1, nc.gpsimd)
+        PO(2, 1)
+        PO(3, 0)
+        AD(2, nc.gpsimd)
+        PO(3, 1)
+        AD(3, nc.vector)

@@ -9,7 +9,13 @@ PACK = 4
 PASS = P * PACK
 NPASS = N // PASS
 HALF = 512
-COLS = 256
+PAD = 8
+WRAW_BUFS = 3
+WB_BUFS = 9
+GF_BUFS = 3
+KB = 1024
+RES = 112 * KB
+GF_BYTES = 4 * PACK * HALF
 
 F32 = mybir.dt.float32
 BF16 = mybir.dt.bfloat16
@@ -23,45 +29,44 @@ MULT = mybir.AluOpType.mult
 FLOPS = 2 * K * N * S
 BYTES = 4 * (N * T + E * N * K + S + K * T) + 2 * 128 * (64 + 32 + 32)
 
-UNITS = ((0, 0, 2), (1, 0, 2), (2, 0, 2))
-NFULL = 6
-
 
 def tile_moe_bdx_lin_none_kernel(tc, dyT, w, gate, offs, pos1, pos2, out):
     nc = tc.nc
     with ExitStack() as ctx:
         held = ctx.enter_context(tc.tile_pool(name="held", bufs=1))
-        wraws = ctx.enter_context(tc.tile_pool(name="wraws", bufs=7))
-        wbfs = ctx.enter_context(tc.tile_pool(name="wbfs", bufs=6))
-        gs = ctx.enter_context(tc.tile_pool(name="gs", bufs=2))
-        psum = ctx.enter_context(tc.psum_pool(name="psum", bufs=8))
+        gs = ctx.enter_context(tc.tile_pool(name="gs", bufs=1))
+        psum = ctx.enter_context(tc.psum_pool(name="psum", bufs=1))
 
         offs_sb = held.tile([P, S // 16], U16, name="offs_sb")
         pos1_sb = held.tile([P, T // 16], U16, name="pos1_sb")
         pos2_sb = held.tile([P, T // 16], U16, name="pos2_sb")
-        gate_sb = held.tile([P, S], F32, name="gate_sb")
+        gate_sb = [held.tile([P, HALF], F32, name=f"gate_sb{h}") for h in range(2)]
         gcodes = [[held.tile([P, HALF], U32, name=f"gcodes{c}_{h}", align_bytes=64) for h in range(2)] for c in range(NPASS)]
         gscales = [[held.tile([P, HALF], U8, name=f"gscales{c}_{h}", align_bytes=64) for h in range(2)] for c in range(NPASS)]
-        wins = {}
+        wins = [[held.tile([P, T + PAD], F32, name=f"win{b}_{j}") for j in range(PACK)] for b in range(NPASS)]
+        for b in range(NPASS):
+            for j in range(PACK):
+                nc.gpsimd.memset(wins[b][j][:, T : T + PAD], 0.0)
 
         def load_win(c, j):
-            wins[c, j] = gs.tile([P, S + 8], F32, name=f"win{j}")
-            nc.gpsimd.memset(wins[c, j][:, T : S + 8], 0.0)
             rows = dyT[c * PASS : (c + 1) * PASS, :].rearrange("(p j) t -> p j t", j=PACK)
-            nc.sync.dma_start(wins[c, j][:, 0:T], rows[:, j, :])
+            nc.sync.dma_start(wins[c][j][:, 0:T], rows[:, j, :])
 
         def load_gate(h):
-            nc.sync.dma_start(gate_sb[:, h * HALF : (h + 1) * HALF], gate[0:P, h * HALF : (h + 1) * HALF])
+            nc.sync.dma_start(gate_sb[h][:], gate[0:P, h * HALF : (h + 1) * HALF])
 
-        wlist = [(e, c) for e in range(E) for c in range(NPASS)]
         wraw = {}
+        parts = [[gs.tile([P, 2, PACK, C], F32, name=f"part{b}_{q}", offset=(48 + 24 * b + 8 * q) * KB, align_bytes=64) for q in range(3)] for b in range(2)]
 
         def load_w(i, half=None):
-            e, c = wlist[i]
-            if i not in wraw:
-                wraw[i] = wraws.tile([P, PACK, K], F32, name="wraw")
+            e, c = divmod(i, NPASS)
             rows = w[e, c * PASS : (c + 1) * PASS, :].rearrange("(p j) k -> p j k", j=PACK)
-            cols = slice(0, K) if half is None else slice(half * COLS, (half + 1) * COLS)
+            cols = slice(0, K) if half is None else slice(half * C, (half + 1) * C)
+            if i >= 6:
+                nc.sync.dma_start(parts[half][(i - 6) // 2][:, i % 2, :, :], rows[:, :, cols])
+                return
+            if i not in wraw:
+                wraw[i] = gs.tile([P, PACK, K], F32, name=f"wraw{i}", offset=8 * i * KB, align_bytes=64)
             nc.sync.dma_start(wraw[i][:, :, cols], rows[:, :, cols])
 
         def interleave(copy, dst, src):
@@ -70,188 +75,217 @@ def tile_moe_bdx_lin_none_kernel(tc, dyT, w, gate, offs, pos1, pos2, out):
                 src.rearrange("p t (c i) -> p c t i", i=4),
             )
 
+        def interleave2(copy, dst, src):
+            copy(
+                dst.rearrange("p (r c i t) -> p r c t i", r=2, i=4, t=PACK),
+                src.rearrange("p r t (c i) -> p r c t i", i=4),
+            )
+
         gfs, gbs, wbs, accs, dxs, rs, codes, scales = {}, {}, {}, {}, {}, {}, {}, {}
         scopy, vcopy = nc.scalar.copy, nc.vector.tensor_copy
 
-        def G(u, j, h=None):
-            if u not in gfs:
-                gfs[u] = gs.tile([P, PACK, S], F32, name="gf")
-            lo, hi = (0, S) if h is None else (h * HALF, (h + 1) * HALF)
-            nc.vector.tensor_tensor(gfs[u][:, j, lo:hi], wins[u, j][:].indirect(offs_sb[:, lo // 16 : hi // 16]), gate_sb[:, lo:hi], MULT)
+        def G(c, h, kb):
+            gfs[c, h] = gs.tile([P, PACK, HALF], F32, name=f"gf{c}_{h}", offset=kb * KB)
+            for j in range(PACK):
+                nc.vector.tensor_tensor(gfs[c, h][:, j, :], wins[c][j][:].indirect(offs_sb[:, h * 32 : (h + 1) * 32]), gate_sb[h][:], MULT)
 
-        def GI(u, p=0):
-            gbs[u, p] = wbfs.tile([P, PACK * HALF], BF16, name="wb", align_bytes=64)
-            interleave(scopy, gbs[u, p][:], gfs[u][:, :, p * HALF : (p + 1) * HALF])
+        def at(name, kb, width=2048):
+            t = gs.tile([P, width], BF16, name=name, offset=kb * KB, align_bytes=64)
+            return t[:].rearrange("p (a x) -> p a x", a=1)
 
-        def GQ(u, p=0):
-            c, h, n = UNITS[u]
-            nc.vector.quantize_mx(out=gcodes[c][h + p][:].bitcast(FP8X4), scales=gscales[c][h + p][:], in_=gbs[u, p][:])
+        def weave(copy, runs, src):
+            a, r = runs.shape[1], src.shape[1]
+            if a == 1 and r == 1:
+                interleave(copy, runs[:, 0, :], src[:, 0, :, :])
+            elif a == 1:
+                interleave2(copy, runs[:, 0, :], src)
+            elif r == 1:
+                copy(runs.rearrange("p a (c i t) -> p a c t i", i=4, t=PACK), src[:, 0, :, :].rearrange("p t (a c i) -> p a c t i", a=a, i=4))
+            else:
+                assert a == r
+                copy(runs.rearrange("p a (c i t) -> p a c t i", i=4, t=PACK), src.rearrange("p r t (c i) -> p r c t i", i=4))
 
-        def new_wb(key):
-            wbs[key] = wbfs.tile([P, PACK * 2 * COLS], BF16, name="wb", align_bytes=64)
-            codes[key] = held.tile([P, 2 * COLS], U32, name=f"codes_{key}", align_bytes=64)
-            scales[key] = held.tile([P, 2 * COLS], U8, name=f"scales_{key}", align_bytes=64)
+        def quantise(cd, sc, runs):
+            n = runs.shape[2] // PACK
+            for a in range(runs.shape[1]):
+                cols = slice(a * n, (a + 1) * n)
+                nc.vector.quantize_mx(out=cd[:, cols].bitcast(FP8X4), scales=sc[:, cols], in_=runs[:, a, :])
 
-        def F(i, copy=scopy, halves=False):
-            new_wb(f"F{i}")
-            wb = wbs[f"F{i}"]
+        def GI(c, h, runs):
+            gbs[c, h] = runs
+            weave(scopy, runs, gfs[c, h][:].rearrange("p (r t) x -> p r t x", r=1))
+
+        def GQ(c, h):
+            quantise(gcodes[c][h], gscales[c][h], gbs[c, h])
+
+        def new_wb(key, width, runs):
+            wbs[key] = runs
+            codes[key] = held.tile([P, width], U32, name=f"codes_{key}", align_bytes=64)
+            scales[key] = held.tile([P, width], U8, name=f"scales_{key}", align_bytes=64)
+
+        def F(i, runs, copy=scopy, halves=False):
+            new_wb(f"F{i}", K, runs)
             if halves:
                 for h in range(2):
-                    interleave(copy, wb[:, h * PACK * COLS : (h + 1) * PACK * COLS], wraw[i][:, :, h * COLS : (h + 1) * COLS])
+                    interleave(copy, runs[:, 0, h * PACK * C : (h + 1) * PACK * C], wraw[i][:, :, h * C : (h + 1) * C])
             else:
-                interleave(copy, wb[:], wraw[i][:])
+                weave(copy, runs, wraw[i][:].rearrange("p (r t) x -> p r t x", r=1))
 
-        def AB(half, i, copy=scopy):
-            r = i % 2
-            key = f"{'AB'[half]}{i - r}"
-            if key not in wbs:
-                new_wb(key)
-            interleave(copy, wbs[key][:, r * PACK * COLS : (r + 1) * PACK * COLS], wraw[i][:, :, half * COLS : (half + 1) * COLS])
+        def A(q, runs, copy=scopy):
+            new_wb(f"A{q}", 2 * C, runs)
+            weave(copy, runs, parts[0][q][:])
+
+        def Q(kt, q, runs, copy=scopy):
+            new_wb(f"Q{kt}{q}", 2 * P, runs)
+            weave(copy, runs, parts[1][q][:, :, :, (kt - 2) * P : (kt - 1) * P])
 
         def WQ(key):
-            nc.vector.quantize_mx(out=codes[key][:].bitcast(FP8X4), scales=scales[key][:], in_=wbs[key][:])
+            quantise(codes[key], scales[key], wbs[key])
 
-        def MM(kt, h, lo=0, hi=6):
-            if lo == 0:
-                accs[kt, h] = psum.tile([P, HALF], F32, name="acc")
-            for p in range(lo, hi):
-                u, c = divmod(p, NPASS)
-                scols = slice(u * C, (u + 1) * C)
-                i = 2 * h * NPASS + p
-                half, inner = divmod(kt, 2)
-                if i < NFULL:
-                    key, k0 = f"F{i}", kt * P
-                else:
-                    key, k0 = f"{'AB'[half]}{i - i % 2}", (i % 2) * COLS + inner * P
-                nc.tensor.matmul_mx(
-                    out=accs[kt, h][:, scols],
-                    lhsT=codes[key][:, k0 : k0 + P].bitcast(FP8X4),
-                    lhsT_scale=scales[key][:, k0 : k0 + P],
-                    rhs=gcodes[c][h][:, scols].bitcast(FP8X4),
-                    rhs_scale=gscales[c][h][:, scols],
-                    start=(c == 0),
-                    stop=(c == NPASS - 1),
-                )
+        def MM(kt, e0, ne, bank):
+            acc = psum.tile([P, ne * C], F32, name=f"bank{bank}")
+            accs[kt, e0] = acc
+            for e in range(e0, e0 + ne):
+                h, u = divmod(e, 2)
+                for c in range(NPASS):
+                    p = u * NPASS + c
+                    if h == 0:
+                        key, k0 = f"F{p}", kt * P
+                    elif kt < 2:
+                        key, k0 = f"A{p // 2}", (p % 2) * C + kt * P
+                    else:
+                        key, k0 = f"Q{kt}{p // 2}", (p % 2) * P
+                    scols = slice(u * C, (u + 1) * C)
+                    nc.tensor.matmul_mx(
+                        out=acc[:, (e - e0) * C : (e - e0 + 1) * C],
+                        lhsT=codes[key][:, k0 : k0 + P].bitcast(FP8X4),
+                        lhsT_scale=scales[key][:, k0 : k0 + P],
+                        rhs=gcodes[c][h][:, scols].bitcast(FP8X4),
+                        rhs_scale=gscales[c][h][:, scols],
+                        start=(c == 0),
+                        stop=(c == NPASS - 1),
+                    )
 
-        def PC(kt, h):
+        def PC(kt, e0):
             if kt not in dxs:
-                dxs[kt] = held.tile([P, S], F32, name=f"dx{kt}")
-            scopy(dxs[kt][:, h * HALF : (h + 1) * HALF], accs[kt, h][:])
+                dxs[kt] = gs.tile([P, S], F32, name=f"dx{kt}", offset=(96 + 4 * kt) * KB)
+            acc = accs[kt, e0]
+            scopy(dxs[kt][:, e0 * C : e0 * C + acc.shape[1]], acc[:])
 
-        def PO(kt, r):
-            rs[kt, r] = gs.tile([P, T], F32, name=f"r{r}")
-            vcopy(rs[kt, r][:], dxs[kt][:].indirect((pos1_sb, pos2_sb)[r][:]))
+        def PA(kt, kb):
+            rs[kt] = gs.tile([P, T], F32, name=f"first{kt}", offset=kb * KB)
+            vcopy(rs[kt][:], dxs[kt][:].indirect(pos1_sb[:]))
 
-        def AD(kt, engine):
-            res = gs.tile([P, T], F32, name="res")
-            engine.tensor_tensor(res[:], rs[kt, 0][:], rs[kt, 1][:], ADD)
-            nc.sync.dma_start(out[kt * P : (kt + 1) * P, :], res[:])
+        def PB(kt, parts=1):
+            n = T // parts
+            for a in range(parts):
+                res = gs.tile([P, n], F32, name=f"res{kt}_{a}", offset=RES + kt * 4 * T + a * 4 * n)
+                cols = slice(a * n, (a + 1) * n)
+                nc.vector.tensor_tensor(res[:], dxs[kt][:].indirect(pos2_sb[:, a * n // 16 : (a + 1) * n // 16]), rs[kt][:, cols], ADD)
+                nc.sync.dma_start(out[kt * P : (kt + 1) * P, cols], res[:])
+
+        def load_lists():
+            nc.sync.dma_start(pos1_sb[:], pos1)
+            nc.sync.dma_start(pos2_sb[:], pos2)
 
         nc.sync.dma_start(offs_sb[:], offs)
-        load_win(0, 0)
+        load_win(0,0)
         load_gate(0)
+        load_win(0,1)
+        load_w(0,0)
+        load_win(0,2)
+        load_win(0,3)
+        load_w(0,1)
         load_gate(1)
-        load_win(0, 1)
-        load_w(0, 0)
-        load_win(0, 2)
-        load_w(0, 1)
-        load_win(0, 3)
         load_w(1)
-        load_win(1, 0)
         load_w(2)
-        load_win(1, 1)
+        load_win(1,0)
         load_w(3)
-        load_win(1, 2)
+        load_win(1,1)
+        load_win(1,2)
         load_w(4)
-        load_win(1, 3)
+        load_win(1,3)
         load_w(5)
-        nc.sync.dma_start(pos1_sb[:], pos1)
-        nc.sync.dma_start(pos2_sb[:], pos2)
-        load_win(2, 0)
-        load_w(6)
-        load_win(2, 1)
-        load_w(7)
-        load_win(2, 2)
-        load_w(8)
-        load_win(2, 3)
-        for i in range(9, 12): load_w(i)
-        G(0, 0, 0)
-        G(0, 0, 1)
-        G(0, 1)
-        F(0, halves=True)
-        F(1)
-        G(0, 2)
-        G(0, 3)
-        GI(0, 0)
-        F(2)
-        F(3)
-        G(1, 0)
+        load_win(2,0)
+        load_win(2,1)
+        load_win(2,2)
+        load_win(2,3)
+        for i in range(6, 12): load_w(i, 0)
+        load_lists()
+        for i in range(6, 12): load_w(i, 1)
+        G(0,0,96)
+        F(0, at("sF0",120), halves=True)
+        G(0,1,104)
+        GI(0,0,at("g0",0))
+        F(1,at("sF1",124))
         WQ("F0")
-        F(4)
-        G(1, 1)
+        GQ(0,0)
+        G(1,0,112)
+        F(2,at("sF2",128))
+        GI(0,1,at("g1",8))
+        F(3,at("sF3",132))
         WQ("F1")
-        F(5)
-        G(1, 2)
-        GQ(0, 0)
         WQ("F2")
-        GI(0, 1)
-        G(1, 3)
+        GQ(0,1)
+        G(1,1,24)
+        F(4,at("sF4",136))
+        GI(1,0,at("g2",16))
         WQ("F3")
-        AB(0, 6)
-        AB(0, 7)
-        G(2, 0)
+        G(2,0,32)
+        F(5,at("sF5",140))
         WQ("F4")
-        GI(1, 0)
-        GI(1, 1)
-        G(2, 1)
+        GQ(1,0)
         WQ("F5")
-        GQ(0, 1)
-        AB(0, 8)
-        AB(0, 9)
-        G(2, 2)
-        WQ("A6")
-        GQ(1, 0)
-        AB(0, 10)
-        AB(0, 11)
-        G(2, 3)
-        GQ(1, 1)
-        GI(2, 0)
-        WQ("A8")
-        WQ("A10")
-        GI(2, 1)
-        GQ(2, 0)
-        for kt in range(4): MM(kt, 0)
-        AB(1, 10, vcopy)
-        AB(1, 11, vcopy)
-        AB(1, 8)
-        AB(1, 6, vcopy)
-        PC(0, 0)
-        GQ(2, 1)
-        AB(1, 9)
-        WQ("B10")
-        AB(1, 7, vcopy)
-        WQ("B6")
-        MM(0, 1)
-        MM(1, 1)
-        PC(1, 0)
-        PC(0, 1)
-        PC(1, 1)
-        WQ("B8")
-        PO(0, 0)
-        PO(0, 1)
-        MM(2, 1)
-        MM(3, 1)
-        PC(2, 0)
-        PC(3, 0)
-        PO(1, 0)
-        PC(2, 1)
-        PC(3, 1)
-        PO(1, 1)
-        AD(0, nc.gpsimd)
-        PO(2, 0)
-        AD(1, nc.gpsimd)
-        PO(2, 1)
-        PO(3, 0)
-        AD(2, nc.gpsimd)
-        PO(3, 1)
-        AD(3, nc.vector)
+        G(2,1,40)
+        GI(1,1,at("g3",144))
+        GQ(1,1)
+        A(0,at("sA0",4))
+        WQ("A0")
+        GI(2,0,at("g4",48))
+        GQ(2,0)
+        A(1,at("sA1",12))
+        WQ("A1")
+        MM(0,0,2,0)
+        MM(1,0,2,1)
+        A(2,at("sA2",20))
+        WQ("A2")
+        GI(2,1,at("g5",56))
+        GQ(2,1)
+        MM(0,2,1,2)
+        MM(0,3,1,3)
+        MM(1,2,1,4)
+        MM(1,3,1,5)
+        Q(2,0,at("sQ20",56,1024),vcopy)
+        Q(2,2,at("sQ22",58,1024),vcopy)
+        Q(2,1,at("sQ21",64,1024))
+        PC(0,0)
+        PC(0,2)
+        PC(0,3)
+        WQ("Q21")
+        WQ("Q20")
+        WQ("Q22")
+        PC(1,0)
+        PC(1,2)
+        PC(1,3)
+        MM(2,0,2,0)
+        MM(2,2,2,6)
+        Q(3,0,at("sQ30",56,1024))
+        Q(3,1,at("sQ31",58,1024))
+        Q(3,2,at("sQ32",64,1024))
+        WQ("Q30")
+        WQ("Q31")
+        WQ("Q32")
+        MM(3,0,2,1)
+        MM(3,2,2,7)
+        PA(0,120)
+        PA(1,122)
+        PB(0)
+        PB(1)
+        PC(2,0)
+        PC(2,2)
+        PC(3,0)
+        PC(3,2)
+        PA(2,64)
+        PB(2)
+        PA(3,124)
+        PB(3,2)

@@ -13,6 +13,7 @@ PAD = 8
 WRAW_BUFS = 3
 WB_BUFS = 9
 GF_BUFS = 3
+LATE = {"F4": 144, "F5": 146}
 KB = 1024
 RES = 112 * KB
 GF_BYTES = 4 * PACK * HALF
@@ -40,20 +41,21 @@ def tile_moe_bdx_lin_none_kernel(tc, dyT, w, gate, offs, pos1, pos2, out):
         offs_sb = held.tile([P, S // 16], U16, name="offs_sb")
         pos1_sb = held.tile([P, T // 16], U16, name="pos1_sb")
         pos2_sb = held.tile([P, T // 16], U16, name="pos2_sb")
-        gate_sb = [held.tile([P, HALF], F32, name=f"gate_sb{h}") for h in range(2)]
+        gate_sb = held.tile([P, S], F32, name="gate_sb")
         gcodes = [[held.tile([P, HALF], U32, name=f"gcodes{c}_{h}", align_bytes=64) for h in range(2)] for c in range(NPASS)]
         gscales = [[held.tile([P, HALF], U8, name=f"gscales{c}_{h}", align_bytes=64) for h in range(2)] for c in range(NPASS)]
-        wins = [[held.tile([P, T + PAD], F32, name=f"win{b}_{j}") for j in range(PACK)] for b in range(NPASS)]
+        wins = [[held.tile([P, (HALF if b == 0 else S) + PAD], F32, name=f"win{b}_{j}") if (b, j) != (2, 3) else None for j in range(PACK)] for b in range(NPASS)]
+        wins[2][3] = gs.tile([P, S + PAD], F32, name="win_last", offset=144 * KB)
         for b in range(NPASS):
             for j in range(PACK):
-                nc.gpsimd.memset(wins[b][j][:, T : T + PAD], 0.0)
+                nc.gpsimd.memset(wins[b][j][:, T:], 0.0)
 
         def load_win(c, j):
             rows = dyT[c * PASS : (c + 1) * PASS, :].rearrange("(p j) t -> p j t", j=PACK)
             nc.sync.dma_start(wins[c][j][:, 0:T], rows[:, j, :])
 
         def load_gate(h):
-            nc.sync.dma_start(gate_sb[h][:], gate[0:P, h * HALF : (h + 1) * HALF])
+            nc.sync.dma_start(gate_sb[:, h * HALF : (h + 1) * HALF], gate[0:P, h * HALF : (h + 1) * HALF])
 
         wraw = {}
         parts = [[gs.tile([P, 2, PACK, C], F32, name=f"part{b}_{q}", offset=(48 + 24 * b + 8 * q) * KB, align_bytes=64) for q in range(3)] for b in range(2)]
@@ -85,9 +87,17 @@ def tile_moe_bdx_lin_none_kernel(tc, dyT, w, gate, offs, pos1, pos2, out):
         scopy, vcopy = nc.scalar.copy, nc.vector.tensor_copy
 
         def G(c, h, kb):
-            gfs[c, h] = gs.tile([P, PACK, HALF], F32, name=f"gf{c}_{h}", offset=kb * KB)
+            t = gs.tile([P, PACK, HALF], F32, name=f"gf{c}_{h}", offset=kb * KB)
+            gfs[c, h] = t[:]
             for j in range(PACK):
-                nc.vector.tensor_tensor(gfs[c, h][:, j, :], wins[c][j][:].indirect(offs_sb[:, h * 32 : (h + 1) * 32]), gate_sb[h][:], MULT)
+                nc.vector.tensor_tensor(t[:, j, :], wins[c][j][:].indirect(offs_sb[:, h * 32 : (h + 1) * 32]), gate_sb[:, h * HALF : (h + 1) * HALF], MULT)
+
+        def GW(c, kb):
+            t = gs.tile([P, PACK, S], F32, name=f"gf{c}", offset=kb * KB)
+            for h in range(2):
+                gfs[c, h] = t[:, :, h * HALF : (h + 1) * HALF]
+            for j in range(PACK):
+                nc.vector.tensor_tensor(t[:, j, :], wins[c][j][:].indirect(offs_sb[:]), gate_sb[:], MULT)
 
         def at(name, kb, width=2048):
             t = gs.tile([P, width], BF16, name=name, offset=kb * KB, align_bytes=64)
@@ -113,14 +123,17 @@ def tile_moe_bdx_lin_none_kernel(tc, dyT, w, gate, offs, pos1, pos2, out):
 
         def GI(c, h, runs):
             gbs[c, h] = runs
-            weave(scopy, runs, gfs[c, h][:].rearrange("p (r t) x -> p r t x", r=1))
+            weave(scopy, runs, gfs[c, h].rearrange("p (r t) x -> p r t x", r=1))
 
         def GQ(c, h):
             quantise(gcodes[c][h], gscales[c][h], gbs[c, h])
 
         def new_wb(key, width, runs):
             wbs[key] = runs
-            codes[key] = held.tile([P, width], U32, name=f"codes_{key}", align_bytes=64)
+            if key in LATE:
+                codes[key] = gs.tile([P, width], U32, name=f"codes_{key}", align_bytes=64, offset=LATE[key] * KB)
+            else:
+                codes[key] = held.tile([P, width], U32, name=f"codes_{key}", align_bytes=64)
             scales[key] = held.tile([P, width], U8, name=f"scales_{key}", align_bytes=64)
 
         def F(i, runs, copy=scopy, halves=False):
@@ -176,10 +189,10 @@ def tile_moe_bdx_lin_none_kernel(tc, dyT, w, gate, offs, pos1, pos2, out):
             rs[kt] = gs.tile([P, T], F32, name=f"first{kt}", offset=kb * KB)
             vcopy(rs[kt][:], dxs[kt][:].indirect(pos1_sb[:]))
 
-        def PB(kt, parts=1):
+        def PB(kt, kb, parts=1):
             n = T // parts
             for a in range(parts):
-                res = gs.tile([P, n], F32, name=f"res{kt}_{a}", offset=RES + kt * 4 * T + a * 4 * n)
+                res = gs.tile([P, n], F32, name=f"res{kt}_{a}", offset=kb * KB + a * 4 * n)
                 cols = slice(a * n, (a + 1) * n)
                 nc.vector.tensor_tensor(res[:], dxs[kt][:].indirect(pos2_sb[:, a * n // 16 : (a + 1) * n // 16]), rs[kt][:, cols], ADD)
                 nc.sync.dma_start(out[kt * P : (kt + 1) * P, cols], res[:])
@@ -206,72 +219,75 @@ def tile_moe_bdx_lin_none_kernel(tc, dyT, w, gate, offs, pos1, pos2, out):
         load_w(4)
         load_win(1,3)
         load_w(5)
+        load_w(6,0)
+        load_w(7,0)
         load_win(2,0)
         load_win(2,1)
+        load_w(8,0)
+        load_w(9,0)
         load_win(2,2)
         load_win(2,3)
-        for i in range(6, 12): load_w(i, 0)
+        load_w(10,0)
+        load_w(11,0)
         load_lists()
         for i in range(6, 12): load_w(i, 1)
         G(0,0,96)
-        F(0, at("sF0",120), halves=True)
+        F(0, at("sF0",128), halves=True)
         G(0,1,104)
         GI(0,0,at("g0",0))
-        F(1,at("sF1",124))
+        F(1,at("sF1",132))
         WQ("F0")
         GQ(0,0)
-        G(1,0,112)
-        F(2,at("sF2",128))
+        GW(1,112)
+        F(2,at("sF2",136))
         GI(0,1,at("g1",8))
-        F(3,at("sF3",132))
+        F(3,at("sF3",140))
         WQ("F1")
         WQ("F2")
         GQ(0,1)
-        G(1,1,24)
-        F(4,at("sF4",136))
-        GI(1,0,at("g2",16))
+        F(4,at("sF4",128))
         WQ("F3")
-        G(2,0,32)
-        F(5,at("sF5",140))
-        WQ("F4")
-        GQ(1,0)
-        WQ("F5")
-        G(2,1,40)
-        GI(1,1,at("g3",144))
-        GQ(1,1)
+        F(5,at("sF5",132))
+        GW(2,24)
         A(0,at("sA0",4))
+        GI(1,0,at("g2",40))
+        GI(1,1,at("g3",48))
+        WQ("F4")
+        WQ("F5")
         WQ("A0")
-        GI(2,0,at("g4",48))
-        GQ(2,0)
+        GQ(1,0)
+        GQ(1,1)
         A(1,at("sA1",12))
         WQ("A1")
-        MM(0,0,2,0)
-        MM(1,0,2,1)
         A(2,at("sA2",20))
         WQ("A2")
-        GI(2,1,at("g5",56))
+        GI(2,0,at("g4",56))
+        GQ(2,0)
+        MM(0,0,2,0)
+        MM(1,0,2,1)
+        GI(2,1,at("g5",64))
         GQ(2,1)
         MM(0,2,1,2)
-        MM(0,3,1,3)
         MM(1,2,1,4)
+        MM(0,3,1,3)
         MM(1,3,1,5)
-        Q(2,0,at("sQ20",56,1024),vcopy)
-        Q(2,2,at("sQ22",58,1024),vcopy)
-        Q(2,1,at("sQ21",64,1024))
+        Q(2,0,at("sQ20",64,1024),vcopy)
+        Q(2,2,at("sQ22",66,1024),vcopy)
+        Q(2,1,at("sQ21",56,1024))
         PC(0,0)
+        PC(1,0)
         PC(0,2)
+        PC(1,2)
         PC(0,3)
+        PC(1,3)
         WQ("Q21")
         WQ("Q20")
         WQ("Q22")
-        PC(1,0)
-        PC(1,2)
-        PC(1,3)
         MM(2,0,2,0)
         MM(2,2,2,6)
-        Q(3,0,at("sQ30",56,1024))
-        Q(3,1,at("sQ31",58,1024))
-        Q(3,2,at("sQ32",64,1024))
+        Q(3,0,at("sQ30",64,1024))
+        Q(3,1,at("sQ31",66,1024))
+        Q(3,2,at("sQ32",56,1024))
         WQ("Q30")
         WQ("Q31")
         WQ("Q32")
@@ -279,13 +295,13 @@ def tile_moe_bdx_lin_none_kernel(tc, dyT, w, gate, offs, pos1, pos2, out):
         MM(3,2,2,7)
         PA(0,120)
         PA(1,122)
-        PB(0)
-        PB(1)
+        PB(0,112)
+        PB(1,56)
         PC(2,0)
-        PC(2,2)
         PC(3,0)
+        PC(2,2)
         PC(3,2)
-        PA(2,64)
-        PB(2)
-        PA(3,124)
-        PB(3,2)
+        PA(2,124)
+        PA(3,126)
+        PB(2,114)
+        PB(3,116,2)

@@ -13,7 +13,7 @@ PAD = 8
 WRAW_BUFS = 3
 WB_BUFS = 9
 GF_BUFS = 3
-LATE = {"F4": 144, "F5": 146}
+LATE = {"F4": 144, "F5": 146, "A0": 149, "A1": 153, "A2": 155}
 KB = 1024
 RES = 112 * KB
 GF_BYTES = 4 * PACK * HALF
@@ -41,10 +41,10 @@ def tile_moe_bdx_lin_none_kernel(tc, dyT, w, gate, offs, pos1, pos2, out):
         offs_sb = held.tile([P, S // 16], U16, name="offs_sb")
         pos1_sb = held.tile([P, T // 16], U16, name="pos1_sb")
         pos2_sb = held.tile([P, T // 16], U16, name="pos2_sb")
-        gate_sb = held.tile([P, S], F32, name="gate_sb")
-        gcodes = [[held.tile([P, HALF], U32, name=f"gcodes{c}_{h}", align_bytes=64) for h in range(2)] for c in range(NPASS)]
+        gate_sb = gs.tile([P, S], F32, name="gate_sb", offset=149 * KB)
+        gcodes = [[held.tile([P, HALF], U32, name=f"gcodes{c}_{h}", align_bytes=64) if (c, h) != (1, 0) else None for h in range(2)] for c in range(NPASS)]
         gscales = [[held.tile([P, HALF], U8, name=f"gscales{c}_{h}", align_bytes=64) for h in range(2)] for c in range(NPASS)]
-        wins = [[held.tile([P, (HALF if b == 0 else S) + PAD], F32, name=f"win{b}_{j}") if (b, j) != (2, 3) else None for j in range(PACK)] for b in range(NPASS)]
+        wins = [[held.tile([P, S + PAD], F32, name=f"win{b}_{j}") if (b, j) != (2, 3) else None for j in range(PACK)] for b in range(NPASS)]
         wins[2][3] = gs.tile([P, S + PAD], F32, name="win_last", offset=144 * KB)
         for b in range(NPASS):
             for j in range(PACK):
@@ -58,12 +58,16 @@ def tile_moe_bdx_lin_none_kernel(tc, dyT, w, gate, offs, pos1, pos2, out):
             nc.sync.dma_start(gate_sb[:, h * HALF : (h + 1) * HALF], gate[0:P, h * HALF : (h + 1) * HALF])
 
         wraw = {}
-        parts = [[gs.tile([P, 2, PACK, C], F32, name=f"part{b}_{q}", offset=(48 + 24 * b + 8 * q) * KB, align_bytes=64) for q in range(3)] for b in range(2)]
+        parts = [[gs.tile([P, 2, PACK, C], F32, name=f"part{b}_{q}", offset=(48 + 24 * b + 8 * q) * KB, align_bytes=64) if (b, q) != (0, 2) else None for q in range(3)] for b in range(2)]
+        lasts = [gs.tile([P, PACK, C], F32, name=f"last{r}", offset=(64 + 4 * r) * KB, align_bytes=64) for r in range(2)]
 
         def load_w(i, half=None):
             e, c = divmod(i, NPASS)
             rows = w[e, c * PASS : (c + 1) * PASS, :].rearrange("(p j) k -> p j k", j=PACK)
             cols = slice(0, K) if half is None else slice(half * C, (half + 1) * C)
+            if i >= 10 and half == 0:
+                nc.sync.dma_start(lasts[i - 10][:], rows[:, :, cols])
+                return
             if i >= 6:
                 nc.sync.dma_start(parts[half][(i - 6) // 2][:, i % 2, :, :], rows[:, :, cols])
                 return
@@ -86,18 +90,16 @@ def tile_moe_bdx_lin_none_kernel(tc, dyT, w, gate, offs, pos1, pos2, out):
         gfs, gbs, wbs, accs, dxs, rs, codes, scales = {}, {}, {}, {}, {}, {}, {}, {}
         scopy, vcopy = nc.scalar.copy, nc.vector.tensor_copy
 
-        def G(c, h, kb):
-            t = gs.tile([P, PACK, HALF], F32, name=f"gf{c}_{h}", offset=kb * KB)
-            gfs[c, h] = t[:]
-            for j in range(PACK):
-                nc.vector.tensor_tensor(t[:, j, :], wins[c][j][:].indirect(offs_sb[:, h * 32 : (h + 1) * 32]), gate_sb[:, h * HALF : (h + 1) * HALF], MULT)
-
-        def GW(c, kb):
+        def GW(c, kb, split=False):
             t = gs.tile([P, PACK, S], F32, name=f"gf{c}", offset=kb * KB)
             for h in range(2):
                 gfs[c, h] = t[:, :, h * HALF : (h + 1) * HALF]
             for j in range(PACK):
-                nc.vector.tensor_tensor(t[:, j, :], wins[c][j][:].indirect(offs_sb[:]), gate_sb[:], MULT)
+                if split and j == 0:
+                    for h in range(2):
+                        nc.vector.tensor_tensor(t[:, j, h * HALF : (h + 1) * HALF], wins[c][j][:].indirect(offs_sb[:, h * 32 : (h + 1) * 32]), gate_sb[:, h * HALF : (h + 1) * HALF], MULT)
+                else:
+                    nc.vector.tensor_tensor(t[:, j, :], wins[c][j][:].indirect(offs_sb[:]), gate_sb[:], MULT)
 
         def at(name, kb, width=2048):
             t = gs.tile([P, width], BF16, name=name, offset=kb * KB, align_bytes=64)
@@ -125,7 +127,9 @@ def tile_moe_bdx_lin_none_kernel(tc, dyT, w, gate, offs, pos1, pos2, out):
             gbs[c, h] = runs
             weave(scopy, runs, gfs[c, h].rearrange("p (r t) x -> p r t x", r=1))
 
-        def GQ(c, h):
+        def GQ(c, h, kb=None):
+            if kb is not None:
+                gcodes[c][h] = gs.tile([P, HALF], U32, name=f"gcodes{c}_{h}", align_bytes=64, offset=kb * KB)
             quantise(gcodes[c][h], gscales[c][h], gbs[c, h])
 
         def new_wb(key, width, runs):
@@ -147,6 +151,11 @@ def tile_moe_bdx_lin_none_kernel(tc, dyT, w, gate, offs, pos1, pos2, out):
         def A(q, runs, copy=scopy):
             new_wb(f"A{q}", 2 * C, runs)
             weave(copy, runs, parts[0][q][:])
+
+        def AS(q, runs, r, copy):
+            if r == 0:
+                new_wb(f"A{q}", 2 * C, runs)
+            interleave(copy, wbs[f"A{q}"][:, 0, r * PACK * C : (r + 1) * PACK * C], lasts[r][:])
 
         def Q(kt, q, runs, copy=scopy):
             new_wb(f"Q{kt}{q}", 2 * P, runs)
@@ -204,19 +213,18 @@ def tile_moe_bdx_lin_none_kernel(tc, dyT, w, gate, offs, pos1, pos2, out):
         nc.sync.dma_start(offs_sb[:], offs)
         load_win(0,0)
         load_gate(0)
-        load_win(0,1)
-        load_w(0,0)
-        load_win(0,2)
-        load_win(0,3)
-        load_w(0,1)
         load_gate(1)
+        load_win(0,1)
+        load_w(0)
+        load_win(0,2)
         load_w(1)
+        load_win(0,3)
         load_w(2)
         load_win(1,0)
         load_w(3)
         load_win(1,1)
-        load_win(1,2)
         load_w(4)
+        load_win(1,2)
         load_win(1,3)
         load_w(5)
         load_w(6,0)
@@ -231,19 +239,18 @@ def tile_moe_bdx_lin_none_kernel(tc, dyT, w, gate, offs, pos1, pos2, out):
         load_w(11,0)
         load_lists()
         for i in range(6, 12): load_w(i, 1)
-        G(0,0,96)
-        F(0, at("sF0",128), halves=True)
-        G(0,1,104)
-        GI(0,0,at("g0",0))
+        GW(0,96,True)
+        F(0, at("sF0",128))
         F(1,at("sF1",132))
-        WQ("F0")
-        GQ(0,0)
-        GW(1,112)
         F(2,at("sF2",136))
-        GI(0,1,at("g1",8))
-        F(3,at("sF3",140))
+        GI(0,0,at("g0",16))
+        GI(0,1,at("g1",20))
+        WQ("F0")
         WQ("F1")
+        GW(1,112)
+        F(3,at("sF3",140))
         WQ("F2")
+        GQ(0,0)
         GQ(0,1)
         F(4,at("sF4",128))
         WQ("F3")
@@ -255,48 +262,52 @@ def tile_moe_bdx_lin_none_kernel(tc, dyT, w, gate, offs, pos1, pos2, out):
         WQ("F4")
         WQ("F5")
         WQ("A0")
-        GQ(1,0)
+        GQ(1,0,151)
         GQ(1,1)
         A(1,at("sA1",12))
         WQ("A1")
-        A(2,at("sA2",20))
+        AS(2,at("sA2",8),0,scopy)
+        AS(2,None,1,vcopy)
         WQ("A2")
         GI(2,0,at("g4",56))
         GQ(2,0)
-        MM(0,0,2,0)
-        MM(1,0,2,1)
+        MM(0,0,1,0)
+        MM(0,1,1,1)
+        MM(1,0,1,6)
+        MM(1,1,1,7)
         GI(2,1,at("g5",64))
         GQ(2,1)
         MM(0,2,1,2)
-        MM(1,2,1,4)
         MM(0,3,1,3)
+        MM(1,2,1,4)
         MM(1,3,1,5)
-        Q(2,0,at("sQ20",64,1024),vcopy)
-        Q(2,2,at("sQ22",66,1024),vcopy)
-        Q(2,1,at("sQ21",56,1024))
+        late = at("sQ2",64,3072)
+        for q in range(3): Q(2,q,late[:, :, q*1024:(q+1)*1024],vcopy)
         PC(0,0)
+        PC(0,1)
         PC(1,0)
+        PC(1,1)
         PC(0,2)
-        PC(1,2)
         PC(0,3)
+        PC(1,2)
         PC(1,3)
-        WQ("Q21")
         WQ("Q20")
+        WQ("Q21")
         WQ("Q22")
         MM(2,0,2,0)
-        MM(2,2,2,6)
-        Q(3,0,at("sQ30",64,1024))
-        Q(3,1,at("sQ31",66,1024))
-        Q(3,2,at("sQ32",56,1024))
+        MM(2,2,2,1)
+        Q(3,0,at("sQ30",149,1024))
+        Q(3,1,at("sQ31",153,1024))
+        Q(3,2,at("sQ32",155,1024))
         WQ("Q30")
         WQ("Q31")
         WQ("Q32")
-        MM(3,0,2,1)
+        MM(3,0,2,6)
         MM(3,2,2,7)
         PA(0,120)
         PA(1,122)
         PB(0,112)
-        PB(1,56)
+        PB(1,155)
         PC(2,0)
         PC(3,0)
         PC(2,2)

@@ -8,15 +8,25 @@ P = 128
 PACK = 4
 PASS = P * PACK
 NPASS = N // PASS
-HALF = 512
-PAD = 8
-WRAW_BUFS = 3
-WB_BUFS = 9
-GF_BUFS = 3
-LATE = {"F4": 144, "F5": 146, "A0": 149, "A1": 153, "A2": 155}
-KB = 1024
-RES = 112 * KB
-GF_BYTES = 4 * PACK * HALF
+HALF = S // 2
+FRONT = K // 2
+PER_COL = 16
+WINDOW = S + 8
+WHOLE = 2 * NPASS
+PAIRS = NPASS
+FIRST_CUT = C
+LAST_CUT = T - P
+
+RAW = 0
+RAW_KB, WOVEN_KB, CODES_KB = 8, 4, 2
+FRONTS = RAW + WHOLE * RAW_KB
+BACKS = FRONTS + PAIRS * RAW_KB
+G0 = BACKS + PAIRS * RAW_KB
+G1 = G0 + 2 * RAW_KB
+STAGE = G1 + 2 * RAW_KB
+LAST_WINDOW = STAGE + 4 * WOVEN_KB
+GATE = LAST_WINDOW + 5
+LATE_CODES = GATE + 4
 
 F32 = mybir.dt.float32
 BF16 = mybir.dt.bfloat16
@@ -28,291 +38,258 @@ ADD = mybir.AluOpType.add
 MULT = mybir.AluOpType.mult
 
 FLOPS = 2 * K * N * S
-BYTES = 4 * (N * T + E * N * K + S + K * T) + 2 * 128 * (64 + 32 + 32)
+BYTES = 4 * (N * T + E * N * K + S + K * T) + 2 * P * (S + 2 * T) // PER_COL
 
 
 def tile_moe_bdx_lin_none_kernel(tc, dyT, w, gate, offs, pos1, pos2, out):
     nc = tc.nc
     with ExitStack() as ctx:
         held = ctx.enter_context(tc.tile_pool(name="held", bufs=1))
-        gs = ctx.enter_context(tc.tile_pool(name="gs", bufs=1))
+        placed = ctx.enter_context(tc.tile_pool(name="placed", bufs=1))
         psum = ctx.enter_context(tc.psum_pool(name="psum", bufs=1))
 
-        offs_sb = held.tile([P, S // 16], U16, name="offs_sb")
-        pos1_sb = held.tile([P, T // 16], U16, name="pos1_sb")
-        pos2_sb = held.tile([P, T // 16], U16, name="pos2_sb")
-        gate_sb = gs.tile([P, S], F32, name="gate_sb", offset=149 * KB)
-        gcodes = [[held.tile([P, HALF], U32, name=f"gcodes{c}_{h}", align_bytes=64) if (c, h) != (1, 0) else None for h in range(2)] for c in range(NPASS)]
-        gscales = [[held.tile([P, HALF], U8, name=f"gscales{c}_{h}", align_bytes=64) for h in range(2)] for c in range(NPASS)]
-        wins = [[held.tile([P, S + PAD], F32, name=f"win{b}_{j}") if (b, j) != (2, 3) else None for j in range(PACK)] for b in range(NPASS)]
-        wins[2][3] = gs.tile([P, S + PAD], F32, name="win_last", offset=144 * KB)
-        for b in range(NPASS):
-            for j in range(PACK):
-                nc.gpsimd.memset(wins[b][j][:, T:], 0.0)
+        def place(name, shape, dtype, kib):
+            return placed.tile(shape, dtype, name=name, offset=kib * 1024, align_bytes=64)
 
-        def load_win(c, j):
-            rows = dyT[c * PASS : (c + 1) * PASS, :].rearrange("(p j) t -> p j t", j=PACK)
-            nc.sync.dma_start(wins[c][j][:, 0:T], rows[:, j, :])
+        def raw_place(i):
+            return RAW + i * RAW_KB
 
-        def load_gate(h):
-            nc.sync.dma_start(gate_sb[:, h * HALF : (h + 1) * HALF], gate[0:P, h * HALF : (h + 1) * HALF])
+        offs_sb = held.tile([P, S // PER_COL], U16, name="offs_sb")
+        pos1_sb = held.tile([P, T // PER_COL], U16, name="pos1_sb")
+        pos2_sb = held.tile([P, T // PER_COL], U16, name="pos2_sb")
+        gate_sb = place("gate_sb", [P, S], F32, GATE)
 
-        wraw = {}
-        parts = [[gs.tile([P, 2, PACK, C], F32, name=f"part{b}_{q}", offset=(48 + 24 * b + 8 * q) * KB, align_bytes=64) if (b, q) != (0, 2) else None for q in range(3)] for b in range(2)]
-        lasts = [gs.tile([P, PACK, C], F32, name=f"last{r}", offset=(64 + 4 * r) * KB, align_bytes=64) for r in range(2)]
+        windows = {(c, r): held.tile([P, WINDOW], F32, name=f"window{c}_{r}") for c in range(NPASS) for r in range(PACK) if (c, r) != (NPASS - 1, PACK - 1)}
+        windows[NPASS - 1, PACK - 1] = place("last_window", [P, WINDOW], F32, LAST_WINDOW)
+        for window in windows.values():
+            nc.gpsimd.memset(window[:, T:], 0.0)
 
-        def load_w(i, half=None):
+        raw = [place(f"raw{i}", [P, PACK, K], F32, raw_place(i)) for i in range(WHOLE)]
+        fronts = [place(f"fronts{q}", [P, 2, PACK, FRONT], F32, FRONTS + q * RAW_KB) for q in range(PAIRS - 1)]
+        last_place = FRONTS + (PAIRS - 1) * RAW_KB
+        last_fronts = [place(f"last_front{u}", [P, PACK, FRONT], F32, last_place + u * WOVEN_KB) for u in range(2)]
+        backs = [place(f"backs{q}", [P, 2, PACK, FRONT], F32, BACKS + q * RAW_KB) for q in range(PAIRS)]
+
+        def load_window(c, r):
+            rows = dyT[c * PASS : (c + 1) * PASS, :].rearrange("(p r) t -> p r t", r=PACK)
+            nc.sync.dma_start(windows[c, r][:, 0:T], rows[:, r, :])
+
+        def weight_rows(i):
             e, c = divmod(i, NPASS)
-            rows = w[e, c * PASS : (c + 1) * PASS, :].rearrange("(p j) k -> p j k", j=PACK)
-            cols = slice(0, K) if half is None else slice(half * C, (half + 1) * C)
-            if i >= 10 and half == 0:
-                nc.sync.dma_start(lasts[i - 10][:], rows[:, :, cols])
-                return
-            if i >= 6:
-                nc.sync.dma_start(parts[half][(i - 6) // 2][:, i % 2, :, :], rows[:, :, cols])
-                return
-            if i not in wraw:
-                wraw[i] = gs.tile([P, PACK, K], F32, name=f"wraw{i}", offset=8 * i * KB, align_bytes=64)
-            nc.sync.dma_start(wraw[i][:, :, cols], rows[:, :, cols])
+            return w[e, c * PASS : (c + 1) * PASS, :].rearrange("(p r) k -> p r k", r=PACK)
 
-        def interleave(copy, dst, src):
-            copy(
-                dst.rearrange("p (c i t) -> p c t i", i=4, t=PACK),
-                src.rearrange("p t (c i) -> p c t i", i=4),
-            )
+        def load_whole(i):
+            nc.sync.dma_start(raw[i][:], weight_rows(i))
 
-        def interleave2(copy, dst, src):
-            copy(
-                dst.rearrange("p (r c i t) -> p r c t i", r=2, i=4, t=PACK),
-                src.rearrange("p r t (c i) -> p r c t i", i=4),
-            )
+        def load_fronts(q):
+            for u in range(2):
+                into = last_fronts[u][:] if q == PAIRS - 1 else fronts[q][:, u, :, :]
+                nc.sync.dma_start(into, weight_rows(WHOLE + 2 * q + u)[:, :, 0:FRONT])
 
-        gfs, gbs, wbs, accs, dxs, rs, codes, scales = {}, {}, {}, {}, {}, {}, {}, {}
-        scopy, vcopy = nc.scalar.copy, nc.vector.tensor_copy
+        def load_backs(q):
+            for u in range(2):
+                nc.sync.dma_start(backs[q][:, u, :, :], weight_rows(WHOLE + 2 * q + u)[:, :, FRONT:K])
 
-        def GW(c, kb, split=False):
-            t = gs.tile([P, PACK, S], F32, name=f"gf{c}", offset=kb * KB)
+        g_raw, g_woven, g_mx = {}, {}, {}
+        w_woven, w_mx = {}, {}
+        w_at = {}
+        acc, dx, first = {}, {}, {}
+
+        def gather_g(c, kib, cuts_of_first=(0, S)):
+            g = place(f"g{c}", [P, PACK, S], F32, kib)
             for h in range(2):
-                gfs[c, h] = t[:, :, h * HALF : (h + 1) * HALF]
-            for j in range(PACK):
-                if split and j == 0:
-                    for h in range(2):
-                        nc.vector.tensor_tensor(t[:, j, h * HALF : (h + 1) * HALF], wins[c][j][:].indirect(offs_sb[:, h * 32 : (h + 1) * 32]), gate_sb[:, h * HALF : (h + 1) * HALF], MULT)
-                else:
-                    nc.vector.tensor_tensor(t[:, j, :], wins[c][j][:].indirect(offs_sb[:]), gate_sb[:], MULT)
+                g_raw[c, h] = g[:, :, h * HALF : (h + 1) * HALF]
+            for r in range(PACK):
+                cuts = cuts_of_first if r == 0 else (0, S)
+                for lo, hi in zip(cuts, cuts[1:]):
+                    picked = windows[c, r][:].indirect(offs_sb[:, lo // PER_COL : hi // PER_COL])
+                    nc.vector.tensor_tensor(g[:, r, lo:hi], picked, gate_sb[:, lo:hi], MULT)
 
-        def at(name, kb, width=2048):
-            t = gs.tile([P, width], BF16, name=name, offset=kb * KB, align_bytes=64)
-            return t[:].rearrange("p (a x) -> p a x", a=1)
+        def weave(copy, dst, src):
+            copy(
+                dst.rearrange("p (x i r) -> p x r i", i=4, r=PACK),
+                src.rearrange("p r (x i) -> p x r i", i=4),
+            )
 
-        def weave(copy, runs, src):
-            a, r = runs.shape[1], src.shape[1]
-            if a == 1 and r == 1:
-                interleave(copy, runs[:, 0, :], src[:, 0, :, :])
-            elif a == 1:
-                interleave2(copy, runs[:, 0, :], src)
-            elif r == 1:
-                copy(runs.rearrange("p a (c i t) -> p a c t i", i=4, t=PACK), src[:, 0, :, :].rearrange("p t (a c i) -> p a c t i", a=a, i=4))
+        def weave_pair(copy, dst, src):
+            copy(
+                dst.rearrange("p (u x i r) -> p u x r i", u=2, i=4, r=PACK),
+                src.rearrange("p u r (x i) -> p u x r i", i=4),
+            )
+
+        def quantise(name, woven, kib):
+            words = woven.shape[1] // PACK
+            if kib is None:
+                codes = held.tile([P, words], U32, name=f"codes_{name}", align_bytes=64)
             else:
-                assert a == r
-                copy(runs.rearrange("p a (c i t) -> p a c t i", i=4, t=PACK), src.rearrange("p r t (c i) -> p r c t i", i=4))
+                codes = place(f"codes_{name}", [P, words], U32, kib)
+            scales = held.tile([P, words], U8, name=f"scales_{name}", align_bytes=64)
+            nc.vector.quantize_mx(out=codes[:].bitcast(FP8X4), scales=scales[:], in_=woven)
+            return codes, scales
 
-        def quantise(cd, sc, runs):
-            n = runs.shape[2] // PACK
-            for a in range(runs.shape[1]):
-                cols = slice(a * n, (a + 1) * n)
-                nc.vector.quantize_mx(out=cd[:, cols].bitcast(FP8X4), scales=sc[:, cols], in_=runs[:, a, :])
+        def weave_g(c, h, kib):
+            g_woven[c, h] = place(f"g_woven{c}_{h}", [P, PACK * HALF], BF16, kib)[:]
+            weave(nc.scalar.copy, g_woven[c, h], g_raw[c, h])
 
-        def GI(c, h, runs):
-            gbs[c, h] = runs
-            weave(scopy, runs, gfs[c, h].rearrange("p (r t) x -> p r t x", r=1))
+        def quantise_g(c, h, kib=None):
+            g_mx[c, h] = quantise(f"g{c}_{h}", g_woven[c, h], kib)
 
-        def GQ(c, h, kb=None):
-            if kb is not None:
-                gcodes[c][h] = gs.tile([P, HALF], U32, name=f"gcodes{c}_{h}", align_bytes=64, offset=kb * KB)
-            quantise(gcodes[c][h], gscales[c][h], gbs[c, h])
+        def weave_whole(i, kib):
+            piece = f"whole{i}"
+            w_woven[piece] = place(f"woven_{piece}", [P, PACK * K], BF16, kib)[:]
+            w_at.update({(i, kt): (piece, kt * P) for kt in range(4)})
+            weave(nc.scalar.copy, w_woven[piece], raw[i][:])
 
-        def new_wb(key, width, runs):
-            wbs[key] = runs
-            if key in LATE:
-                codes[key] = gs.tile([P, width], U32, name=f"codes_{key}", align_bytes=64, offset=LATE[key] * KB)
+        def weave_fronts(q, kib):
+            piece = f"fronts{q}"
+            w_woven[piece] = place(f"woven_{piece}", [P, PACK * 2 * FRONT], BF16, kib)[:]
+            w_at.update({(WHOLE + 2 * q + u, kt): (piece, u * FRONT + kt * P) for u in range(2) for kt in range(2)})
+            if q < PAIRS - 1:
+                weave_pair(nc.scalar.copy, w_woven[piece], fronts[q][:])
             else:
-                codes[key] = held.tile([P, width], U32, name=f"codes_{key}", align_bytes=64)
-            scales[key] = held.tile([P, width], U8, name=f"scales_{key}", align_bytes=64)
+                for u, copy in enumerate((nc.scalar.copy, nc.vector.tensor_copy)):
+                    weave(copy, w_woven[piece][:, u * PACK * FRONT : (u + 1) * PACK * FRONT], last_fronts[u][:])
 
-        def F(i, runs, copy=scopy, halves=False):
-            new_wb(f"F{i}", K, runs)
-            if halves:
-                for h in range(2):
-                    interleave(copy, runs[:, 0, h * PACK * C : (h + 1) * PACK * C], wraw[i][:, :, h * C : (h + 1) * C])
-            else:
-                weave(copy, runs, wraw[i][:].rearrange("p (r t) x -> p r t x", r=1))
+        def weave_backs(q, kt, woven, copy):
+            piece = f"backs{q}_{kt}"
+            w_woven[piece] = woven
+            w_at.update({(WHOLE + 2 * q + u, kt): (piece, u * P) for u in range(2)})
+            weave_pair(copy, woven, backs[q][:, :, :, kt * P - FRONT : (kt + 1) * P - FRONT])
 
-        def A(q, runs, copy=scopy):
-            new_wb(f"A{q}", 2 * C, runs)
-            weave(copy, runs, parts[0][q][:])
+        def quantise_w(piece, kib=None):
+            w_mx[piece] = quantise(piece, w_woven[piece], kib)
 
-        def AS(q, runs, r, copy):
-            if r == 0:
-                new_wb(f"A{q}", 2 * C, runs)
-            interleave(copy, wbs[f"A{q}"][:, 0, r * PACK * C : (r + 1) * PACK * C], lasts[r][:])
-
-        def Q(kt, q, runs, copy=scopy):
-            new_wb(f"Q{kt}{q}", 2 * P, runs)
-            weave(copy, runs, parts[1][q][:, :, :, (kt - 2) * P : (kt - 1) * P])
-
-        def WQ(key):
-            quantise(codes[key], scales[key], wbs[key])
-
-        def MM(kt, e0, ne, bank):
-            acc = psum.tile([P, ne * C], F32, name=f"bank{bank}")
-            accs[kt, e0] = acc
-            for e in range(e0, e0 + ne):
+        def multiply(kt, experts, bank):
+            acc[kt, experts[0]] = psum.tile([P, len(experts) * C], F32, name=f"bank{bank}")
+            for at, e in enumerate(experts):
                 h, u = divmod(e, 2)
+                slots = slice(u * C, (u + 1) * C)
                 for c in range(NPASS):
-                    p = u * NPASS + c
-                    if h == 0:
-                        key, k0 = f"F{p}", kt * P
-                    elif kt < 2:
-                        key, k0 = f"A{p // 2}", (p % 2) * C + kt * P
-                    else:
-                        key, k0 = f"Q{kt}{p // 2}", (p % 2) * P
-                    scols = slice(u * C, (u + 1) * C)
+                    piece, col = w_at[e * NPASS + c, kt]
+                    w_codes, w_scales = w_mx[piece]
+                    g_codes, g_scales = g_mx[c, h]
                     nc.tensor.matmul_mx(
-                        out=acc[:, (e - e0) * C : (e - e0 + 1) * C],
-                        lhsT=codes[key][:, k0 : k0 + P].bitcast(FP8X4),
-                        lhsT_scale=scales[key][:, k0 : k0 + P],
-                        rhs=gcodes[c][h][:, scols].bitcast(FP8X4),
-                        rhs_scale=gscales[c][h][:, scols],
+                        out=acc[kt, experts[0]][:, at * C : (at + 1) * C],
+                        lhsT=w_codes[:, col : col + P].bitcast(FP8X4),
+                        lhsT_scale=w_scales[:, col : col + P],
+                        rhs=g_codes[:, slots].bitcast(FP8X4),
+                        rhs_scale=g_scales[:, slots],
                         start=(c == 0),
                         stop=(c == NPASS - 1),
                     )
 
-        def PC(kt, e0):
-            if kt not in dxs:
-                dxs[kt] = gs.tile([P, S], F32, name=f"dx{kt}", offset=(96 + 4 * kt) * KB)
-            acc = accs[kt, e0]
-            scopy(dxs[kt][:, e0 * C : e0 * C + acc.shape[1]], acc[:])
+        def empty(kt, e):
+            if kt not in dx:
+                dx[kt] = place(f"dx{kt}", [P, S], F32, G0 + kt * WOVEN_KB)
+            bank = acc[kt, e]
+            nc.scalar.copy(dx[kt][:, e * C : e * C + bank.shape[1]], bank[:])
 
-        def PA(kt, kb):
-            rs[kt] = gs.tile([P, T], F32, name=f"first{kt}", offset=kb * KB)
-            vcopy(rs[kt][:], dxs[kt][:].indirect(pos1_sb[:]))
+        def gather_first(kt):
+            first[kt] = place(f"first{kt}", [P, T], F32, G1 + RAW_KB + kt * CODES_KB)
+            nc.vector.tensor_copy(first[kt][:], dx[kt][:].indirect(pos1_sb[:]))
 
-        def PB(kt, kb, parts=1):
-            n = T // parts
-            for a in range(parts):
-                res = gs.tile([P, n], F32, name=f"res{kt}_{a}", offset=kb * KB + a * 4 * n)
-                cols = slice(a * n, (a + 1) * n)
-                nc.vector.tensor_tensor(res[:], dxs[kt][:].indirect(pos2_sb[:, a * n // 16 : (a + 1) * n // 16]), rs[kt][:, cols], ADD)
-                nc.sync.dma_start(out[kt * P : (kt + 1) * P, cols], res[:])
-
-        def load_lists():
-            nc.sync.dma_start(pos1_sb[:], pos1)
-            nc.sync.dma_start(pos2_sb[:], pos2)
+        def gather_second_and_store(kt, kib, cuts=(0, T)):
+            for lo, hi in zip(cuts, cuts[1:]):
+                total = placed.tile([P, hi - lo], F32, name=f"total{kt}_{lo}", offset=kib * 1024 + 4 * lo, align_bytes=64)
+                picked = dx[kt][:].indirect(pos2_sb[:, lo // PER_COL : hi // PER_COL])
+                nc.vector.tensor_tensor(total[:], picked, first[kt][:, lo:hi], ADD)
+                nc.sync.dma_start(out[kt * P : (kt + 1) * P, lo:hi], total[:])
 
         nc.sync.dma_start(offs_sb[:], offs)
-        load_win(0,0)
-        load_gate(0)
-        load_gate(1)
-        load_win(0,1)
-        load_w(0)
-        load_win(0,2)
-        load_w(1)
-        load_win(0,3)
-        load_w(2)
-        load_win(1,0)
-        load_w(3)
-        load_win(1,1)
-        load_w(4)
-        load_win(1,2)
-        load_win(1,3)
-        load_w(5)
-        load_w(6,0)
-        load_w(7,0)
-        load_win(2,0)
-        load_win(2,1)
-        load_w(8,0)
-        load_w(9,0)
-        load_win(2,2)
-        load_win(2,3)
-        load_w(10,0)
-        load_w(11,0)
-        load_lists()
-        for i in range(6, 12): load_w(i, 1)
-        GW(0,96,True)
-        F(0, at("sF0",128))
-        F(1,at("sF1",132))
-        F(2,at("sF2",136))
-        GI(0,0,at("g0",16))
-        GI(0,1,at("g1",20))
-        WQ("F0")
-        WQ("F1")
-        GW(1,112)
-        F(3,at("sF3",140))
-        WQ("F2")
-        GQ(0,0)
-        GQ(0,1)
-        F(4,at("sF4",128))
-        WQ("F3")
-        F(5,at("sF5",132))
-        GW(2,24)
-        A(0,at("sA0",4))
-        GI(1,0,at("g2",40))
-        GI(1,1,at("g3",48))
-        WQ("F4")
-        WQ("F5")
-        WQ("A0")
-        GQ(1,0,151)
-        GQ(1,1)
-        A(1,at("sA1",12))
-        WQ("A1")
-        AS(2,at("sA2",8),0,scopy)
-        AS(2,None,1,vcopy)
-        WQ("A2")
-        GI(2,0,at("g4",56))
-        GQ(2,0)
-        MM(0,0,1,0)
-        MM(0,1,1,1)
-        MM(1,0,1,6)
-        MM(1,1,1,7)
-        GI(2,1,at("g5",64))
-        GQ(2,1)
-        MM(0,2,1,2)
-        MM(0,3,1,3)
-        MM(1,2,1,4)
-        MM(1,3,1,5)
-        late = at("sQ2",64,3072)
-        for q in range(3): Q(2,q,late[:, :, q*1024:(q+1)*1024],vcopy)
-        PC(0,0)
-        PC(0,1)
-        PC(1,0)
-        PC(1,1)
-        PC(0,2)
-        PC(0,3)
-        PC(1,2)
-        PC(1,3)
-        WQ("Q20")
-        WQ("Q21")
-        WQ("Q22")
-        MM(2,0,2,0)
-        MM(2,2,2,1)
-        Q(3,0,at("sQ30",149,1024))
-        Q(3,1,at("sQ31",153,1024))
-        Q(3,2,at("sQ32",155,1024))
-        WQ("Q30")
-        WQ("Q31")
-        WQ("Q32")
-        MM(3,0,2,6)
-        MM(3,2,2,7)
-        PA(0,120)
-        PA(1,122)
-        PB(0,112)
-        PB(1,155)
-        PC(2,0)
-        PC(3,0)
-        PC(2,2)
-        PC(3,2)
-        PA(2,124)
-        PA(3,126)
-        PB(2,114)
-        PB(3,116,2)
+        load_window(0, 0)
+        for lo, hi in ((0, FIRST_CUT), (FIRST_CUT, S)):
+            nc.sync.dma_start(gate_sb[:, lo:hi], gate[0:P, lo:hi])
+        for i in range(NPASS):
+            load_window(0, i + 1)
+            load_whole(i)
+        load_window(1, 0)
+        load_whole(3)
+        load_window(1, 1)
+        load_whole(4)
+        load_window(1, 2)
+        load_window(1, 3)
+        load_whole(5)
+        for q in range(PAIRS - 1):
+            load_fronts(q)
+            load_window(2, 2 * q)
+            load_window(2, 2 * q + 1)
+        load_fronts(PAIRS - 1)
+        nc.sync.dma_start(pos1_sb[:], pos1)
+        nc.sync.dma_start(pos2_sb[:], pos2)
+        for q in range(PAIRS):
+            load_backs(q)
+
+        gather_g(0, G0, (0, FIRST_CUT, S))
+        for i in range(NPASS):
+            weave_whole(i, STAGE + i * WOVEN_KB)
+        for h in range(2):
+            weave_g(0, h, raw_place(2) + h * WOVEN_KB)
+        quantise_w("whole0")
+        quantise_w("whole1")
+
+        gather_g(1, G1)
+        weave_whole(3, STAGE + 3 * WOVEN_KB)
+        quantise_w("whole2")
+        for h in range(2):
+            quantise_g(0, h)
+        weave_whole(4, STAGE)
+        quantise_w("whole3")
+        weave_whole(5, STAGE + WOVEN_KB)
+
+        gather_g(2, raw_place(3))
+        weave_fronts(0, raw_place(0) + WOVEN_KB)
+        weave_g(1, 0, raw_place(5))
+        weave_g(1, 1, FRONTS)
+        quantise_w("whole4", LAST_WINDOW)
+        quantise_w("whole5", LAST_WINDOW + CODES_KB)
+        quantise_w("fronts0", GATE)
+        quantise_g(1, 0, GATE + CODES_KB)
+        quantise_g(1, 1)
+        weave_fronts(1, raw_place(1) + WOVEN_KB)
+        quantise_w("fronts1", LATE_CODES)
+        weave_fronts(2, raw_place(1))
+        quantise_w("fronts2", LATE_CODES + CODES_KB)
+
+        weave_g(2, 0, FRONTS + RAW_KB)
+        quantise_g(2, 0)
+        for kt, banks in ((0, (0, 1)), (1, (6, 7))):
+            for e in range(2):
+                multiply(kt, [e], banks[e])
+        weave_g(2, 1, last_place)
+        quantise_g(2, 1)
+        for kt, banks in ((0, (2, 3)), (1, (4, 5))):
+            for u in range(2):
+                multiply(kt, [2 + u], banks[u])
+
+        quarter = PACK * 2 * P
+        woven2 = place("woven_backs_2", [P, PAIRS * quarter], BF16, last_place)
+        for q in range(PAIRS):
+            weave_backs(q, 2, woven2[:, q * quarter : (q + 1) * quarter], nc.vector.tensor_copy)
+        for h in range(2):
+            for kt in range(2):
+                for u in range(2):
+                    empty(kt, 2 * h + u)
+        for q in range(PAIRS):
+            quantise_w(f"backs{q}_2")
+
+        multiply(2, [0, 1], 0)
+        multiply(2, [2, 3], 1)
+        woven3_places = (GATE, LATE_CODES, LATE_CODES + CODES_KB)
+        for q in range(PAIRS):
+            weave_backs(q, 3, place(f"woven_backs{q}_3", [P, quarter], BF16, woven3_places[q])[:], nc.scalar.copy)
+        for q in range(PAIRS):
+            quantise_w(f"backs{q}_3")
+        multiply(3, [0, 1], 6)
+        multiply(3, [2, 3], 7)
+
+        gather_first(0)
+        gather_first(1)
+        gather_second_and_store(0, G1)
+        gather_second_and_store(1, woven3_places[-1])
+        for e in (0, 2):
+            for kt in (2, 3):
+                empty(kt, e)
+        gather_first(2)
+        gather_first(3)
+        gather_second_and_store(2, G1 + CODES_KB)
+        gather_second_and_store(3, G1 + 2 * CODES_KB, (0, LAST_CUT, T))

@@ -12,21 +12,23 @@ HALF = S // 2
 FRONT = K // 2
 PER_COL = 16
 WINDOW = S + 8
-WHOLE = 2 * NPASS
+EARLY = 2 * NPASS
 PAIRS = NPASS
+HALVED = (1, 2)
 FIRST_CUT = C
 LAST_CUT = T - P
 
-RAW = 0
-RAW_KB, WOVEN_KB, CODES_KB = 8, 4, 2
-FRONTS = RAW + WHOLE * RAW_KB
-BACKS = FRONTS + PAIRS * RAW_KB
-G0 = BACKS + PAIRS * RAW_KB
-G1 = G0 + 2 * RAW_KB
-STAGE = G1 + 2 * RAW_KB
-LAST_WINDOW = STAGE + 4 * WOVEN_KB
-GATE = LAST_WINDOW + 5
-LATE_CODES = GATE + 4
+KIB = 1024
+WINDOW_BYTES = 65 * 64
+WINDOWS = 0
+LAST_WINDOW = WINDOWS + 11 * WINDOW_BYTES
+GATE = WINDOWS + 12 * WINDOW_BYTES
+RAW = GATE + 4 * KIB
+LATE_RAW = RAW + EARLY * 8 * KIB
+G0 = LATE_RAW + PAIRS * 16 * KIB
+G1 = G0 + 16 * KIB
+EARLY_WOVEN = G1 + 16 * KIB
+LATE_WOVEN = EARLY_WOVEN + PAIRS * 8 * KIB
 
 F32 = mybir.dt.float32
 BF16 = mybir.dt.bfloat16
@@ -48,27 +50,28 @@ def tile_moe_bdx_lin_none_kernel(tc, dyT, w, gate, offs, pos1, pos2, out):
         placed = ctx.enter_context(tc.tile_pool(name="placed", bufs=1))
         psum = ctx.enter_context(tc.psum_pool(name="psum", bufs=1))
 
-        def place(name, shape, dtype, kib):
-            return placed.tile(shape, dtype, name=name, offset=kib * 1024, align_bytes=64)
+        def place(name, shape, dtype, at):
+            return placed.tile(shape, dtype, name=name, offset=at, align_bytes=64)
 
         def raw_place(i):
-            return RAW + i * RAW_KB
+            return RAW + i * 8 * KIB
 
         offs_sb = held.tile([P, S // PER_COL], U16, name="offs_sb")
         pos1_sb = held.tile([P, T // PER_COL], U16, name="pos1_sb")
         pos2_sb = held.tile([P, T // PER_COL], U16, name="pos2_sb")
         gate_sb = place("gate_sb", [P, S], F32, GATE)
 
-        windows = {(c, r): held.tile([P, WINDOW], F32, name=f"window{c}_{r}") for c in range(NPASS) for r in range(PACK) if (c, r) != (NPASS - 1, PACK - 1)}
-        windows[NPASS - 1, PACK - 1] = place("last_window", [P, WINDOW], F32, LAST_WINDOW)
-        for window in windows.values():
-            nc.gpsimd.memset(window[:, T:], 0.0)
+        windows = {}
+        for c in range(NPASS):
+            for r in range(PACK):
+                windows[c, r] = place(f"window{c}_{r}", [P, WINDOW], F32, WINDOWS + (c * PACK + r) * WINDOW_BYTES)
+                nc.gpsimd.memset(windows[c, r][:, T:], 0.0)
 
-        raw = [place(f"raw{i}", [P, PACK, K], F32, raw_place(i)) for i in range(WHOLE)]
-        fronts = [place(f"fronts{q}", [P, 2, PACK, FRONT], F32, FRONTS + q * RAW_KB) for q in range(PAIRS - 1)]
-        last_place = FRONTS + (PAIRS - 1) * RAW_KB
-        last_fronts = [place(f"last_front{u}", [P, PACK, FRONT], F32, last_place + u * WOVEN_KB) for u in range(2)]
-        backs = [place(f"backs{q}", [P, 2, PACK, FRONT], F32, BACKS + q * RAW_KB) for q in range(PAIRS)]
+        raw = {i: place(f"raw{i}", [P, PACK, K], F32, raw_place(i)) for i in range(EARLY) if i not in HALVED}
+        halves = {(i, f): place(f"raw{i}_{f}", [P, PACK, FRONT], F32, raw_place(i) + f * 4 * KIB) for i in HALVED for f in range(2)}
+        late_raw = place("late_raw", [P, 2, PACK, K], F32, LATE_RAW)
+        late_halves = {(q, f): place(f"late_raw{q}_{f}", [P, 2, PACK, FRONT], F32, LATE_RAW + (2 * q + f) * 8 * KIB) for q in (1, 2) for f in range(2)}
+        early_woven = [place(f"early_woven{q}", [P, 2, 2, PACK * FRONT], BF16, EARLY_WOVEN + q * 8 * KIB) for q in range(PAIRS)]
 
         def load_window(c, r):
             rows = dyT[c * PASS : (c + 1) * PASS, :].rearrange("(p r) t -> p r t", r=PACK)
@@ -78,25 +81,35 @@ def tile_moe_bdx_lin_none_kernel(tc, dyT, w, gate, offs, pos1, pos2, out):
             e, c = divmod(i, NPASS)
             return w[e, c * PASS : (c + 1) * PASS, :].rearrange("(p r) k -> p r k", r=PACK)
 
-        def load_whole(i):
-            nc.sync.dma_start(raw[i][:], weight_rows(i))
+        def load_late_halves(f):
+            for q in (1, 2):
+                for u in range(2):
+                    nc.sync.dma_start(late_halves[q, f][:, u, :, :], weight_rows(EARLY + 2 * q + u)[:, :, f * FRONT : (f + 1) * FRONT])
 
-        def load_fronts(q):
-            for u in range(2):
-                into = last_fronts[u][:] if q == PAIRS - 1 else fronts[q][:, u, :, :]
-                nc.sync.dma_start(into, weight_rows(WHOLE + 2 * q + u)[:, :, 0:FRONT])
-
-        def load_backs(q):
-            for u in range(2):
-                nc.sync.dma_start(backs[q][:, u, :, :], weight_rows(WHOLE + 2 * q + u)[:, :, FRONT:K])
+        def load_weight(i):
+            rows = weight_rows(i)
+            if i in HALVED:
+                for f in range(2):
+                    nc.sync.dma_start(halves[i, f][:], rows[:, :, f * FRONT : (f + 1) * FRONT])
+            elif i < EARLY:
+                nc.sync.dma_start(raw[i][:], rows)
+            else:
+                nc.sync.dma_start(late_raw[:, i - EARLY, :, :], rows)
 
         g_raw, g_woven, g_mx = {}, {}, {}
         w_woven, w_mx = {}, {}
         w_at = {}
         acc, dx, first = {}, {}, {}
+        code_places = [WINDOWS]
+        scale_places = [WINDOWS + 36 * KIB]
+        late_places = [LATE_WOVEN]
 
-        def gather_g(c, kib, cuts_of_first=(0, S)):
-            g = place(f"g{c}", [P, PACK, S], F32, kib)
+        def take(places, size):
+            places.append(places[-1] + size)
+            return places[-2]
+
+        def gather_g(c, at, cuts_of_first=(0, S)):
+            g = place(f"g{c}", [P, PACK, S], F32, at)
             for h in range(2):
                 g_raw[c, h] = g[:, :, h * HALF : (h + 1) * HALF]
             for r in range(PACK):
@@ -111,65 +124,74 @@ def tile_moe_bdx_lin_none_kernel(tc, dyT, w, gate, offs, pos1, pos2, out):
                 src.rearrange("p r (x i) -> p x r i", i=4),
             )
 
-        def weave_pair(copy, dst, src):
-            copy(
-                dst.rearrange("p (u x i r) -> p u x r i", u=2, i=4, r=PACK),
-                src.rearrange("p u r (x i) -> p u x r i", i=4),
-            )
-
-        def quantise(name, woven, kib):
+        def quantise(name, woven, scales_at=None, codes_at=None):
             words = woven.shape[1] // PACK
-            if kib is None:
-                codes = held.tile([P, words], U32, name=f"codes_{name}", align_bytes=64)
-            else:
-                codes = place(f"codes_{name}", [P, words], U32, kib)
-            scales = held.tile([P, words], U8, name=f"scales_{name}", align_bytes=64)
+            if codes_at is None:
+                codes_at = take(code_places, 4 * words)
+            codes = place(f"codes_{name}", [P, words], U32, codes_at)
+            if scales_at is None:
+                scales_at = take(scale_places, words)
+            scales = place(f"scales_{name}", [P, words], U8, scales_at)
             nc.vector.quantize_mx(out=codes[:].bitcast(FP8X4), scales=scales[:], in_=woven)
             return codes, scales
 
-        def weave_g(c, h, kib):
-            g_woven[c, h] = place(f"g_woven{c}_{h}", [P, PACK * HALF], BF16, kib)[:]
+        def weave_g(c, h, at):
+            g_woven[c, h] = place(f"g_woven{c}_{h}", [P, PACK * HALF], BF16, at)[:]
             weave(nc.scalar.copy, g_woven[c, h], g_raw[c, h])
 
-        def quantise_g(c, h, kib=None):
-            g_mx[c, h] = quantise(f"g{c}_{h}", g_woven[c, h], kib)
+        def quantise_g(c, h, scales_at=None):
+            g_mx[c, h] = quantise(f"g{c}_{h}", g_woven[c, h], scales_at)
 
-        def weave_whole(i, kib):
-            piece = f"whole{i}"
-            w_woven[piece] = place(f"woven_{piece}", [P, PACK * K], BF16, kib)[:]
-            w_at.update({(i, kt): (piece, kt * P) for kt in range(4)})
-            weave(nc.scalar.copy, w_woven[piece], raw[i][:])
-
-        def weave_fronts(q, kib):
-            piece = f"fronts{q}"
-            w_woven[piece] = place(f"woven_{piece}", [P, PACK * 2 * FRONT], BF16, kib)[:]
-            w_at.update({(WHOLE + 2 * q + u, kt): (piece, u * FRONT + kt * P) for u in range(2) for kt in range(2)})
-            if q < PAIRS - 1:
-                weave_pair(nc.scalar.copy, w_woven[piece], fronts[q][:])
+        def weave_early(i):
+            q, u = divmod(i, 2)
+            for kt in range(4):
+                w_at[i, kt] = (f"early{q}_{kt // 2}", u * FRONT + (kt % 2) * P)
+            if i in HALVED:
+                for f in range(2):
+                    weave(nc.scalar.copy, early_woven[q][:, f, u, :], halves[i, f][:])
             else:
-                for u, copy in enumerate((nc.scalar.copy, nc.vector.tensor_copy)):
-                    weave(copy, w_woven[piece][:, u * PACK * FRONT : (u + 1) * PACK * FRONT], last_fronts[u][:])
+                nc.scalar.copy(
+                    early_woven[q][:, :, u, :].rearrange("p f (x i r) -> p f x r i", i=4, r=PACK),
+                    raw[i][:].rearrange("p r (f x i) -> p f x r i", f=2, i=4),
+                )
 
-        def weave_backs(q, kt, woven, copy):
-            piece = f"backs{q}_{kt}"
-            w_woven[piece] = woven
-            w_at.update({(WHOLE + 2 * q + u, kt): (piece, u * P) for u in range(2)})
-            weave_pair(copy, woven, backs[q][:, :, :, kt * P - FRONT : (kt + 1) * P - FRONT])
+        def quantise_early(q, f, scales_at):
+            woven = early_woven[q][:, f, :, :].rearrange("p u x -> p (u x)")
+            w_mx[f"early{q}_{f}"] = quantise(f"early{q}_{f}", woven, scales_at)
 
-        def quantise_w(piece, kib=None):
-            w_mx[piece] = quantise(piece, w_woven[piece], kib)
+        def weave_late(q, kts, copy, at=None):
+            piece = f"late{q}_{kts[0]}"
+            width = len(kts) * P
+            if at is None:
+                at = take(late_places, 2 * 2 * PACK * width)
+            w_woven[piece] = place(f"woven_{piece}", [P, 2 * PACK * width], BF16, at)[:]
+            for u in range(2):
+                for kt in kts:
+                    w_at[EARLY + 2 * q + u, kt] = (piece, u * width + (kt - kts[0]) * P)
+            if q == 0:
+                source = late_raw[:, :, :, kts[0] * P : kts[0] * P + width]
+            else:
+                source = late_halves[q, kts[0] // 2][:, :, :, kts[0] % 2 * P : kts[0] % 2 * P + width]
+            copy(
+                w_woven[piece].rearrange("p (u x i r) -> p u x r i", u=2, i=4, r=PACK),
+                source.rearrange("p u r (x i) -> p u x r i", i=4),
+            )
+            return at
 
-        def multiply(kt, experts, bank):
-            acc[kt, experts[0]] = psum.tile([P, len(experts) * C], F32, name=f"bank{bank}")
-            for at, e in enumerate(experts):
-                h, u = divmod(e, 2)
+        def quantise_late(q, kt, scales_at=None, codes_at=None):
+            piece = f"late{q}_{kt}"
+            w_mx[piece] = quantise(piece, w_woven[piece], scales_at, codes_at)
+
+        def multiply(kt, h):
+            acc[kt, h] = psum.tile([P, HALF], F32, name=f"bank{kt}_{h}")
+            for u in range(2):
                 slots = slice(u * C, (u + 1) * C)
                 for c in range(NPASS):
-                    piece, col = w_at[e * NPASS + c, kt]
+                    piece, col = w_at[(2 * h + u) * NPASS + c, kt]
                     w_codes, w_scales = w_mx[piece]
                     g_codes, g_scales = g_mx[c, h]
                     nc.tensor.matmul_mx(
-                        out=acc[kt, experts[0]][:, at * C : (at + 1) * C],
+                        out=acc[kt, h][:, slots],
                         lhsT=w_codes[:, col : col + P].bitcast(FP8X4),
                         lhsT_scale=w_scales[:, col : col + P],
                         rhs=g_codes[:, slots].bitcast(FP8X4),
@@ -178,19 +200,18 @@ def tile_moe_bdx_lin_none_kernel(tc, dyT, w, gate, offs, pos1, pos2, out):
                         stop=(c == NPASS - 1),
                     )
 
-        def empty(kt, e):
+        def empty(kt, h):
             if kt not in dx:
-                dx[kt] = place(f"dx{kt}", [P, S], F32, G0 + kt * WOVEN_KB)
-            bank = acc[kt, e]
-            nc.scalar.copy(dx[kt][:, e * C : e * C + bank.shape[1]], bank[:])
+                dx[kt] = place(f"dx{kt}", [P, S], F32, (LATE_RAW + 32 * KIB if kt < 2 else G0) + kt * 4 * KIB)
+            nc.scalar.copy(dx[kt][:, h * HALF : (h + 1) * HALF], acc[kt, h][:])
 
         def gather_first(kt):
-            first[kt] = place(f"first{kt}", [P, T], F32, G1 + RAW_KB + kt * CODES_KB)
+            first[kt] = place(f"first{kt}", [P, T], F32, G1 + 8 * KIB + kt * 2 * KIB)
             nc.vector.tensor_copy(first[kt][:], dx[kt][:].indirect(pos1_sb[:]))
 
-        def gather_second_and_store(kt, kib, cuts=(0, T)):
+        def gather_second_and_store(kt, at, cuts=(0, T)):
             for lo, hi in zip(cuts, cuts[1:]):
-                total = placed.tile([P, hi - lo], F32, name=f"total{kt}_{lo}", offset=kib * 1024 + 4 * lo, align_bytes=64)
+                total = place(f"total{kt}_{lo}", [P, hi - lo], F32, at + 4 * lo)
                 picked = dx[kt][:].indirect(pos2_sb[:, lo // PER_COL : hi // PER_COL])
                 nc.vector.tensor_tensor(total[:], picked, first[kt][:, lo:hi], ADD)
                 nc.sync.dma_start(out[kt * P : (kt + 1) * P, lo:hi], total[:])
@@ -201,95 +222,83 @@ def tile_moe_bdx_lin_none_kernel(tc, dyT, w, gate, offs, pos1, pos2, out):
             nc.sync.dma_start(gate_sb[:, lo:hi], gate[0:P, lo:hi])
         for i in range(NPASS):
             load_window(0, i + 1)
-            load_whole(i)
+            load_weight(i)
         load_window(1, 0)
-        load_whole(3)
         load_window(1, 1)
-        load_whole(4)
+        load_weight(3)
         load_window(1, 2)
+        load_weight(4)
         load_window(1, 3)
-        load_whole(5)
-        for q in range(PAIRS - 1):
-            load_fronts(q)
-            load_window(2, 2 * q)
-            load_window(2, 2 * q + 1)
-        load_fronts(PAIRS - 1)
+        load_window(2, 0)
+        for r in range(1, PACK):
+            load_weight(4 + r)
+            load_window(2, r)
+        load_late_halves(0)
         nc.sync.dma_start(pos1_sb[:], pos1)
         nc.sync.dma_start(pos2_sb[:], pos2)
-        for q in range(PAIRS):
-            load_backs(q)
+        load_late_halves(1)
 
         gather_g(0, G0, (0, FIRST_CUT, S))
-        for i in range(NPASS):
-            weave_whole(i, STAGE + i * WOVEN_KB)
+        for i in range(3):
+            weave_early(i)
         for h in range(2):
-            weave_g(0, h, raw_place(2) + h * WOVEN_KB)
-        quantise_w("whole0")
-        quantise_w("whole1")
-
+            weave_g(0, h, raw_place(2) + (1 - h) * 4 * KIB)
         gather_g(1, G1)
-        weave_whole(3, STAGE + 3 * WOVEN_KB)
-        quantise_w("whole2")
+        for i in range(3, 6):
+            weave_early(i)
         for h in range(2):
-            quantise_g(0, h)
-        weave_whole(4, STAGE)
-        quantise_w("whole3")
-        weave_whole(5, STAGE + WOVEN_KB)
+            weave_g(1, h, raw_place(4) + h * 4 * KIB)
+        gather_g(2, raw_place(0))
+        weave_late(0, (0, 1), nc.scalar.copy)
+        weave_late(0, (2,), nc.scalar.copy)
+        for h in range(2):
+            weave_g(2, h, raw_place(3) + h * 4 * KIB)
 
-        gather_g(2, raw_place(3))
-        weave_fronts(0, raw_place(0) + WOVEN_KB)
-        weave_g(1, 0, raw_place(5))
-        weave_g(1, 1, FRONTS)
-        quantise_w("whole4", LAST_WINDOW)
-        quantise_w("whole5", LAST_WINDOW + CODES_KB)
-        quantise_w("fronts0", GATE)
-        quantise_g(1, 0, GATE + CODES_KB)
-        quantise_g(1, 1)
-        weave_fronts(1, raw_place(1) + WOVEN_KB)
-        quantise_w("fronts1", LATE_CODES)
-        weave_fronts(2, raw_place(1))
-        quantise_w("fronts2", LATE_CODES + CODES_KB)
-
-        weave_g(2, 0, FRONTS + RAW_KB)
-        quantise_g(2, 0)
-        for kt, banks in ((0, (0, 1)), (1, (6, 7))):
-            for e in range(2):
-                multiply(kt, [e], banks[e])
-        weave_g(2, 1, last_place)
-        quantise_g(2, 1)
-        for kt, banks in ((0, (2, 3)), (1, (4, 5))):
-            for u in range(2):
-                multiply(kt, [2 + u], banks[u])
-
-        quarter = PACK * 2 * P
-        woven2 = place("woven_backs_2", [P, PAIRS * quarter], BF16, last_place)
         for q in range(PAIRS):
-            weave_backs(q, 2, woven2[:, q * quarter : (q + 1) * quarter], nc.vector.tensor_copy)
+            quantise_early(q, 0, GATE + q * 512)
+        for c in range(2):
+            for h in range(2):
+                quantise_g(c, h, GATE + (3 + 2 * c + h) * 512)
+        quantise_late(0, 0, GATE + 7 * 512)
+        weave_late(1, (0,), nc.vector.tensor_copy, LAST_WINDOW)
+        quantise_late(1, 0)
+        quantise_g(2, 0)
+        weave_late(2, (0,), nc.vector.tensor_copy, LAST_WINDOW + 2 * KIB)
+        quantise_g(2, 1)
+        last = take(late_places, 10 * KIB)
+        quantise_late(2, 0, last + 5 * KIB)
+        multiply(0, 0)
+        multiply(1, 0)
+        multiply(0, 1)
+        for q in (1, 2):
+            woven1 = weave_late(q, (1,), nc.scalar.copy)
+        quantise_late(1, 1)
+        quantise_late(2, 1, last + 2 * KIB - 128, last + 8 * KIB - 512)
+        multiply(1, 1)
+        for q in range(PAIRS):
+            quantise_early(q, 1, woven1 + q * 512)
+        quantise_late(0, 2, woven1 + PAIRS * 512)
+        multiply(2, 0)
+        multiply(3, 0)
         for h in range(2):
             for kt in range(2):
-                for u in range(2):
-                    empty(kt, 2 * h + u)
-        for q in range(PAIRS):
-            quantise_w(f"backs{q}_2")
-
-        multiply(2, [0, 1], 0)
-        multiply(2, [2, 3], 1)
-        woven3_places = (GATE, LATE_CODES, LATE_CODES + CODES_KB)
-        for q in range(PAIRS):
-            weave_backs(q, 3, place(f"woven_backs{q}_3", [P, quarter], BF16, woven3_places[q])[:], nc.scalar.copy)
-        for q in range(PAIRS):
-            quantise_w(f"backs{q}_3")
-        multiply(3, [0, 1], 6)
-        multiply(3, [2, 3], 7)
-
+                empty(kt, h)
+        late = ((1, 2), (2, 2), (0, 3), (1, 3), (2, 3))
+        late_at = [last + 2 * KIB * j for j in range(5)]
+        for (q, kt), at in zip(late, late_at):
+            last_woven = weave_late(q, (kt,), nc.scalar.copy, at)
         gather_first(0)
         gather_first(1)
         gather_second_and_store(0, G1)
-        gather_second_and_store(1, woven3_places[-1])
-        for e in (0, 2):
+        for q, kt in late:
+            quantise_late(q, kt)
+        multiply(2, 1)
+        multiply(3, 1)
+        gather_second_and_store(1, last_woven)
+        for h in range(2):
             for kt in (2, 3):
-                empty(kt, e)
+                empty(kt, h)
         gather_first(2)
         gather_first(3)
-        gather_second_and_store(2, G1 + CODES_KB)
-        gather_second_and_store(3, G1 + 2 * CODES_KB, (0, LAST_CUT, T))
+        gather_second_and_store(2, G1 + 2 * KIB)
+        gather_second_and_store(3, G1 + 4 * KIB, (0, LAST_CUT, T))

@@ -14,21 +14,29 @@ PER_COL = 16
 WINDOW = S + 8
 EARLY = 2 * NPASS
 PAIRS = NPASS
-HALVED = (1, 2)
+HALVED = 2
 FIRST_CUT = C
 LAST_CUT = T - P
 
 KIB = 1024
+RAW_TILE = 8 * KIB
+WIDE = 4 * KIB
+PIECE = 2 * KIB
+WIDE_SCALES = 512
+PIECE_CODES, PIECE_SCALES = KIB, 256
 WINDOW_BYTES = 65 * 64
+ALL_CODES = 36 * KIB
+
 WINDOWS = 0
-LAST_WINDOW = WINDOWS + 11 * WINDOW_BYTES
-GATE = WINDOWS + 12 * WINDOW_BYTES
-RAW = GATE + 4 * KIB
-LATE_RAW = RAW + EARLY * 8 * KIB
-G0 = LATE_RAW + PAIRS * 16 * KIB
-G1 = G0 + 16 * KIB
-EARLY_WOVEN = G1 + 16 * KIB
-LATE_WOVEN = EARLY_WOVEN + PAIRS * 8 * KIB
+LAST_WINDOW = WINDOWS + (NPASS * PACK - 1) * WINDOW_BYTES
+GATE = LAST_WINDOW + WINDOW_BYTES
+RAW = GATE + 4 * S
+LATE_RAW = RAW + EARLY * RAW_TILE
+LAST_FRONTS = LATE_RAW + 4 * RAW_TILE
+G0 = LATE_RAW + PAIRS * 2 * RAW_TILE
+G1 = G0 + 2 * RAW_TILE
+EARLY_WOVEN = G1 + 2 * RAW_TILE
+FRESH = EARLY_WOVEN + PAIRS * RAW_TILE
 
 F32 = mybir.dt.float32
 BF16 = mybir.dt.bfloat16
@@ -54,7 +62,7 @@ def tile_moe_bdx_lin_none_kernel(tc, dyT, w, gate, offs, pos1, pos2, out):
             return placed.tile(shape, dtype, name=name, offset=at, align_bytes=64)
 
         def raw_place(i):
-            return RAW + i * 8 * KIB
+            return RAW + i * RAW_TILE
 
         offs_sb = held.tile([P, S // PER_COL], U16, name="offs_sb")
         pos1_sb = held.tile([P, T // PER_COL], U16, name="pos1_sb")
@@ -67,11 +75,15 @@ def tile_moe_bdx_lin_none_kernel(tc, dyT, w, gate, offs, pos1, pos2, out):
                 windows[c, r] = place(f"window{c}_{r}", [P, WINDOW], F32, WINDOWS + (c * PACK + r) * WINDOW_BYTES)
                 nc.gpsimd.memset(windows[c, r][:, T:], 0.0)
 
-        raw = {i: place(f"raw{i}", [P, PACK, K], F32, raw_place(i)) for i in range(EARLY) if i not in HALVED}
-        halves = {(i, f): place(f"raw{i}_{f}", [P, PACK, FRONT], F32, raw_place(i) + f * 4 * KIB) for i in HALVED for f in range(2)}
-        late_raw = place("late_raw", [P, 2, PACK, K], F32, LATE_RAW)
-        late_halves = {(q, f): place(f"late_raw{q}_{f}", [P, 2, PACK, FRONT], F32, LATE_RAW + (2 * q + f) * 8 * KIB) for q in (1, 2) for f in range(2)}
-        early_woven = [place(f"early_woven{q}", [P, 2, 2, PACK * FRONT], BF16, EARLY_WOVEN + q * 8 * KIB) for q in range(PAIRS)]
+        raw = {i: place(f"raw{i}", [P, PACK, K], F32, raw_place(i)) for i in range(EARLY) if i != HALVED}
+        raw_halves = [place(f"raw_half{f}", [P, PACK, FRONT], F32, raw_place(HALVED) + f * WIDE) for f in range(2)]
+        raw_pair0 = place("raw_pair0", [P, 2, PACK, K], F32, LATE_RAW)
+        raw_pair_halves = {
+            (q, f): place(f"raw_pair{q}_{f}", [P, 2, PACK, FRONT], F32, LATE_RAW + (2 * q + f) * RAW_TILE)
+            for q in range(1, PAIRS)
+            for f in range(2)
+        }
+        early_woven = [place(f"early_woven{q}", [P, 2, 2, PACK * FRONT], BF16, EARLY_WOVEN + q * RAW_TILE) for q in range(PAIRS)]
 
         def load_window(c, r):
             rows = dyT[c * PASS : (c + 1) * PASS, :].rearrange("(p r) t -> p r t", r=PACK)
@@ -81,32 +93,28 @@ def tile_moe_bdx_lin_none_kernel(tc, dyT, w, gate, offs, pos1, pos2, out):
             e, c = divmod(i, NPASS)
             return w[e, c * PASS : (c + 1) * PASS, :].rearrange("(p r) k -> p r k", r=PACK)
 
-        def load_late_halves(f):
-            for q in (1, 2):
-                for u in range(2):
-                    nc.sync.dma_start(late_halves[q, f][:, u, :, :], weight_rows(EARLY + 2 * q + u)[:, :, f * FRONT : (f + 1) * FRONT])
+        def weight_half(i, f):
+            return weight_rows(i)[:, :, f * FRONT : (f + 1) * FRONT]
 
-        def load_weight(i):
-            rows = weight_rows(i)
-            if i in HALVED:
-                for f in range(2):
-                    nc.sync.dma_start(halves[i, f][:], rows[:, :, f * FRONT : (f + 1) * FRONT])
-            elif i < EARLY:
-                nc.sync.dma_start(raw[i][:], rows)
-            else:
-                nc.sync.dma_start(late_raw[:, i - EARLY, :, :], rows)
+        def load_whole(i):
+            into = raw[i][:] if i < EARLY else raw_pair0[:, i - EARLY, :, :]
+            nc.sync.dma_start(into, weight_rows(i))
+
+        def load_pair_halves(f):
+            for q in range(1, PAIRS):
+                for u in range(2):
+                    nc.sync.dma_start(raw_pair_halves[q, f][:, u, :, :], weight_half(EARLY + 2 * q + u, f))
 
         g_raw, g_woven, g_mx = {}, {}, {}
-        w_woven, w_mx = {}, {}
-        w_at = {}
+        late_woven = {}
+        w_mx = {}
         acc, dx, first = {}, {}, {}
-        code_places = [WINDOWS]
-        scale_places = [WINDOWS + 36 * KIB]
-        late_places = [LATE_WOVEN]
+        next_free = {"codes": WINDOWS, "scales": WINDOWS + ALL_CODES, "fresh": FRESH}
+        taken = {kind: [] for kind in next_free}
 
-        def take(places, size):
-            places.append(places[-1] + size)
-            return places[-2]
+        def take(kind, size):
+            taken[kind].append(size)
+            return next_free[kind] + sum(taken[kind]) - size
 
         def gather_g(c, at, cuts_of_first=(0, S)):
             g = place(f"g{c}", [P, PACK, S], F32, at)
@@ -118,95 +126,110 @@ def tile_moe_bdx_lin_none_kernel(tc, dyT, w, gate, offs, pos1, pos2, out):
                     picked = windows[c, r][:].indirect(offs_sb[:, lo // PER_COL : hi // PER_COL])
                     nc.vector.tensor_tensor(g[:, r, lo:hi], picked, gate_sb[:, lo:hi], MULT)
 
-        def weave(copy, dst, src):
-            copy(
+        def weave(dst, src):
+            nc.scalar.copy(
                 dst.rearrange("p (x i r) -> p x r i", i=4, r=PACK),
                 src.rearrange("p r (x i) -> p x r i", i=4),
             )
 
-        def quantise(name, woven, scales_at=None, codes_at=None):
+        def quantise(name, woven, scales_at, codes_at=None):
             words = woven.shape[1] // PACK
             if codes_at is None:
-                codes_at = take(code_places, 4 * words)
+                codes_at = take("codes", 4 * words)
             codes = place(f"codes_{name}", [P, words], U32, codes_at)
             if scales_at is None:
-                scales_at = take(scale_places, words)
+                scales_at = take("scales", words)
             scales = place(f"scales_{name}", [P, words], U8, scales_at)
             nc.vector.quantize_mx(out=codes[:].bitcast(FP8X4), scales=scales[:], in_=woven)
             return codes, scales
 
         def weave_g(c, h, at):
             g_woven[c, h] = place(f"g_woven{c}_{h}", [P, PACK * HALF], BF16, at)[:]
-            weave(nc.scalar.copy, g_woven[c, h], g_raw[c, h])
+            weave(g_woven[c, h], g_raw[c, h])
 
         def quantise_g(c, h, scales_at=None):
             g_mx[c, h] = quantise(f"g{c}_{h}", g_woven[c, h], scales_at)
 
-        def weave_early(i):
+        def weave_whole(i):
             q, u = divmod(i, 2)
-            for kt in range(4):
-                w_at[i, kt] = (f"early{q}_{kt // 2}", u * FRONT + (kt % 2) * P)
-            if i in HALVED:
-                for f in range(2):
-                    weave(nc.scalar.copy, early_woven[q][:, f, u, :], halves[i, f][:])
-            else:
-                nc.scalar.copy(
-                    early_woven[q][:, :, u, :].rearrange("p f (x i r) -> p f x r i", i=4, r=PACK),
-                    raw[i][:].rearrange("p r (f x i) -> p f x r i", f=2, i=4),
-                )
+            nc.scalar.copy(
+                early_woven[q][:, :, u, :].rearrange("p f (x i r) -> p f x r i", i=4, r=PACK),
+                raw[i][:].rearrange("p r (f x i) -> p f x r i", f=2, i=4),
+            )
+
+        def weave_half(f):
+            q, u = divmod(HALVED, 2)
+            weave(early_woven[q][:, f, u, :], raw_halves[f][:])
+
+        def hand_out(mx, tiles, kts):
+            for at, key in enumerate([(i, kt) for i in tiles for kt in kts]):
+                w_mx[key] = [part[:, at * P : (at + 1) * P] for part in mx]
 
         def quantise_early(q, f, scales_at):
             woven = early_woven[q][:, f, :, :].rearrange("p u x -> p (u x)")
-            w_mx[f"early{q}_{f}"] = quantise(f"early{q}_{f}", woven, scales_at)
+            hand_out(quantise(f"early{q}_{f}", woven, scales_at), (2 * q, 2 * q + 1), (2 * f, 2 * f + 1))
 
         def weave_late(q, kts, copy, at=None):
-            piece = f"late{q}_{kts[0]}"
             width = len(kts) * P
             if at is None:
-                at = take(late_places, 2 * 2 * PACK * width)
-            w_woven[piece] = place(f"woven_{piece}", [P, 2 * PACK * width], BF16, at)[:]
-            for u in range(2):
-                for kt in kts:
-                    w_at[EARLY + 2 * q + u, kt] = (piece, u * width + (kt - kts[0]) * P)
+                at = take("fresh", len(kts) * PIECE)
+            woven = place(f"late_woven{q}_{kts[0]}", [P, 2 * PACK * width], BF16, at)[:]
+            late_woven[q, kts[0]] = woven, kts
             if q == 0:
-                source = late_raw[:, :, :, kts[0] * P : kts[0] * P + width]
+                source, col = raw_pair0, kts[0] * P
             else:
-                source = late_halves[q, kts[0] // 2][:, :, :, kts[0] % 2 * P : kts[0] % 2 * P + width]
+                source, col = raw_pair_halves[q, kts[0] // 2], kts[0] % 2 * P
             copy(
-                w_woven[piece].rearrange("p (u x i r) -> p u x r i", u=2, i=4, r=PACK),
-                source.rearrange("p u r (x i) -> p u x r i", i=4),
+                woven.rearrange("p (u x i r) -> p u x r i", u=2, i=4, r=PACK),
+                source[:, :, :, col : col + width].rearrange("p u r (x i) -> p u x r i", i=4),
             )
             return at
 
         def quantise_late(q, kt, scales_at=None, codes_at=None):
-            piece = f"late{q}_{kt}"
-            w_mx[piece] = quantise(piece, w_woven[piece], scales_at, codes_at)
+            woven, kts = late_woven[q, kt]
+            hand_out(quantise(f"late{q}_{kt}", woven, scales_at, codes_at), (EARLY + 2 * q, EARLY + 2 * q + 1), kts)
 
-        def multiply(kt, h):
-            acc[kt, h] = psum.tile([P, HALF], F32, name=f"bank{kt}_{h}")
+        def group(into, e, kt):
+            h, u = divmod(e, 2)
+            slots = slice(u * C, (u + 1) * C)
+            for c in range(NPASS):
+                w_codes, w_scales = w_mx[e * NPASS + c, kt]
+                g_codes, g_scales = g_mx[c, h]
+                nc.tensor.matmul_mx(
+                    out=into,
+                    lhsT=w_codes.bitcast(FP8X4),
+                    lhsT_scale=w_scales,
+                    rhs=g_codes[:, slots].bitcast(FP8X4),
+                    rhs_scale=g_scales[:, slots],
+                    start=(c == 0),
+                    stop=(c == NPASS - 1),
+                )
+
+        def multiply_front(kt, h):
+            acc[kt, h] = []
             for u in range(2):
-                slots = slice(u * C, (u + 1) * C)
-                for c in range(NPASS):
-                    piece, col = w_at[(2 * h + u) * NPASS + c, kt]
-                    w_codes, w_scales = w_mx[piece]
-                    g_codes, g_scales = g_mx[c, h]
-                    nc.tensor.matmul_mx(
-                        out=acc[kt, h][:, slots],
-                        lhsT=w_codes[:, col : col + P].bitcast(FP8X4),
-                        lhsT_scale=w_scales[:, col : col + P],
-                        rhs=g_codes[:, slots].bitcast(FP8X4),
-                        rhs_scale=g_scales[:, slots],
-                        start=(c == 0),
-                        stop=(c == NPASS - 1),
-                    )
+                bank = psum.tile([P, HALF], F32, name=f"bank{kt}_{h}_{u}")
+                acc[kt, h].append(bank[:, 0:C])
+                group(bank[:, 0:C], 2 * h + u, kt)
 
-        def empty(kt, h):
-            if kt not in dx:
-                dx[kt] = place(f"dx{kt}", [P, S], F32, (LATE_RAW + 32 * KIB if kt < 2 else G0) + kt * 4 * KIB)
-            nc.scalar.copy(dx[kt][:, h * HALF : (h + 1) * HALF], acc[kt, h][:])
+        def multiply_back(kt, h):
+            bank = psum.tile([P, HALF], F32, name=f"bank{kt - 2}_{h}_0")
+            acc[kt, h] = [bank[:]]
+            for u in range(2):
+                group(bank[:, u * C : (u + 1) * C], 2 * h + u, kt)
+
+        def empty(kts, at):
+            for h in range(2):
+                for kt in kts:
+                    if h == 0:
+                        dx[kt] = place(f"dx{kt}", [P, S], F32, at + kt % 2 * WIDE)
+                    col = h * HALF
+                    for sums in acc[kt, h]:
+                        nc.scalar.copy(dx[kt][:, col : col + sums.shape[1]], sums)
+                        col = col + sums.shape[1]
 
         def gather_first(kt):
-            first[kt] = place(f"first{kt}", [P, T], F32, G1 + 8 * KIB + kt * 2 * KIB)
+            first[kt] = place(f"first{kt}", [P, T], F32, G1 + RAW_TILE + kt * PIECE)
             nc.vector.tensor_copy(first[kt][:], dx[kt][:].indirect(pos1_sb[:]))
 
         def gather_second_and_store(kt, at, cuts=(0, T)):
@@ -216,89 +239,91 @@ def tile_moe_bdx_lin_none_kernel(tc, dyT, w, gate, offs, pos1, pos2, out):
                 nc.vector.tensor_tensor(total[:], picked, first[kt][:, lo:hi], ADD)
                 nc.sync.dma_start(out[kt * P : (kt + 1) * P, lo:hi], total[:])
 
-        nc.sync.dma_start(offs_sb[:], offs)
         load_window(0, 0)
+        nc.sync.dma_start(offs_sb[:], offs)
         for lo, hi in ((0, FIRST_CUT), (FIRST_CUT, S)):
             nc.sync.dma_start(gate_sb[:, lo:hi], gate[0:P, lo:hi])
-        for i in range(NPASS):
-            load_window(0, i + 1)
-            load_weight(i)
-        load_window(1, 0)
+        for i in range(HALVED):
+            load_window(0, 1 + i)
+            load_whole(i)
+        for f, (c, r) in enumerate(((0, PACK - 1), (1, 0))):
+            load_window(c, r)
+            nc.sync.dma_start(raw_halves[f][:], weight_half(HALVED, f))
         load_window(1, 1)
-        load_weight(3)
+        load_whole(3)
         load_window(1, 2)
-        load_weight(4)
         load_window(1, 3)
-        load_window(2, 0)
-        for r in range(1, PACK):
-            load_weight(4 + r)
+        for r in range(PACK):
+            load_whole(4 + r)
             load_window(2, r)
-        load_late_halves(0)
+        load_pair_halves(0)
         nc.sync.dma_start(pos1_sb[:], pos1)
         nc.sync.dma_start(pos2_sb[:], pos2)
-        load_late_halves(1)
+        load_pair_halves(1)
 
         gather_g(0, G0, (0, FIRST_CUT, S))
-        for i in range(3):
-            weave_early(i)
-        for h in range(2):
-            weave_g(0, h, raw_place(2) + (1 - h) * 4 * KIB)
+        weave_whole(0)
+        weave_whole(1)
+        weave_half(0)
+        weave_g(0, 0, raw_place(HALVED))
+        weave_g(0, 1, raw_place(1))
         gather_g(1, G1)
-        for i in range(3, 6):
-            weave_early(i)
+        weave_half(1)
+        weave_whole(3)
+        weave_whole(4)
         for h in range(2):
-            weave_g(1, h, raw_place(4) + h * 4 * KIB)
-        gather_g(2, raw_place(0))
+            weave_g(1, h, raw_place(4) + h * WIDE)
+        gather_g(2, G0)
+        weave_whole(5)
         weave_late(0, (0, 1), nc.scalar.copy)
         weave_late(0, (2,), nc.scalar.copy)
         for h in range(2):
-            weave_g(2, h, raw_place(3) + h * 4 * KIB)
+            weave_g(2, h, raw_place(5) + h * WIDE)
 
-        for q in range(PAIRS):
-            quantise_early(q, 0, GATE + q * 512)
+        quantise_early(0, 0, take("fresh", WIDE_SCALES))
+        on_gate = [GATE + j * WIDE_SCALES for j in range(4 * S // WIDE_SCALES)]
+        for q in range(1, PAIRS):
+            quantise_early(q, 0, on_gate[q])
         for c in range(2):
             for h in range(2):
-                quantise_g(c, h, GATE + (3 + 2 * c + h) * 512)
-        quantise_late(0, 0, GATE + 7 * 512)
-        weave_late(1, (0,), nc.vector.tensor_copy, LAST_WINDOW)
-        quantise_late(1, 0)
+                quantise_g(c, h, on_gate[PAIRS + 2 * c + h])
+        quantise_late(0, 0, on_gate[-1])
+        for q in range(1, PAIRS):
+            weave_late(q, (0,), nc.vector.tensor_copy, LAST_WINDOW + (q - 1) * PIECE)
         quantise_g(2, 0)
-        weave_late(2, (0,), nc.vector.tensor_copy, LAST_WINDOW + 2 * KIB)
+        quantise_late(1, 0)
         quantise_g(2, 1)
-        last = take(late_places, 10 * KIB)
-        quantise_late(2, 0, last + 5 * KIB)
-        multiply(0, 0)
-        multiply(1, 0)
-        multiply(0, 1)
-        for q in (1, 2):
-            woven1 = weave_late(q, (1,), nc.scalar.copy)
+
+        last_pieces = ((1, 2), (2, 2), (0, 3), (1, 3), (2, 3))
+        last_places = [take("fresh", PIECE) for piece in last_pieces]
+        quantise_late(2, 0, last_places[2] + PIECE // 2)
+        multiply_front(0, 0)
+        multiply_front(1, 0)
+        multiply_front(0, 1)
+        row1_places = [weave_late(q, (1,), nc.scalar.copy) for q in range(1, PAIRS)]
         quantise_late(1, 1)
-        quantise_late(2, 1, last + 2 * KIB - 128, last + 8 * KIB - 512)
-        multiply(1, 1)
+        quantise_late(2, 1, last_places[1] - PIECE_SCALES // 2, last_places[4] - PIECE_CODES // 2)
+        multiply_front(1, 1)
+
         for q in range(PAIRS):
-            quantise_early(q, 1, woven1 + q * 512)
-        quantise_late(0, 2, woven1 + PAIRS * 512)
-        multiply(2, 0)
-        multiply(3, 0)
-        for h in range(2):
-            for kt in range(2):
-                empty(kt, h)
-        late = ((1, 2), (2, 2), (0, 3), (1, 3), (2, 3))
-        late_at = [last + 2 * KIB * j for j in range(5)]
-        for (q, kt), at in zip(late, late_at):
-            last_woven = weave_late(q, (kt,), nc.scalar.copy, at)
+            quantise_early(q, 1, row1_places[-1] + q * WIDE_SCALES)
+        quantise_late(0, 2, row1_places[-1] + PAIRS * WIDE_SCALES)
+        empty((0, 1), LAST_FRONTS)
+        multiply_back(2, 0)
+        multiply_back(3, 0)
+        for (q, kt), at in zip(last_pieces, last_places):
+            weave_late(q, (kt,), nc.scalar.copy, at)
+
         gather_first(0)
         gather_first(1)
         gather_second_and_store(0, G1)
-        for q, kt in late:
+        for q, kt in last_pieces:
             quantise_late(q, kt)
-        multiply(2, 1)
-        multiply(3, 1)
-        gather_second_and_store(1, last_woven)
-        for h in range(2):
-            for kt in (2, 3):
-                empty(kt, h)
+        multiply_back(2, 1)
+        multiply_back(3, 1)
+        gather_second_and_store(1, last_places[-2])
+        empty((2, 3), RAW)
         gather_first(2)
         gather_first(3)
-        gather_second_and_store(2, G1 + 2 * KIB)
-        gather_second_and_store(3, G1 + 4 * KIB, (0, LAST_CUT, T))
+        gather_second_and_store(2, G1 + PIECE)
+        gather_second_and_store(3, G1 + 2 * PIECE, (0, LAST_CUT, T))

@@ -128,8 +128,8 @@ def tile_moe_bdx_lin_none_kernel(tc, dyT, w, gate, offs, pos1, pos2, out):
 
         def weave(dst, src):
             nc.scalar.copy(
-                dst.rearrange("p (x i r) -> p x r i", i=4, r=PACK),
-                src.rearrange("p r (x i) -> p x r i", i=4),
+                dst.rearrange("p (x i r) -> p x r i", i=2, r=PACK),
+                src.rearrange("p r (x i) -> p x r i", i=2),
             )
 
         def quantise(name, woven, scales_at, codes_at=None):
@@ -153,8 +153,8 @@ def tile_moe_bdx_lin_none_kernel(tc, dyT, w, gate, offs, pos1, pos2, out):
         def weave_whole(i):
             q, u = divmod(i, 2)
             nc.scalar.copy(
-                early_woven[q][:, :, u, :].rearrange("p f (x i r) -> p f x r i", i=4, r=PACK),
-                raw[i][:].rearrange("p r (f x i) -> p f x r i", f=2, i=4),
+                early_woven[q][:, :, u, :].rearrange("p f (x i r) -> p f x r i", i=2, r=PACK),
+                raw[i][:].rearrange("p r (f x i) -> p f x r i", f=2, i=2),
             )
 
         def weave_half(f):
@@ -169,7 +169,7 @@ def tile_moe_bdx_lin_none_kernel(tc, dyT, w, gate, offs, pos1, pos2, out):
             woven = early_woven[q][:, f, :, :].rearrange("p u x -> p (u x)")
             hand_out(quantise(f"early{q}_{f}", woven, scales_at), (2 * q, 2 * q + 1), (2 * f, 2 * f + 1))
 
-        def weave_late(q, kts, copy, at=None):
+        def weave_late(q, kts, copy, at=None, i=2):
             width = len(kts) * P
             if at is None:
                 at = take("fresh", len(kts) * PIECE)
@@ -180,8 +180,8 @@ def tile_moe_bdx_lin_none_kernel(tc, dyT, w, gate, offs, pos1, pos2, out):
             else:
                 source, col = raw_pair_halves[q, kts[0] // 2], kts[0] % 2 * P
             copy(
-                woven.rearrange("p (u x i r) -> p u x r i", u=2, i=4, r=PACK),
-                source[:, :, :, col : col + width].rearrange("p u r (x i) -> p u x r i", i=4),
+                woven.rearrange("p (u x i r) -> p u x r i", u=2, i=i, r=PACK),
+                source[:, :, :, col : col + width].rearrange("p u r (x i) -> p u x r i", i=i),
             )
             return at
 
@@ -289,7 +289,7 @@ def tile_moe_bdx_lin_none_kernel(tc, dyT, w, gate, offs, pos1, pos2, out):
                 quantise_g(c, h, on_gate[PAIRS + 2 * c + h])
         quantise_late(0, 0, on_gate[-1])
         for q in range(1, PAIRS):
-            weave_late(q, (0,), nc.vector.tensor_copy, LAST_WINDOW + (q - 1) * PIECE)
+            weave_late(q, (0,), nc.vector.tensor_copy, LAST_WINDOW + (q - 1) * PIECE, 4)
         quantise_g(2, 0)
         quantise_late(1, 0)
         quantise_g(2, 1)

@@ -75,9 +75,8 @@ def tile_moe_bdx_lin_none_kernel(tc, dyT, w, gate, offs, pos1, pos2, out):
                 windows[c, r] = place(f"window{c}_{r}", [P, WINDOW], F32, WINDOWS + (c * PACK + r) * WINDOW_BYTES)
                 nc.gpsimd.memset(windows[c, r][:, T:], 0.0)
 
-        raw = {i: place(f"raw{i}", [P, PACK, K], F32, raw_place(i)) for i in range(EARLY) if i != HALVED}
+        raw = {i: place(f"raw{i}", [P, PACK, K], F32, raw_place(i)) for i in range(EARLY + 2) if i != HALVED}
         raw_halves = [place(f"raw_half{f}", [P, PACK, FRONT], F32, raw_place(HALVED) + f * WIDE) for f in range(2)]
-        raw_pair0 = place("raw_pair0", [P, 2, PACK, K], F32, LATE_RAW)
         raw_pair_halves = {
             (q, f): place(f"raw_pair{q}_{f}", [P, 2, PACK, FRONT], F32, LATE_RAW + (2 * q + f) * RAW_TILE)
             for q in range(1, PAIRS)
@@ -97,8 +96,7 @@ def tile_moe_bdx_lin_none_kernel(tc, dyT, w, gate, offs, pos1, pos2, out):
             return weight_rows(i)[:, :, f * FRONT : (f + 1) * FRONT]
 
         def load_whole(i):
-            into = raw[i][:] if i < EARLY else raw_pair0[:, i - EARLY, :, :]
-            nc.sync.dma_start(into, weight_rows(i))
+            nc.sync.dma_start(raw[i][:], weight_rows(i))
 
         def load_pair_halves(f):
             for q in range(1, PAIRS):
@@ -157,6 +155,20 @@ def tile_moe_bdx_lin_none_kernel(tc, dyT, w, gate, offs, pos1, pos2, out):
                 raw[i][:].rearrange("p r (f x i) -> p f x r i", f=2, i=2),
             )
 
+        def weave_six():
+            nc.scalar.copy(
+                woven_six[:].rearrange("p f (x i r) -> p f x r i", i=2, r=PACK),
+                raw[EARLY][:].rearrange("p r (f x i) -> p f x r i", f=2, i=2),
+            )
+
+        def quantise_six(f, scales_at):
+            hand_out(quantise(f"six{f}", woven_six[:, f, :], scales_at), (EARLY,), (2 * f, 2 * f + 1))
+
+        def weave_seven(f, at):
+            woven = place(f"woven_seven{f}", [P, PACK * FRONT], BF16, at)[:]
+            late_woven[0, 2 * f] = woven, (2 * f, 2 * f + 1)
+            weave(woven, raw[EARLY + 1][:, :, f * FRONT : (f + 1) * FRONT])
+
         def weave_half(f):
             q, u = divmod(HALVED, 2)
             weave(early_woven[q][:, f, u, :], raw_halves[f][:])
@@ -169,25 +181,22 @@ def tile_moe_bdx_lin_none_kernel(tc, dyT, w, gate, offs, pos1, pos2, out):
             woven = early_woven[q][:, f, :, :].rearrange("p u x -> p (u x)")
             hand_out(quantise(f"early{q}_{f}", woven, scales_at), (2 * q, 2 * q + 1), (2 * f, 2 * f + 1))
 
-        def weave_late(q, kts, copy, at=None, i=2):
+        def weave_late(q, kts, copy, at=None):
             width = len(kts) * P
             if at is None:
                 at = take("fresh", len(kts) * PIECE)
             woven = place(f"late_woven{q}_{kts[0]}", [P, 2 * PACK * width], BF16, at)[:]
             late_woven[q, kts[0]] = woven, kts
-            if q == 0:
-                source, col = raw_pair0, kts[0] * P
-            else:
-                source, col = raw_pair_halves[q, kts[0] // 2], kts[0] % 2 * P
+            source, col = raw_pair_halves[q, kts[0] // 2], kts[0] % 2 * P
             copy(
-                woven.rearrange("p (u x i r) -> p u x r i", u=2, i=i, r=PACK),
-                source[:, :, :, col : col + width].rearrange("p u r (x i) -> p u x r i", i=i),
+                woven.rearrange("p (u x i r) -> p u x r i", u=2, i=2, r=PACK),
+                source[:, :, :, col : col + width].rearrange("p u r (x i) -> p u x r i", i=2),
             )
             return at
 
         def quantise_late(q, kt, scales_at=None, codes_at=None):
             woven, kts = late_woven[q, kt]
-            hand_out(quantise(f"late{q}_{kt}", woven, scales_at, codes_at), (EARLY + 2 * q, EARLY + 2 * q + 1), kts)
+            hand_out(quantise(f"late{q}_{kt}", woven, scales_at, codes_at), (EARLY + 2 * q, EARLY + 2 * q + 1) if q else (EARLY + 1,), kts)
 
         def group(into, e, kt):
             h, u = divmod(e, 2)
@@ -219,10 +228,9 @@ def tile_moe_bdx_lin_none_kernel(tc, dyT, w, gate, offs, pos1, pos2, out):
                 group(bank[:, u * C : (u + 1) * C], 2 * h + u, kt)
 
         def empty(kts, at):
-            for h in range(2):
-                for kt in kts:
-                    if h == 0:
-                        dx[kt] = place(f"dx{kt}", [P, S], F32, at + kt % 2 * WIDE)
+            for kt in kts:
+                dx[kt] = place(f"dx{kt}", [P, S], F32, at + kt % 2 * WIDE)
+                for h in range(2):
                     col = h * HALF
                     for sums in acc[kt, h]:
                         nc.scalar.copy(dx[kt][:, col : col + sums.shape[1]], sums)
@@ -246,16 +254,19 @@ def tile_moe_bdx_lin_none_kernel(tc, dyT, w, gate, offs, pos1, pos2, out):
         for i in range(HALVED):
             load_window(0, 1 + i)
             load_whole(i)
-        for f, (c, r) in enumerate(((0, PACK - 1), (1, 0))):
-            load_window(c, r)
-            nc.sync.dma_start(raw_halves[f][:], weight_half(HALVED, f))
+        load_window(0, PACK - 1)
+        nc.sync.dma_start(raw_halves[0][:], weight_half(HALVED, 0))
+        load_window(1, 0)
         load_window(1, 1)
-        load_whole(3)
+        nc.sync.dma_start(raw_halves[1][:], weight_half(HALVED, 1))
         load_window(1, 2)
+        load_whole(3)
         load_window(1, 3)
-        for r in range(PACK):
-            load_whole(4 + r)
+        load_whole(4)
+        load_window(2, 0)
+        for r in range(1, PACK):
             load_window(2, r)
+            load_whole(4 + r)
         load_pair_halves(0)
         nc.sync.dma_start(pos1_sb[:], pos1)
         nc.sync.dma_start(pos2_sb[:], pos2)
@@ -275,26 +286,29 @@ def tile_moe_bdx_lin_none_kernel(tc, dyT, w, gate, offs, pos1, pos2, out):
             weave_g(1, h, raw_place(4) + h * WIDE)
         gather_g(2, G0)
         weave_whole(5)
-        weave_late(0, (0, 1), nc.scalar.copy)
-        weave_late(0, (2,), nc.scalar.copy)
+        woven_six = place("woven_six", [P, 2, PACK * FRONT], BF16, take("fresh", WIDE))
+        weave_six()
         for h in range(2):
             weave_g(2, h, raw_place(5) + h * WIDE)
+        weave_seven(0, take("fresh", PIECE))
 
         quantise_early(0, 0, take("fresh", WIDE_SCALES))
         on_gate = [GATE + j * WIDE_SCALES for j in range(4 * S // WIDE_SCALES)]
         for q in range(1, PAIRS):
-            quantise_early(q, 0, on_gate[q])
+            quantise_early(q, 0, on_gate[q - 1])
         for c in range(2):
             for h in range(2):
-                quantise_g(c, h, on_gate[PAIRS + 2 * c + h])
-        quantise_late(0, 0, on_gate[-1])
+                quantise_g(c, h, on_gate[2 + 2 * c + h])
+        quantise_six(0, on_gate[-2])
+        quantise_early(0, 1, on_gate[-1])
         for q in range(1, PAIRS):
-            weave_late(q, (0,), nc.vector.tensor_copy, LAST_WINDOW + (q - 1) * PIECE, 4)
+            weave_late(q, (0,), nc.vector.tensor_copy, LAST_WINDOW + (q - 1) * PIECE)
         quantise_g(2, 0)
         quantise_late(1, 0)
         quantise_g(2, 1)
+        quantise_late(0, 0)
 
-        last_pieces = ((1, 2), (2, 2), (0, 3), (1, 3), (2, 3))
+        last_pieces = ((0, 2), (1, 2), (2, 2), (1, 3), (2, 3))
         last_places = [take("fresh", PIECE) for piece in last_pieces]
         quantise_late(2, 0, last_places[2] + PIECE // 2)
         multiply_front(0, 0)
@@ -305,14 +319,17 @@ def tile_moe_bdx_lin_none_kernel(tc, dyT, w, gate, offs, pos1, pos2, out):
         quantise_late(2, 1, last_places[1] - PIECE_SCALES // 2, last_places[4] - PIECE_CODES // 2)
         multiply_front(1, 1)
 
-        for q in range(PAIRS):
+        for q in range(1, PAIRS):
             quantise_early(q, 1, row1_places[-1] + q * WIDE_SCALES)
-        quantise_late(0, 2, row1_places[-1] + PAIRS * WIDE_SCALES)
+        quantise_six(1, row1_places[-1])
         empty((0, 1), LAST_FRONTS)
         multiply_back(2, 0)
         multiply_back(3, 0)
         for (q, kt), at in zip(last_pieces, last_places):
-            weave_late(q, (kt,), nc.scalar.copy, at)
+            if q:
+                weave_late(q, (kt,), nc.scalar.copy, at)
+            else:
+                weave_seven(1, at)
 
         gather_first(0)
         gather_first(1)

@@ -62,7 +62,7 @@ def tile_moe_bdx_lin_none_kernel(tc, dyT, w, gate, offs, pos1, pos2, out):
             return placed.tile(shape, dtype, name=name, offset=at, align_bytes=64)
 
         def raw_place(i):
-            return RAW + i * RAW_TILE
+            return RAW + (i if i < EARLY else {6: 11, 7: 6}[i]) * RAW_TILE
 
         offs_sb = held.tile([P, S // PER_COL], U16, name="offs_sb")
         pos1_sb = held.tile([P, T // PER_COL], U16, name="pos1_sb")
@@ -78,7 +78,7 @@ def tile_moe_bdx_lin_none_kernel(tc, dyT, w, gate, offs, pos1, pos2, out):
         raw = {i: place(f"raw{i}", [P, PACK, K], F32, raw_place(i)) for i in range(EARLY + 2) if i != HALVED}
         raw_halves = [place(f"raw_half{f}", [P, PACK, FRONT], F32, raw_place(HALVED) + f * WIDE) for f in range(2)]
         raw_pair_halves = {
-            (q, f): place(f"raw_pair{q}_{f}", [P, 2, PACK, FRONT], F32, LATE_RAW + (2 * q + f) * RAW_TILE)
+            (q, f): place(f"raw_pair{q}_{f}", [P, 2, PACK, FRONT], F32, LATE_RAW + (q + 2 - 2 * f) * RAW_TILE)
             for q in range(1, PAIRS)
             for f in range(2)
         }
@@ -227,9 +227,9 @@ def tile_moe_bdx_lin_none_kernel(tc, dyT, w, gate, offs, pos1, pos2, out):
             for u in range(2):
                 group(bank[:, u * C : (u + 1) * C], 2 * h + u, kt)
 
-        def empty(kts, at):
+        def empty(kts, at, step=WIDE):
             for kt in kts:
-                dx[kt] = place(f"dx{kt}", [P, S], F32, at + kt % 2 * WIDE)
+                dx[kt] = place(f"dx{kt}", [P, S], F32, at + kt % 2 * step)
                 for h in range(2):
                     col = h * HALF
                     for sums in acc[kt, h]:
@@ -264,9 +264,12 @@ def tile_moe_bdx_lin_none_kernel(tc, dyT, w, gate, offs, pos1, pos2, out):
         load_window(1, 3)
         load_whole(4)
         load_window(2, 0)
-        for r in range(1, PACK):
-            load_window(2, r)
-            load_whole(4 + r)
+        load_window(2, 1)
+        load_whole(5)
+        load_window(2, 2)
+        load_window(2, 3)
+        load_whole(6)
+        load_whole(7)
         load_pair_halves(0)
         nc.sync.dma_start(pos1_sb[:], pos1)
         nc.sync.dma_start(pos2_sb[:], pos2)
@@ -294,19 +297,19 @@ def tile_moe_bdx_lin_none_kernel(tc, dyT, w, gate, offs, pos1, pos2, out):
 
         quantise_early(0, 0, take("fresh", WIDE_SCALES))
         on_gate = [GATE + j * WIDE_SCALES for j in range(4 * S // WIDE_SCALES)]
-        for q in range(1, PAIRS):
-            quantise_early(q, 0, on_gate[q - 1])
+        quantise_early(1, 0, LAST_WINDOW - WINDOW_BYTES)
+        quantise_early(2, 0, on_gate[1])
         for c in range(2):
             for h in range(2):
                 quantise_g(c, h, on_gate[2 + 2 * c + h])
         quantise_six(0, on_gate[-2])
         quantise_early(0, 1, on_gate[-1])
-        for q in range(1, PAIRS):
-            weave_late(q, (0,), nc.vector.tensor_copy, LAST_WINDOW + (q - 1) * PIECE)
         quantise_g(2, 0)
-        quantise_late(1, 0)
         quantise_g(2, 1)
+        for q in range(1, PAIRS):
+            weave_late(q, (0,), nc.vector.tensor_copy, G0 + (q - 1) * PIECE)
         quantise_late(0, 0)
+        quantise_late(1, 0)
 
         last_pieces = ((0, 2), (1, 2), (2, 2), (1, 3), (2, 3))
         last_places = [take("fresh", PIECE) for piece in last_pieces]
@@ -314,15 +317,16 @@ def tile_moe_bdx_lin_none_kernel(tc, dyT, w, gate, offs, pos1, pos2, out):
         multiply_front(0, 0)
         multiply_front(1, 0)
         multiply_front(0, 1)
-        row1_places = [weave_late(q, (1,), nc.scalar.copy) for q in range(1, PAIRS)]
+        for q in range(1, PAIRS):
+            weave_late(q, (1,), nc.scalar.copy)
         quantise_late(1, 1)
         quantise_late(2, 1, last_places[1] - PIECE_SCALES // 2, last_places[4] - PIECE_CODES // 2)
         multiply_front(1, 1)
 
         for q in range(1, PAIRS):
-            quantise_early(q, 1, row1_places[-1] + q * WIDE_SCALES)
-        quantise_six(1, row1_places[-1])
-        empty((0, 1), LAST_FRONTS)
+            quantise_early(q, 1, LAST_FRONTS + PIECE + q * WIDE_SCALES)
+        quantise_six(1, LAST_FRONTS + PIECE)
+        empty((0, 1), LAST_FRONTS - PIECE, RAW_TILE)
         multiply_back(2, 0)
         multiply_back(3, 0)
         for (q, kt), at in zip(last_pieces, last_places):
@@ -338,8 +342,8 @@ def tile_moe_bdx_lin_none_kernel(tc, dyT, w, gate, offs, pos1, pos2, out):
             quantise_late(q, kt)
         multiply_back(2, 1)
         multiply_back(3, 1)
-        gather_second_and_store(1, last_places[-2])
-        empty((2, 3), RAW)
+        gather_second_and_store(1, LATE_RAW + RAW_TILE)
+        empty((2, 3), raw_place(3))
         gather_first(2)
         gather_first(3)
         gather_second_and_store(2, G1 + PIECE)

@@ -198,10 +198,10 @@ def tile_moe_bdx_lin_none_kernel(tc, dyT, w, gate, offs, pos1, pos2, out):
             woven, kts = late_woven[q, kt]
             hand_out(quantise(f"late{q}_{kt}", woven, scales_at, codes_at), (EARLY + 2 * q, EARLY + 2 * q + 1) if q else (EARLY + 1,), kts)
 
-        def group(into, e, kt):
+        def group(into, e, kt, passes=(0, 1, 2)):
             h, u = divmod(e, 2)
             slots = slice(u * C, (u + 1) * C)
-            for c in range(NPASS):
+            for c in passes:
                 w_codes, w_scales = w_mx[e * NPASS + c, kt]
                 g_codes, g_scales = g_mx[c, h]
                 nc.tensor.matmul_mx(
@@ -210,8 +210,8 @@ def tile_moe_bdx_lin_none_kernel(tc, dyT, w, gate, offs, pos1, pos2, out):
                     lhsT_scale=w_scales,
                     rhs=g_codes[:, slots].bitcast(FP8X4),
                     rhs_scale=g_scales[:, slots],
-                    start=(c == 0),
-                    stop=(c == NPASS - 1),
+                    start=(c == passes[0]),
+                    stop=(c == passes[-1]),
                 )
 
         def multiply_front(kt, h):
@@ -222,10 +222,17 @@ def tile_moe_bdx_lin_none_kernel(tc, dyT, w, gate, offs, pos1, pos2, out):
                 group(bank[:, 0:C], 2 * h + u, kt)
 
         def multiply_back(kt, h):
-            bank = psum.tile([P, HALF], F32, name=f"bank{kt - 2}_{h}_0")
-            acc[kt, h] = [bank[:]]
-            for u in range(2):
-                group(bank[:, u * C : (u + 1) * C], 2 * h + u, kt)
+            if h == 0:
+                bank = psum.tile([P, HALF], F32, name=f"bank{kt - 2}_0_0")
+                acc[kt, h] = [bank[:]]
+                for u in range(2):
+                    group(bank[:, u * C : (u + 1) * C], u, kt)
+            else:
+                acc[kt, h] = []
+                for u in range(2):
+                    bank = psum.tile([P, HALF], F32, name=f"bank{kt - 2}_1_{u}")
+                    acc[kt, h].append(bank[:, 0:C])
+                    group(bank[:, 0:C], 2 + u, kt, (0, 2, 1) if (kt, u) == (2, 0) else (0, 1, 2))
 
         def empty(kts, at, step=WIDE):
             for kt in kts:
@@ -311,16 +318,16 @@ def tile_moe_bdx_lin_none_kernel(tc, dyT, w, gate, offs, pos1, pos2, out):
         quantise_late(0, 0)
         quantise_late(1, 0)
 
-        last_pieces = ((0, 2), (1, 2), (2, 2), (1, 3), (2, 3))
+        last_pieces = ((1, 2), (2, 2), (0, 2), (1, 3), (2, 3))
         last_places = [take("fresh", PIECE) for piece in last_pieces]
-        quantise_late(2, 0, last_places[2] + PIECE // 2)
+        quantise_late(2, 0)
         multiply_front(0, 0)
         multiply_front(1, 0)
         multiply_front(0, 1)
         for q in range(1, PAIRS):
             weave_late(q, (1,), nc.scalar.copy)
         quantise_late(1, 1)
-        quantise_late(2, 1, last_places[1] - PIECE_SCALES // 2, last_places[4] - PIECE_CODES // 2)
+        quantise_late(2, 1, last_places[1] - PIECE_SCALES // 2, last_places[3] - PIECE_CODES // 2)
         multiply_front(1, 1)
 
         for q in range(1, PAIRS):
@@ -329,22 +336,30 @@ def tile_moe_bdx_lin_none_kernel(tc, dyT, w, gate, offs, pos1, pos2, out):
         empty((0, 1), LAST_FRONTS - PIECE, RAW_TILE)
         multiply_back(2, 0)
         multiply_back(3, 0)
-        for (q, kt), at in zip(last_pieces, last_places):
-            if q:
-                weave_late(q, (kt,), nc.scalar.copy, at)
-            else:
-                weave_seven(1, at)
+        weave_late(1, (2,), nc.scalar.copy, last_places[0])
+        weave_late(2, (2,), nc.scalar.copy, last_places[1])
+        weave_seven(1, last_places[2])
+        weave_late(1, (3,), nc.scalar.copy, last_places[3])
 
         gather_first(0)
         gather_first(1)
         gather_second_and_store(0, G1)
-        for q, kt in last_pieces:
-            quantise_late(q, kt)
+        quantise_late(1, 2)
+        quantise_late(2, 2)
+        quantise_late(0, 2, last_places[4] + PIECE // 2 - PIECE_SCALES // 2)
         multiply_back(2, 1)
-        multiply_back(3, 1)
-        gather_second_and_store(1, LATE_RAW + RAW_TILE)
-        empty((2, 3), raw_place(3))
+        gather_second_and_store(1, raw_place(EARLY + 1))
+        quantise_late(1, 3)
+        empty((2,), raw_place(3))
+        ends = []
+        for u in range(2):
+            ends.append(place(f"woven_end{u}", [P, PACK * P], BF16, last_places[4] + u * PIECE // 2)[:])
+            weave(ends[u], raw_pair_halves[2, 1][:, u, :, P:FRONT])
         gather_first(2)
+        for u in range(2):
+            hand_out(quantise(f"end{u}", ends[u], None), (EARLY + 4 + u,), (3,))
+        multiply_back(3, 1)
+        gather_second_and_store(2, LATE_RAW + 2 * RAW_TILE)
+        empty((3,), raw_place(3))
         gather_first(3)
-        gather_second_and_store(2, G1 + PIECE)
         gather_second_and_store(3, G1 + 2 * PIECE, (0, LAST_CUT, T))

@@ -14,6 +14,8 @@ PER_COL = 16
 WINDOW = S + 8
 EARLY = 2 * NPASS
 PAIRS = NPASS
+SIX, SEVEN, TEN, ELEVEN = 6, 7, 10, 11
+LATE_PAIRS = (1, 2)
 HALVED = 2
 FIRST_CUT = C
 LAST_CUT = T - P
@@ -28,12 +30,16 @@ WINDOW_BYTES = 65 * 64
 ALL_CODES = 36 * KIB
 
 WINDOWS = 0
-LAST_WINDOW = WINDOWS + (NPASS * PACK - 1) * WINDOW_BYTES
-GATE = LAST_WINDOW + WINDOW_BYTES
+GATE = WINDOWS + NPASS * PACK * WINDOW_BYTES
+LAST_WINDOW_BUT_ONE = GATE - 2 * WINDOW_BYTES
 RAW = GATE + 4 * S
-LATE_RAW = RAW + EARLY * RAW_TILE
-LAST_FRONTS = LATE_RAW + 4 * RAW_TILE
-G0 = LATE_RAW + PAIRS * 2 * RAW_TILE
+RAW_SEVEN = RAW + EARLY * RAW_TILE
+BACKS_1 = RAW_SEVEN + RAW_TILE
+BACK_TEN = BACKS_1 + RAW_TILE
+FRONTS_1 = BACK_TEN + RAW_TILE
+FRONTS_2 = FRONTS_1 + RAW_TILE
+RAW_SIX = FRONTS_2 + RAW_TILE
+G0 = RAW_SIX + RAW_TILE
 G1 = G0 + 2 * RAW_TILE
 EARLY_WOVEN = G1 + 2 * RAW_TILE
 FRESH = EARLY_WOVEN + PAIRS * RAW_TILE
@@ -62,7 +68,10 @@ def tile_moe_bdx_lin_none_kernel(tc, dyT, w, gate, offs, pos1, pos2, out):
             return placed.tile(shape, dtype, name=name, offset=at, align_bytes=64)
 
         def raw_place(i):
-            return RAW + (i if i < EARLY else {6: 11, 7: 6}[i]) * RAW_TILE
+            return {SIX: RAW_SIX, SEVEN: RAW_SEVEN}.get(i, RAW + i * RAW_TILE)
+
+        def quarter_place(kt):
+            return BACK_TEN + kt * PIECE
 
         offs_sb = held.tile([P, S // PER_COL], U16, name="offs_sb")
         pos1_sb = held.tile([P, T // PER_COL], U16, name="pos1_sb")
@@ -75,13 +84,14 @@ def tile_moe_bdx_lin_none_kernel(tc, dyT, w, gate, offs, pos1, pos2, out):
                 windows[c, r] = place(f"window{c}_{r}", [P, WINDOW], F32, WINDOWS + (c * PACK + r) * WINDOW_BYTES)
                 nc.gpsimd.memset(windows[c, r][:, T:], 0.0)
 
-        raw = {i: place(f"raw{i}", [P, PACK, K], F32, raw_place(i)) for i in range(EARLY + 2) if i != HALVED}
+        raw = {i: place(f"raw{i}", [P, PACK, K], F32, raw_place(i)) for i in range(SEVEN + 1) if i != HALVED}
         raw_halves = [place(f"raw_half{f}", [P, PACK, FRONT], F32, raw_place(HALVED) + f * WIDE) for f in range(2)]
-        raw_pair_halves = {
-            (q, f): place(f"raw_pair{q}_{f}", [P, 2, PACK, FRONT], F32, LATE_RAW + (q + 2 - 2 * f) * RAW_TILE)
-            for q in range(1, PAIRS)
-            for f in range(2)
+        raw_pair = {
+            key: place(f"raw_pair{key[0]}_{key[1]}", [P, 2, PACK, FRONT], F32, at)
+            for key, at in (((1, 0), FRONTS_1), ((1, 1), BACKS_1), ((2, 0), FRONTS_2))
         }
+        raw_back_ten = place("raw_back_ten", [P, PACK, FRONT], F32, BACK_TEN)
+        raw_quarter = {kt: place(f"raw_quarter{kt}", [P, PACK, P], F32, quarter_place(kt)) for kt in (2, 3)}
         early_woven = [place(f"early_woven{q}", [P, 2, 2, PACK * FRONT], BF16, EARLY_WOVEN + q * RAW_TILE) for q in range(PAIRS)]
 
         def load_window(c, r):
@@ -98,13 +108,15 @@ def tile_moe_bdx_lin_none_kernel(tc, dyT, w, gate, offs, pos1, pos2, out):
         def load_whole(i):
             nc.sync.dma_start(raw[i][:], weight_rows(i))
 
-        def load_pair_halves(f):
-            for q in range(1, PAIRS):
-                for u in range(2):
-                    nc.sync.dma_start(raw_pair_halves[q, f][:, u, :, :], weight_half(EARLY + 2 * q + u, f))
+        def late_pair(q):
+            return (SIX + 2 * q, SEVEN + 2 * q)
+
+        def load_pair(q, f):
+            for u, i in enumerate(late_pair(q)):
+                nc.sync.dma_start(raw_pair[q, f][:, u, :, :], weight_half(i, f))
 
         g_raw, g_woven, g_mx = {}, {}, {}
-        late_woven = {}
+        pieces = {}
         w_mx = {}
         acc, dx, first = {}, {}, {}
         next_free = {"codes": WINDOWS, "scales": WINDOWS + ALL_CODES, "fresh": FRESH}
@@ -148,26 +160,15 @@ def tile_moe_bdx_lin_none_kernel(tc, dyT, w, gate, offs, pos1, pos2, out):
         def quantise_g(c, h, scales_at=None):
             g_mx[c, h] = quantise(f"g{c}_{h}", g_woven[c, h], scales_at)
 
-        def weave_whole(i):
-            q, u = divmod(i, 2)
+        def weave_whole(i, dst):
             nc.scalar.copy(
-                early_woven[q][:, :, u, :].rearrange("p f (x i r) -> p f x r i", i=2, r=PACK),
+                dst.rearrange("p f (x i r) -> p f x r i", i=2, r=PACK),
                 raw[i][:].rearrange("p r (f x i) -> p f x r i", f=2, i=2),
             )
 
-        def weave_six():
-            nc.scalar.copy(
-                woven_six[:].rearrange("p f (x i r) -> p f x r i", i=2, r=PACK),
-                raw[EARLY][:].rearrange("p r (f x i) -> p f x r i", f=2, i=2),
-            )
-
-        def quantise_six(f, scales_at):
-            hand_out(quantise(f"six{f}", woven_six[:, f, :], scales_at), (EARLY,), (2 * f, 2 * f + 1))
-
-        def weave_seven(f, at):
-            woven = place(f"woven_seven{f}", [P, PACK * FRONT], BF16, at)[:]
-            late_woven[0, 2 * f] = woven, (2 * f, 2 * f + 1)
-            weave(woven, raw[EARLY + 1][:, :, f * FRONT : (f + 1) * FRONT])
+        def weave_early(i):
+            q, u = divmod(i, 2)
+            weave_whole(i, early_woven[q][:, :, u, :])
 
         def weave_half(f):
             q, u = divmod(HALVED, 2)
@@ -181,27 +182,37 @@ def tile_moe_bdx_lin_none_kernel(tc, dyT, w, gate, offs, pos1, pos2, out):
             woven = early_woven[q][:, f, :, :].rearrange("p u x -> p (u x)")
             hand_out(quantise(f"early{q}_{f}", woven, scales_at), (2 * q, 2 * q + 1), (2 * f, 2 * f + 1))
 
-        def weave_late(q, kts, copy, at=None):
-            width = len(kts) * P
-            if at is None:
-                at = take("fresh", len(kts) * PIECE)
-            woven = place(f"late_woven{q}_{kts[0]}", [P, 2 * PACK * width], BF16, at)[:]
-            late_woven[q, kts[0]] = woven, kts
-            source, col = raw_pair_halves[q, kts[0] // 2], kts[0] % 2 * P
+        def quantise_six(f, scales_at):
+            hand_out(quantise(f"six{f}", woven_six[:, f, :], scales_at), (SIX,), (2 * f, 2 * f + 1))
+
+        def new_piece(name, tiles, kts, at):
+            woven = place(f"woven_{name}", [P, len(tiles) * len(kts) * PACK * P], BF16, at)[:]
+            pieces[name] = woven, tiles, kts
+            return woven
+
+        def weave_seven(f, at):
+            woven = new_piece(f"seven{f}", (SEVEN,), (2 * f, 2 * f + 1), at)
+            weave(woven, raw[SEVEN][:, :, f * FRONT : (f + 1) * FRONT])
+
+        def weave_pair(q, kt, copy, at):
+            woven = new_piece(f"pair{q}_{kt}", late_pair(q), (kt,), at)
+            col = kt % 2 * P
             copy(
                 woven.rearrange("p (u x i r) -> p u x r i", u=2, i=2, r=PACK),
-                source[:, :, :, col : col + width].rearrange("p u r (x i) -> p u x r i", i=2),
+                raw_pair[q, kt // 2][:, :, :, col : col + P].rearrange("p u r (x i) -> p u x r i", i=2),
             )
-            return at
 
-        def quantise_late(q, kt, scales_at=None, codes_at=None):
-            woven, kts = late_woven[q, kt]
-            hand_out(quantise(f"late{q}_{kt}", woven, scales_at, codes_at), (EARLY + 2 * q, EARLY + 2 * q + 1) if q else (EARLY + 1,), kts)
+        def last_backs(kt):
+            return raw_back_ten[:, :, (kt - 2) * P : (kt - 1) * P], raw_quarter[kt][:]
 
-        def group(into, e, kt, passes=(0, 1, 2)):
+        def quantise_piece(name, scales_at=None, codes_at=None):
+            woven, tiles, kts = pieces[name]
+            hand_out(quantise(name, woven, scales_at, codes_at), tiles, kts)
+
+        def group(into, e, kt):
             h, u = divmod(e, 2)
             slots = slice(u * C, (u + 1) * C)
-            for c in passes:
+            for c in range(NPASS):
                 w_codes, w_scales = w_mx[e * NPASS + c, kt]
                 g_codes, g_scales = g_mx[c, h]
                 nc.tensor.matmul_mx(
@@ -210,38 +221,29 @@ def tile_moe_bdx_lin_none_kernel(tc, dyT, w, gate, offs, pos1, pos2, out):
                     lhsT_scale=w_scales,
                     rhs=g_codes[:, slots].bitcast(FP8X4),
                     rhs_scale=g_scales[:, slots],
-                    start=(c == passes[0]),
-                    stop=(c == passes[-1]),
+                    start=(c == 0),
+                    stop=(c == NPASS - 1),
                 )
 
-        def multiply_front(kt, h):
+        def multiply_apart(kt, h):
             acc[kt, h] = []
             for u in range(2):
-                bank = psum.tile([P, HALF], F32, name=f"bank{kt}_{h}_{u}")
+                bank = psum.tile([P, HALF], F32, name=f"bank{kt % 2}_{h}_{u}")
                 acc[kt, h].append(bank[:, 0:C])
                 group(bank[:, 0:C], 2 * h + u, kt)
 
-        def multiply_back(kt, h):
-            if h == 0:
-                bank = psum.tile([P, HALF], F32, name=f"bank{kt - 2}_0_0")
-                acc[kt, h] = [bank[:]]
-                for u in range(2):
-                    group(bank[:, u * C : (u + 1) * C], u, kt)
-            else:
-                acc[kt, h] = []
-                for u in range(2):
-                    bank = psum.tile([P, HALF], F32, name=f"bank{kt - 2}_1_{u}")
-                    acc[kt, h].append(bank[:, 0:C])
-                    group(bank[:, 0:C], 2 + u, kt, (0, 2, 1) if (kt, u) == (2, 0) else (0, 1, 2))
+        def multiply_together(kt):
+            bank = psum.tile([P, HALF], F32, name=f"bank{kt % 2}_0_0")
+            acc[kt, 0] = [bank[:]]
+            for u in range(2):
+                group(bank[:, u * C : (u + 1) * C], u, kt)
 
-        def empty(kts, at, step=WIDE):
-            for kt in kts:
-                dx[kt] = place(f"dx{kt}", [P, S], F32, at + kt % 2 * step)
-                for h in range(2):
-                    col = h * HALF
-                    for sums in acc[kt, h]:
-                        nc.scalar.copy(dx[kt][:, col : col + sums.shape[1]], sums)
-                        col = col + sums.shape[1]
+        def empty(kt, at):
+            dx[kt] = place(f"dx{kt}", [P, S], F32, at)
+            col = 0
+            for sums in acc[kt, 0] + acc[kt, 1]:
+                nc.scalar.copy(dx[kt][:, col : col + sums.shape[1]], sums)
+                col = col + sums.shape[1]
 
         def gather_first(kt):
             first[kt] = place(f"first{kt}", [P, T], F32, G1 + RAW_TILE + kt * PIECE)
@@ -269,97 +271,99 @@ def tile_moe_bdx_lin_none_kernel(tc, dyT, w, gate, offs, pos1, pos2, out):
         load_window(1, 2)
         load_whole(3)
         load_window(1, 3)
-        load_whole(4)
-        load_window(2, 0)
-        load_window(2, 1)
-        load_whole(5)
-        load_window(2, 2)
-        load_window(2, 3)
-        load_whole(6)
-        load_whole(7)
-        load_pair_halves(0)
+        for j in range(2):
+            load_whole(4 + j)
+            load_window(2, 2 * j)
+            load_window(2, 2 * j + 1)
+        load_whole(SIX)
+        load_whole(SEVEN)
+        for q in LATE_PAIRS:
+            load_pair(q, 0)
         nc.sync.dma_start(pos1_sb[:], pos1)
         nc.sync.dma_start(pos2_sb[:], pos2)
-        load_pair_halves(1)
+        load_pair(1, 1)
+        nc.sync.dma_start(raw_back_ten[:], weight_half(TEN, 1))
+        for kt in (2, 3):
+            nc.sync.dma_start(raw_quarter[kt][:], weight_rows(ELEVEN)[:, :, kt * P : (kt + 1) * P])
 
         gather_g(0, G0, (0, FIRST_CUT, S))
-        weave_whole(0)
-        weave_whole(1)
+        weave_early(0)
+        weave_early(1)
         weave_half(0)
         weave_g(0, 0, raw_place(HALVED))
         weave_g(0, 1, raw_place(1))
         gather_g(1, G1)
         weave_half(1)
-        weave_whole(3)
-        weave_whole(4)
+        weave_early(3)
+        weave_early(4)
         for h in range(2):
             weave_g(1, h, raw_place(4) + h * WIDE)
         gather_g(2, G0)
-        weave_whole(5)
+        weave_early(5)
         woven_six = place("woven_six", [P, 2, PACK * FRONT], BF16, take("fresh", WIDE))
-        weave_six()
+        weave_whole(SIX, woven_six[:])
         for h in range(2):
             weave_g(2, h, raw_place(5) + h * WIDE)
         weave_seven(0, take("fresh", PIECE))
 
         quantise_early(0, 0, take("fresh", WIDE_SCALES))
-        on_gate = [GATE + j * WIDE_SCALES for j in range(4 * S // WIDE_SCALES)]
-        quantise_early(1, 0, LAST_WINDOW - WINDOW_BYTES)
-        quantise_early(2, 0, on_gate[1])
+        on_gate = [GATE + j * WIDE_SCALES for j in range(1, 4 * S // WIDE_SCALES)]
+        quantise_early(1, 0, LAST_WINDOW_BUT_ONE)
+        quantise_early(2, 0, on_gate[0])
         for c in range(2):
             for h in range(2):
-                quantise_g(c, h, on_gate[2 + 2 * c + h])
+                quantise_g(c, h, on_gate[1 + 2 * c + h])
         quantise_six(0, on_gate[-2])
         quantise_early(0, 1, on_gate[-1])
+
         quantise_g(2, 0)
         quantise_g(2, 1)
-        for q in range(1, PAIRS):
-            weave_late(q, (0,), nc.vector.tensor_copy, G0 + (q - 1) * PIECE)
-        quantise_late(0, 0)
-        quantise_late(1, 0)
-
-        last_pieces = ((1, 2), (2, 2), (0, 2), (1, 3), (2, 3))
-        last_places = [take("fresh", PIECE) for piece in last_pieces]
-        quantise_late(2, 0)
-        multiply_front(0, 0)
-        multiply_front(1, 0)
-        multiply_front(0, 1)
-        for q in range(1, PAIRS):
-            weave_late(q, (1,), nc.scalar.copy)
-        quantise_late(1, 1)
-        quantise_late(2, 1, last_places[1] - PIECE_SCALES // 2, last_places[3] - PIECE_CODES // 2)
-        multiply_front(1, 1)
+        for q in LATE_PAIRS:
+            weave_pair(q, 0, nc.vector.tensor_copy, G0 + (q - 1) * PIECE)
+        quantise_piece("seven0")
+        quantise_piece("pair1_0")
+        tail = [take("fresh", PIECE) for j in range(5)]
+        quantise_piece("pair2_0")
+        multiply_apart(0, 0)
+        multiply_apart(1, 0)
+        multiply_apart(0, 1)
+        for q in LATE_PAIRS:
+            weave_pair(q, 1, nc.scalar.copy, take("fresh", PIECE))
+        quantise_piece("pair1_1")
+        quantise_piece("pair2_1", tail[1] - PIECE_SCALES // 2, tail[3] - PIECE_CODES // 2)
+        multiply_apart(1, 1)
 
         for q in range(1, PAIRS):
-            quantise_early(q, 1, LAST_FRONTS + PIECE + q * WIDE_SCALES)
-        quantise_six(1, LAST_FRONTS + PIECE)
-        empty((0, 1), LAST_FRONTS - PIECE, RAW_TILE)
-        multiply_back(2, 0)
-        multiply_back(3, 0)
-        weave_late(1, (2,), nc.scalar.copy, last_places[0])
-        weave_late(2, (2,), nc.scalar.copy, last_places[1])
-        weave_seven(1, last_places[2])
-        weave_late(1, (3,), nc.scalar.copy, last_places[3])
+            quantise_early(q, 1, FRONTS_2 + PIECE + q * WIDE_SCALES)
+        quantise_six(1, FRONTS_2 + PIECE)
+        for kt in range(2):
+            empty(kt, FRONTS_2 - PIECE + kt * RAW_TILE)
+        multiply_together(2)
+        multiply_together(3)
+        weave_seven(1, tail[0])
+        weave_pair(1, 2, nc.scalar.copy, tail[1])
+        woven = new_piece("pair2_2", late_pair(2), (2,), tail[2])
+        for u, source in enumerate(last_backs(2)):
+            weave(woven[:, u * PACK * P : (u + 1) * PACK * P], source)
+        weave_pair(1, 3, nc.scalar.copy, tail[3])
 
         gather_first(0)
         gather_first(1)
         gather_second_and_store(0, G1)
-        quantise_late(1, 2)
-        quantise_late(2, 2)
-        quantise_late(0, 2, last_places[4] + PIECE // 2 - PIECE_SCALES // 2)
-        multiply_back(2, 1)
-        gather_second_and_store(1, raw_place(EARLY + 1))
-        quantise_late(1, 3)
-        empty((2,), raw_place(3))
-        ends = []
-        for u in range(2):
-            ends.append(place(f"woven_end{u}", [P, PACK * P], BF16, last_places[4] + u * PIECE // 2)[:])
-            weave(ends[u], raw_pair_halves[2, 1][:, u, :, P:FRONT])
+        quantise_piece("seven1")
+        quantise_piece("pair1_2")
+        quantise_piece("pair2_2", tail[4] + PIECE // 2 - PIECE_SCALES // 2)
+        multiply_apart(2, 1)
+        gather_second_and_store(1, quarter_place(2))
+        quantise_piece("pair1_3")
+        empty(2, raw_place(3))
+        for u, source in enumerate(last_backs(3)):
+            weave(new_piece(f"end{u}", late_pair(2)[u : u + 1], (3,), tail[4] + u * PIECE // 2), source)
         gather_first(2)
         for u in range(2):
-            hand_out(quantise(f"end{u}", ends[u], None), (EARLY + 4 + u,), (3,))
-        multiply_back(3, 1)
-        gather_second_and_store(2, LATE_RAW + 2 * RAW_TILE)
-        empty((3,), raw_place(3))
+            quantise_piece(f"end{u}")
+        multiply_apart(3, 1)
+        gather_second_and_store(2, quarter_place(3))
+        empty(3, raw_place(3) + WIDE)
         gather_first(3)
         gather_second_and_store(3, G1 + 2 * PIECE, (0, LAST_CUT, T))

@@ -11,38 +11,22 @@ NPASS = N // PASS
 HALF = S // 2
 FRONT = K // 2
 PER_COL = 16
-WINDOW = S + 8
-EARLY = 2 * NPASS
-PAIRS = NPASS
-SIX, SEVEN, TEN, ELEVEN = 6, 7, 10, 11
-LATE_PAIRS = (1, 2)
-HALVED = 2
-FIRST_CUT = C
-LAST_CUT = T - P
+TAIL = 8
 
 KIB = 1024
 RAW_TILE = 8 * KIB
 WIDE = 4 * KIB
 PIECE = 2 * KIB
-WIDE_SCALES = 512
-PIECE_CODES, PIECE_SCALES = KIB, 256
 WINDOW_BYTES = 65 * 64
-ALL_CODES = 36 * KIB
+UNIT = PIECE + 512
 
 WINDOWS = 0
 GATE = WINDOWS + NPASS * PACK * WINDOW_BYTES
-LAST_WINDOW_BUT_ONE = GATE - 2 * WINDOW_BYTES
 RAW = GATE + 4 * S
-RAW_SEVEN = RAW + EARLY * RAW_TILE
-BACKS_1 = RAW_SEVEN + RAW_TILE
-BACK_TEN = BACKS_1 + RAW_TILE
-FRONTS_1 = BACK_TEN + RAW_TILE
-FRONTS_2 = FRONTS_1 + RAW_TILE
-RAW_SIX = FRONTS_2 + RAW_TILE
-G0 = RAW_SIX + RAW_TILE
-G1 = G0 + 2 * RAW_TILE
-EARLY_WOVEN = G1 + 2 * RAW_TILE
-FRESH = EARLY_WOVEN + PAIRS * RAW_TILE
+PICKED = RAW + 12 * RAW_TILE
+RING = PICKED + 4 * RAW_TILE
+LATE = RING + 3 * WIDE
+CODES = LATE + 4 * WIDE
 
 F32 = mybir.dt.float32
 BF16 = mybir.dt.bfloat16
@@ -52,6 +36,7 @@ U8 = mybir.dt.uint8
 FP8X4 = mybir.dt.float8_e4m3fn_x4
 ADD = mybir.AluOpType.add
 MULT = mybir.AluOpType.mult
+COPY = mybir.ActivationFunctionType.Copy
 
 FLOPS = 2 * K * N * S
 BYTES = 4 * (N * T + E * N * K + S + K * T) + 2 * P * (S + 2 * T) // PER_COL
@@ -68,31 +53,27 @@ def tile_moe_bdx_lin_none_kernel(tc, dyT, w, gate, offs, pos1, pos2, out):
             return placed.tile(shape, dtype, name=name, offset=at, align_bytes=64)
 
         def raw_place(i):
-            return {SIX: RAW_SIX, SEVEN: RAW_SEVEN}.get(i, RAW + i * RAW_TILE)
+            return RAW + i * RAW_TILE
 
-        def quarter_place(kt):
-            return BACK_TEN + kt * PIECE
+        def half_place(i, f):
+            return raw_place(10) + (2 * f + i - 10) * WIDE
 
         offs_sb = held.tile([P, S // PER_COL], U16, name="offs_sb")
         pos1_sb = held.tile([P, T // PER_COL], U16, name="pos1_sb")
         pos2_sb = held.tile([P, T // PER_COL], U16, name="pos2_sb")
-        gate_sb = place("gate_sb", [P, S], F32, GATE)
+        gate_sb = [place(f"gate{h}", [P, HALF], F32, GATE + h * PIECE) for h in range(2)]
 
         windows = {}
         for c in range(NPASS):
             for r in range(PACK):
-                windows[c, r] = place(f"window{c}_{r}", [P, WINDOW], F32, WINDOWS + (c * PACK + r) * WINDOW_BYTES)
+                width = (HALF if c == 0 else S) + TAIL
+                windows[c, r] = place(f"window{c}_{r}", [P, width], F32, WINDOWS + (c * PACK + r) * WINDOW_BYTES)
                 nc.gpsimd.memset(windows[c, r][:, T:], 0.0)
 
-        raw = {i: place(f"raw{i}", [P, PACK, K], F32, raw_place(i)) for i in range(SEVEN + 1) if i != HALVED}
-        raw_halves = [place(f"raw_half{f}", [P, PACK, FRONT], F32, raw_place(HALVED) + f * WIDE) for f in range(2)]
-        raw_pair = {
-            key: place(f"raw_pair{key[0]}_{key[1]}", [P, 2, PACK, FRONT], F32, at)
-            for key, at in (((1, 0), FRONTS_1), ((1, 1), BACKS_1), ((2, 0), FRONTS_2))
-        }
-        raw_back_ten = place("raw_back_ten", [P, PACK, FRONT], F32, BACK_TEN)
-        raw_quarter = {kt: place(f"raw_quarter{kt}", [P, PACK, P], F32, quarter_place(kt)) for kt in (2, 3)}
-        early_woven = [place(f"early_woven{q}", [P, 2, 2, PACK * FRONT], BF16, EARLY_WOVEN + q * RAW_TILE) for q in range(PAIRS)]
+        raw = {i: place(f"raw{i}", [P, PACK, K], F32, raw_place(i)) for i in range(10)}
+        raw_half = {(i, f): place(f"raw{i}_{f}", [P, PACK, FRONT], F32, half_place(i, f)) for f in range(2) for i in (10, 11)}
+        picked = {}
+        banks = {(kt, h): psum.tile([P, HALF], F32, name=f"bank{kt}_{h}") for kt in range(4) for h in range(2)}
 
         def load_window(c, r):
             rows = dyT[c * PASS : (c + 1) * PASS, :].rearrange("(p r) t -> p r t", r=PACK)
@@ -102,268 +83,201 @@ def tile_moe_bdx_lin_none_kernel(tc, dyT, w, gate, offs, pos1, pos2, out):
             e, c = divmod(i, NPASS)
             return w[e, c * PASS : (c + 1) * PASS, :].rearrange("(p r) k -> p r k", r=PACK)
 
-        def weight_half(i, f):
-            return weight_rows(i)[:, :, f * FRONT : (f + 1) * FRONT]
-
         def load_whole(i):
             nc.sync.dma_start(raw[i][:], weight_rows(i))
 
-        def late_pair(q):
-            return (SIX + 2 * q, SEVEN + 2 * q)
+        def load_half(i, f):
+            nc.sync.dma_start(raw_half[i, f][:], weight_rows(i)[:, :, f * FRONT : (f + 1) * FRONT])
 
-        def load_pair(q, f):
-            for u, i in enumerate(late_pair(q)):
-                nc.sync.dma_start(raw_pair[q, f][:, u, :, :], weight_half(i, f))
+        def load_gate(h):
+            nc.sync.dma_start(gate_sb[h][:], gate[0:P, h * HALF : (h + 1) * HALF])
 
-        g_raw, g_woven, g_mx = {}, {}, {}
-        pieces = {}
-        w_mx = {}
-        acc, dx, first = {}, {}, {}
-        next_free = {"codes": WINDOWS, "scales": WINDOWS + ALL_CODES, "fresh": FRESH}
-        taken = {kind: [] for kind in next_free}
+        woven, mx = {}, {}
+        count = {"fresh": 0, "windows": 0}
 
-        def take(kind, size):
-            taken[kind].append(size)
-            return next_free[kind] + sum(taken[kind]) - size
+        def entries(lst, lo, hi):
+            return lst[:, lo // PER_COL : hi // PER_COL]
 
-        def gather_g(c, at, cuts_of_first=(0, S)):
-            g = place(f"g{c}", [P, PACK, S], F32, at)
-            for h in range(2):
-                g_raw[c, h] = g[:, :, h * HALF : (h + 1) * HALF]
-            for r in range(PACK):
-                cuts = cuts_of_first if r == 0 else (0, S)
-                for lo, hi in zip(cuts, cuts[1:]):
-                    picked = windows[c, r][:].indirect(offs_sb[:, lo // PER_COL : hi // PER_COL])
-                    nc.vector.tensor_tensor(g[:, r, lo:hi], picked, gate_sb[:, lo:hi], MULT)
-
-        def weave(dst, src):
-            nc.scalar.copy(
-                dst.rearrange("p (x i r) -> p x r i", i=2, r=PACK),
+        def weave(copy, name, src, at):
+            woven[name] = place(f"woven_{name}", [P, PACK * src.shape[2]], BF16, at)[:]
+            copy(
+                woven[name].rearrange("p (x i r) -> p x r i", i=2, r=PACK),
                 src.rearrange("p r (x i) -> p x r i", i=2),
             )
 
-        def quantise(name, woven, scales_at, codes_at=None):
-            words = woven.shape[1] // PACK
-            if codes_at is None:
-                codes_at = take("codes", 4 * words)
-            codes = place(f"codes_{name}", [P, words], U32, codes_at)
-            if scales_at is None:
-                scales_at = take("scales", words)
-            scales = place(f"scales_{name}", [P, words], U8, scales_at)
-            nc.vector.quantize_mx(out=codes[:].bitcast(FP8X4), scales=scales[:], in_=woven)
-            return codes, scales
-
-        def weave_g(c, h, at):
-            g_woven[c, h] = place(f"g_woven{c}_{h}", [P, PACK * HALF], BF16, at)[:]
-            weave(g_woven[c, h], g_raw[c, h])
-
-        def quantise_g(c, h, scales_at=None):
-            g_mx[c, h] = quantise(f"g{c}_{h}", g_woven[c, h], scales_at)
-
-        def weave_whole(i, dst):
-            nc.scalar.copy(
-                dst.rearrange("p f (x i r) -> p f x r i", i=2, r=PACK),
-                raw[i][:].rearrange("p r (f x i) -> p f x r i", f=2, i=2),
+        def weave_gated(c, h, src, at):
+            name = f"g{c}_{h}"
+            woven[name] = place(f"woven_{name}", [P, PACK * HALF], BF16, at)[:]
+            weights = gate_sb[h][:].rearrange("p (x i) -> p x i", i=2).unsqueeze(2).to_broadcast([P, HALF // 2, PACK, 2])
+            nc.vector.tensor_tensor(
+                woven[name].rearrange("p (x i r) -> p x r i", i=2, r=PACK),
+                src.rearrange("p r (x i) -> p x r i", i=2),
+                weights,
+                MULT,
             )
 
-        def weave_early(i):
-            q, u = divmod(i, 2)
-            weave_whole(i, early_woven[q][:, :, u, :])
+        def quantise(name, kind="windows", at=None):
+            words = woven[name].shape[1] // PACK
+            if at is None:
+                at = {"fresh": CODES, "windows": WINDOWS}[kind] + count[kind] * UNIT
+                count[kind] = count[kind] + 1
+            codes = place(f"codes_{name}", [P, words], U32, at)
+            scales = place(f"scales_{name}", [P, words], U8, at + PIECE)
+            nc.vector.quantize_mx(out=codes[:].bitcast(FP8X4), scales=scales[:], in_=woven[name])
+            mx[name] = codes, scales
 
-        def weave_half(f):
-            q, u = divmod(HALVED, 2)
-            weave(early_woven[q][:, f, u, :], raw_halves[f][:])
-
-        def hand_out(mx, tiles, kts):
-            for at, key in enumerate([(i, kt) for i in tiles for kt in kts]):
-                w_mx[key] = [part[:, at * P : (at + 1) * P] for part in mx]
-
-        def quantise_early(q, f, scales_at):
-            woven = early_woven[q][:, f, :, :].rearrange("p u x -> p (u x)")
-            hand_out(quantise(f"early{q}_{f}", woven, scales_at), (2 * q, 2 * q + 1), (2 * f, 2 * f + 1))
-
-        def quantise_six(f, scales_at):
-            hand_out(quantise(f"six{f}", woven_six[:, f, :], scales_at), (SIX,), (2 * f, 2 * f + 1))
-
-        def new_piece(name, tiles, kts, at):
-            woven = place(f"woven_{name}", [P, len(tiles) * len(kts) * PACK * P], BF16, at)[:]
-            pieces[name] = woven, tiles, kts
-            return woven
-
-        def weave_seven(f, at):
-            woven = new_piece(f"seven{f}", (SEVEN,), (2 * f, 2 * f + 1), at)
-            weave(woven, raw[SEVEN][:, :, f * FRONT : (f + 1) * FRONT])
-
-        def weave_pair(q, kt, copy, at):
-            woven = new_piece(f"pair{q}_{kt}", late_pair(q), (kt,), at)
-            col = kt % 2 * P
-            copy(
-                woven.rearrange("p (u x i r) -> p u x r i", u=2, i=2, r=PACK),
-                raw_pair[q, kt // 2][:, :, :, col : col + P].rearrange("p u r (x i) -> p u x r i", i=2),
-            )
-
-        def last_backs(kt):
-            return raw_back_ten[:, :, (kt - 2) * P : (kt - 1) * P], raw_quarter[kt][:]
-
-        def quantise_piece(name, scales_at=None, codes_at=None):
-            woven, tiles, kts = pieces[name]
-            hand_out(quantise(name, woven, scales_at, codes_at), tiles, kts)
-
-        def group(into, e, kt):
+        def multiply(i, name, kts):
+            e, c = divmod(i, NPASS)
             h, u = divmod(e, 2)
             slots = slice(u * C, (u + 1) * C)
-            for c in range(NPASS):
-                w_codes, w_scales = w_mx[e * NPASS + c, kt]
-                g_codes, g_scales = g_mx[c, h]
+            w_codes, w_scales = mx[name]
+            g_codes, g_scales = mx[f"g{c}_{h}"]
+            for at, kt in enumerate(kts):
+                cols = slice(at * P, (at + 1) * P)
                 nc.tensor.matmul_mx(
-                    out=into,
-                    lhsT=w_codes.bitcast(FP8X4),
-                    lhsT_scale=w_scales,
+                    out=banks[kt, h][:, slots],
+                    lhsT=w_codes[:, cols].bitcast(FP8X4),
+                    lhsT_scale=w_scales[:, cols],
                     rhs=g_codes[:, slots].bitcast(FP8X4),
                     rhs_scale=g_scales[:, slots],
-                    start=(c == 0),
-                    stop=(c == NPASS - 1),
+                    start=(u == 0 and c == 0),
+                    stop=(u == 1 and c == NPASS - 1),
                 )
 
-        def multiply_apart(kt, h):
-            acc[kt, h] = []
-            for u in range(2):
-                bank = psum.tile([P, HALF], F32, name=f"bank{kt % 2}_{h}_{u}")
-                acc[kt, h].append(bank[:, 0:C])
-                group(bank[:, 0:C], 2 * h + u, kt)
+        dx = {}
+        first = {}
 
-        def multiply_together(kt):
-            bank = psum.tile([P, HALF], F32, name=f"bank{kt % 2}_0_0")
-            acc[kt, 0] = [bank[:]]
-            for u in range(2):
-                group(bank[:, u * C : (u + 1) * C], u, kt)
+        def empty(kt, h):
+            if h == 0:
+                dx[kt] = place(f"dx{kt}", [P, S], F32, raw_place(0) + kt * WIDE)
+            nc.scalar.copy(dx[kt][:, h * HALF : (h + 1) * HALF], banks[kt, h][:])
 
-        def empty(kt, at):
-            dx[kt] = place(f"dx{kt}", [P, S], F32, at)
-            col = 0
-            for sums in acc[kt, 0] + acc[kt, 1]:
-                nc.scalar.copy(dx[kt][:, col : col + sums.shape[1]], sums)
-                col = col + sums.shape[1]
+        def gather_first(kt, lo, hi):
+            first[kt, lo] = place(f"first{kt}_{lo}", [P, hi - lo], F32, raw_place(3) + kt * PIECE + 4 * lo)
+            nc.scalar.activation(first[kt, lo][:], dx[kt][:].indirect(entries(pos1_sb, lo, hi)), COPY)
 
-        def gather_first(kt):
-            first[kt] = place(f"first{kt}", [P, T], F32, G1 + RAW_TILE + kt * PIECE)
-            nc.vector.tensor_copy(first[kt][:], dx[kt][:].indirect(pos1_sb[:]))
+        def gather_second_and_store(kt, lo, hi, at):
+            total = place(f"total{kt}_{lo}", [P, hi - lo], F32, at + 4 * lo)
+            nc.vector.tensor_tensor(total[:], dx[kt][:].indirect(entries(pos2_sb, lo, hi)), first[kt, lo][:], ADD)
+            nc.sync.dma_start(out[kt * P : (kt + 1) * P, lo:hi], total[:])
 
-        def gather_second_and_store(kt, at, cuts=(0, T)):
-            for lo, hi in zip(cuts, cuts[1:]):
-                total = place(f"total{kt}_{lo}", [P, hi - lo], F32, at + 4 * lo)
-                picked = dx[kt][:].indirect(pos2_sb[:, lo // PER_COL : hi // PER_COL])
-                nc.vector.tensor_tensor(total[:], picked, first[kt][:, lo:hi], ADD)
-                nc.sync.dma_start(out[kt * P : (kt + 1) * P, lo:hi], total[:])
-
-        load_window(0, 0)
         nc.sync.dma_start(offs_sb[:], offs)
-        for lo, hi in ((0, FIRST_CUT), (FIRST_CUT, S)):
-            nc.sync.dma_start(gate_sb[:, lo:hi], gate[0:P, lo:hi])
-        for i in range(HALVED):
-            load_window(0, 1 + i)
-            load_whole(i)
-        load_window(0, PACK - 1)
-        nc.sync.dma_start(raw_halves[0][:], weight_half(HALVED, 0))
+        load_window(0, 0)
+        load_gate(0)
+        for r in range(1, PACK):
+            load_window(0, r)
         load_window(1, 0)
+        load_whole(0)
         load_window(1, 1)
-        nc.sync.dma_start(raw_halves[1][:], weight_half(HALVED, 1))
+        load_gate(1)
         load_window(1, 2)
-        load_whole(3)
+        load_whole(1)
         load_window(1, 3)
-        for j in range(2):
-            load_whole(4 + j)
-            load_window(2, 2 * j)
-            load_window(2, 2 * j + 1)
-        load_whole(SIX)
-        load_whole(SEVEN)
-        for q in LATE_PAIRS:
-            load_pair(q, 0)
+        load_window(2, 0)
+        load_whole(2)
+        load_window(2, 1)
+        load_window(2, 2)
+        load_whole(3)
+        load_window(2, 3)
+        for i in range(4, 10):
+            load_whole(i)
+        load_half(10, 0)
+        load_half(11, 0)
         nc.sync.dma_start(pos1_sb[:], pos1)
         nc.sync.dma_start(pos2_sb[:], pos2)
-        load_pair(1, 1)
-        nc.sync.dma_start(raw_back_ten[:], weight_half(TEN, 1))
-        for kt in (2, 3):
-            nc.sync.dma_start(raw_quarter[kt][:], weight_rows(ELEVEN)[:, :, kt * P : (kt + 1) * P])
+        load_half(10, 1)
+        load_half(11, 1)
 
-        gather_g(0, G0, (0, FIRST_CUT, S))
-        weave_early(0)
-        weave_early(1)
-        weave_half(0)
-        weave_g(0, 0, raw_place(HALVED))
-        weave_g(0, 1, raw_place(1))
-        gather_g(1, G1)
-        weave_half(1)
-        weave_early(3)
-        weave_early(4)
         for h in range(2):
-            weave_g(1, h, raw_place(4) + h * WIDE)
-        gather_g(2, G0)
-        weave_early(5)
-        woven_six = place("woven_six", [P, 2, PACK * FRONT], BF16, take("fresh", WIDE))
-        weave_whole(SIX, woven_six[:])
-        for h in range(2):
-            weave_g(2, h, raw_place(5) + h * WIDE)
-        weave_seven(0, take("fresh", PIECE))
+            picked[0, h] = place(f"picked0_{h}", [P, PACK, HALF], F32, PICKED + h * RAW_TILE)
+        for r in range(PACK):
+            nc.vector.tensor_tensor(picked[0, 0][:, r, :], windows[0, r][:].indirect(entries(offs_sb, 0, HALF)), gate_sb[0][:], MULT)
+            nc.scalar.activation(picked[0, 1][:, r, :], windows[0, r][:].indirect(entries(offs_sb, HALF, S)), COPY)
 
-        quantise_early(0, 0, take("fresh", WIDE_SCALES))
-        on_gate = [GATE + j * WIDE_SCALES for j in range(1, 4 * S // WIDE_SCALES)]
-        quantise_early(1, 0, LAST_WINDOW_BUT_ONE)
-        quantise_early(2, 0, on_gate[0])
-        for c in range(2):
+        def gather_pass(c, at):
+            whole = place(f"picked{c}", [P, PACK, S], F32, at)
+            for r in range(PACK):
+                nc.scalar.activation(whole[:, r, :], windows[c, r][:].indirect(offs_sb[:]), COPY)
             for h in range(2):
-                quantise_g(c, h, on_gate[1 + 2 * c + h])
-        quantise_six(0, on_gate[-2])
-        quantise_early(0, 1, on_gate[-1])
+                picked[c, h] = whole[:, :, h * HALF : (h + 1) * HALF]
 
-        quantise_g(2, 0)
-        quantise_g(2, 1)
-        for q in LATE_PAIRS:
-            weave_pair(q, 0, nc.vector.tensor_copy, G0 + (q - 1) * PIECE)
-        quantise_piece("seven0")
-        quantise_piece("pair1_0")
-        tail = [take("fresh", PIECE) for j in range(5)]
-        quantise_piece("pair2_0")
-        multiply_apart(0, 0)
-        multiply_apart(1, 0)
-        multiply_apart(0, 1)
-        for q in LATE_PAIRS:
-            weave_pair(q, 1, nc.scalar.copy, take("fresh", PIECE))
-        quantise_piece("pair1_1")
-        quantise_piece("pair2_1", tail[1] - PIECE_SCALES // 2, tail[3] - PIECE_CODES // 2)
-        multiply_apart(1, 1)
+        gather_pass(1, PICKED + 2 * RAW_TILE)
+        on_v, on_s = nc.vector.tensor_copy, nc.scalar.copy
+        ALL = range(4)
 
-        for q in range(1, PAIRS):
-            quantise_early(q, 1, FRONTS_2 + PIECE + q * WIDE_SCALES)
-        quantise_six(1, FRONTS_2 + PIECE)
+        weave(on_v, "w0", raw[0][:], RING)
+        weave(on_v, "g0_0", picked[0, 0][:], LATE)
+        quantise("w0", "fresh")
+        weave_gated(0, 1, picked[0, 1][:], LATE + WIDE)
+        gather_pass(2, PICKED)
+        quantise("g0_0", "fresh")
+        multiply(0, "w0", ALL)
+        weave(on_v, "w1", raw[1][:], RING + WIDE)
+        quantise("g0_1", "fresh")
+        weave(on_v, "w2", raw[2][:], RING + 2 * WIDE)
+        quantise("w1", "fresh")
+        weave_gated(1, 0, picked[1, 0], raw_place(2))
+        quantise("w2", "fresh")
+        weave_gated(1, 1, picked[1, 1], raw_place(2) + WIDE)
+        quantise("g1_0", "fresh")
+        multiply(1, "w1", ALL)
+        weave(on_v, "w3", raw[3][:], RING)
+        quantise("g1_1", "fresh")
+        weave(on_v, "w4", raw[4][:], RING + WIDE)
+        quantise("w3", "fresh")
+        multiply(3, "w3", ALL)
+        weave_gated(2, 0, picked[2, 0], raw_place(4))
+        quantise("w4", "fresh")
+        multiply(4, "w4", ALL)
+        for i in range(5, 8):
+            weave(on_s, f"w{i}", raw[i][:], LATE + (i - 5) * WIDE)
+        for f in range(2):
+            weave(on_s, f"w8_{f}", raw[8][:, :, f * FRONT : (f + 1) * FRONT], LATE + 3 * WIDE + f * PIECE)
+        weave_gated(2, 1, picked[2, 1], raw_place(4) + WIDE)
+        quantise("g2_0")
+        multiply(2, "w2", ALL)
+        quantise("w6")
+        multiply(6, "w6", ALL)
+        quantise("g2_1")
+        quantise("w5", at=raw_place(7))
+        multiply(5, "w5", ALL)
+        quantise("w7")
+        multiply(7, "w7", ALL)
+        for kt in ALL:
+            empty(kt, 0)
+
+        weave(on_v, "w9_0", raw[9][:, :, 0:FRONT], RING + 2 * WIDE)
+        quantise("w8_0")
+        multiply(8, "w8_0", (0, 1))
+        weave(on_v, "w10_0", raw_half[10, 0][:], RING + 2 * WIDE + PIECE)
+        quantise("w9_0")
+        multiply(9, "w9_0", (0, 1))
+        weave(on_v, "w11_0", raw_half[11, 0][:], RING)
+        quantise("w10_0")
+        multiply(10, "w10_0", (0, 1))
+        weave(on_v, "w9_1", raw[9][:, :, FRONT:K], half_place(11, 0))
+        quantise("w11_0")
+        multiply(11, "w11_0", (0, 1))
+        weave(on_v, "w10_1", raw_half[10, 1][:], half_place(11, 0) + PIECE)
+        quantise("w8_1")
+        multiply(8, "w8_1", (2, 3))
+        quantise("w9_1")
+        multiply(9, "w9_1", (2, 3))
+        weave(on_v, "w11_1", raw_half[11, 1][:], RING + PIECE)
+        quantise("w10_1")
+        multiply(10, "w10_1", (2, 3))
+        quantise("w11_1")
+        multiply(11, "w11_1", (2, 3))
+
         for kt in range(2):
-            empty(kt, FRONTS_2 - PIECE + kt * RAW_TILE)
-        multiply_together(2)
-        multiply_together(3)
-        weave_seven(1, tail[0])
-        weave_pair(1, 2, nc.scalar.copy, tail[1])
-        woven = new_piece("pair2_2", late_pair(2), (2,), tail[2])
-        for u, source in enumerate(last_backs(2)):
-            weave(woven[:, u * PACK * P : (u + 1) * PACK * P], source)
-        weave_pair(1, 3, nc.scalar.copy, tail[3])
-
-        gather_first(0)
-        gather_first(1)
-        gather_second_and_store(0, G1)
-        quantise_piece("seven1")
-        quantise_piece("pair1_2")
-        quantise_piece("pair2_2", tail[4] + PIECE // 2 - PIECE_SCALES // 2)
-        multiply_apart(2, 1)
-        gather_second_and_store(1, quarter_place(2))
-        quantise_piece("pair1_3")
-        empty(2, raw_place(3))
-        for u, source in enumerate(last_backs(3)):
-            weave(new_piece(f"end{u}", late_pair(2)[u : u + 1], (3,), tail[4] + u * PIECE // 2), source)
-        gather_first(2)
-        for u in range(2):
-            quantise_piece(f"end{u}")
-        multiply_apart(3, 1)
-        gather_second_and_store(2, quarter_place(3))
-        empty(3, raw_place(3) + WIDE)
-        gather_first(3)
-        gather_second_and_store(3, G1 + 2 * PIECE, (0, LAST_CUT, T))
+            empty(kt, 1)
+        for kt in range(2):
+            gather_first(kt, 0, T)
+            gather_second_and_store(kt, 0, T, half_place(11, 1) + kt * PIECE)
+        for kt in range(2, 4):
+            empty(kt, 1)
+        gather_first(2, 0, T)
+        gather_second_and_store(2, 0, T, raw_place(5))
+        for lo in (0, T // 2):
+            gather_first(3, lo, lo + T // 2)
+            gather_second_and_store(3, lo, lo + T // 2, raw_place(5) + PIECE)

@@ -1,6 +1,7 @@
 from contextlib import ExitStack
 
 import concourse.mybir as mybir
+from concourse.masks import make_identity
 
 K, T, E, C, N = 512, 512, 4, 256, 1536
 S = E * C
@@ -21,11 +22,10 @@ WINDOW_BYTES = 65 * 64
 UNIT = PIECE + 512
 
 WINDOWS = 0
-GATE = WINDOWS + NPASS * PACK * WINDOW_BYTES
-RAW = GATE + 4 * S
+RAW = WINDOWS + NPASS * PACK * WINDOW_BYTES
 PICKED = RAW + 12 * RAW_TILE
 RING = PICKED + 4 * RAW_TILE
-LATE = RING + 3 * WIDE
+LATE = RING + 4 * WIDE
 CODES = LATE + 4 * WIDE
 
 F32 = mybir.dt.float32
@@ -61,19 +61,27 @@ def tile_moe_bdx_lin_none_kernel(tc, dyT, w, gate, offs, pos1, pos2, out):
         offs_sb = held.tile([P, S // PER_COL], U16, name="offs_sb")
         pos1_sb = held.tile([P, T // PER_COL], U16, name="pos1_sb")
         pos2_sb = held.tile([P, T // PER_COL], U16, name="pos2_sb")
-        gate_sb = [place(f"gate{h}", [P, HALF], F32, GATE + h * PIECE) for h in range(2)]
+        gate_sb = held.tile([P, 2, PACK], F32, name="gate_sb")
+        identity = held.tile([P, P], F32, name="identity")
+        make_identity(nc, identity[:])
 
         windows = {}
         for c in range(NPASS):
             for r in range(PACK):
                 width = (HALF if c == 0 else S) + TAIL
                 windows[c, r] = place(f"window{c}_{r}", [P, width], F32, WINDOWS + (c * PACK + r) * WINDOW_BYTES)
-                nc.gpsimd.memset(windows[c, r][:, T:], 0.0)
+                if c == NPASS - 1:
+                    nc.gpsimd.memset(windows[c, r][:, T:], 0.0)
+                elif (c, r) == (1, PACK - 1):
+                    nc.scalar.copy(windows[c, r][:, T:], windows[1, 0][:, T:])
+                else:
+                    nc.vector.memset(windows[c, r][:, T:], 0.0)
 
         raw = {i: place(f"raw{i}", [P, PACK, K], F32, raw_place(i)) for i in range(10)}
         raw_half = {(i, f): place(f"raw{i}_{f}", [P, PACK, FRONT], F32, half_place(i, f)) for f in range(2) for i in (10, 11)}
         picked = {}
-        banks = {(kt, h): psum.tile([P, HALF], F32, name=f"bank{kt}_{h}") for kt in range(4) for h in range(2)}
+        spread = [psum.tile([P, HALF], F32, name=f"bank{2 + h}_1") for h in range(2)]
+        banks = {}
 
         def load_window(c, r):
             rows = dyT[c * PASS : (c + 1) * PASS, :].rearrange("(p r) t -> p r t", r=PACK)
@@ -89,8 +97,8 @@ def tile_moe_bdx_lin_none_kernel(tc, dyT, w, gate, offs, pos1, pos2, out):
         def load_half(i, f):
             nc.sync.dma_start(raw_half[i, f][:], weight_rows(i)[:, :, f * FRONT : (f + 1) * FRONT])
 
-        def load_gate(h):
-            nc.sync.dma_start(gate_sb[h][:], gate[0:P, h * HALF : (h + 1) * HALF])
+        def on_g(dst, src):
+            nc.gpsimd.tensor_scalar(dst.rearrange("p x r i -> p x i r"), src.rearrange("p x r i -> p x i r"), 1.0, 0.0, MULT, ADD)
 
         woven, mx = {}, {}
         count = {"fresh": 0, "windows": 0}
@@ -108,7 +116,7 @@ def tile_moe_bdx_lin_none_kernel(tc, dyT, w, gate, offs, pos1, pos2, out):
         def weave_gated(c, h, src, at):
             name = f"g{c}_{h}"
             woven[name] = place(f"woven_{name}", [P, PACK * HALF], BF16, at)[:]
-            weights = gate_sb[h][:].rearrange("p (x i) -> p x i", i=2).unsqueeze(2).to_broadcast([P, HALF // 2, PACK, 2])
+            weights = spread[h][:].rearrange("p (x i) -> p x i", i=2).unsqueeze(2).to_broadcast([P, HALF // 2, PACK, 2])
             nc.vector.tensor_tensor(
                 woven[name].rearrange("p (x i r) -> p x r i", i=2, r=PACK),
                 src.rearrange("p r (x i) -> p x r i", i=2),
@@ -134,6 +142,8 @@ def tile_moe_bdx_lin_none_kernel(tc, dyT, w, gate, offs, pos1, pos2, out):
             g_codes, g_scales = mx[f"g{c}_{h}"]
             for at, kt in enumerate(kts):
                 cols = slice(at * P, (at + 1) * P)
+                if (kt, h) not in banks:
+                    banks[kt, h] = psum.tile([P, HALF], F32, name=f"bank{kt}_{h}")
                 nc.tensor.matmul_mx(
                     out=banks[kt, h][:, slots],
                     lhsT=w_codes[:, cols].bitcast(FP8X4),
@@ -147,10 +157,10 @@ def tile_moe_bdx_lin_none_kernel(tc, dyT, w, gate, offs, pos1, pos2, out):
         dx = {}
         first = {}
 
-        def empty(kt, h):
+        def empty(kt, h, copy=nc.scalar.copy):
             if h == 0:
                 dx[kt] = place(f"dx{kt}", [P, S], F32, raw_place(0) + kt * WIDE)
-            nc.scalar.copy(dx[kt][:, h * HALF : (h + 1) * HALF], banks[kt, h][:])
+            copy(dx[kt][:, h * HALF : (h + 1) * HALF], banks[kt, h][:])
 
         def gather_first(kt, lo, hi):
             first[kt, lo] = place(f"first{kt}_{lo}", [P, hi - lo], F32, raw_place(3) + kt * PIECE + 4 * lo)
@@ -161,25 +171,26 @@ def tile_moe_bdx_lin_none_kernel(tc, dyT, w, gate, offs, pos1, pos2, out):
             nc.vector.tensor_tensor(total[:], dx[kt][:].indirect(entries(pos2_sb, lo, hi)), first[kt, lo][:], ADD)
             nc.sync.dma_start(out[kt * P : (kt + 1) * P, lo:hi], total[:])
 
-        nc.sync.dma_start(offs_sb[:], offs)
         load_window(0, 0)
-        load_gate(0)
-        for r in range(1, PACK):
-            load_window(0, r)
+        nc.sync.dma_start(offs_sb[:], offs)
+        load_window(0, 1)
+        nc.sync.dma_start(gate_sb[:], gate[0, :].rearrange("(h p j) -> p h j", h=2, j=PACK))
+        load_window(0, 2)
+        load_window(0, 3)
         load_window(1, 0)
         load_whole(0)
         load_window(1, 1)
-        load_gate(1)
-        load_window(1, 2)
         load_whole(1)
+        load_window(1, 2)
         load_window(1, 3)
-        load_window(2, 0)
         load_whole(2)
-        load_window(2, 1)
-        load_window(2, 2)
+        load_window(2, 0)
         load_whole(3)
+        load_window(2, 1)
+        load_whole(4)
+        load_window(2, 2)
         load_window(2, 3)
-        for i in range(4, 10):
+        for i in range(5, 10):
             load_whole(i)
         load_half(10, 0)
         load_half(11, 0)
@@ -189,9 +200,13 @@ def tile_moe_bdx_lin_none_kernel(tc, dyT, w, gate, offs, pos1, pos2, out):
         load_half(11, 1)
 
         for h in range(2):
+            for j in range(PACK):
+                nc.tensor.transpose(spread[h][:, j::PACK], gate_sb[:, h, j : j + 1].to_broadcast([P, P]), identity[:])
+
+        for h in range(2):
             picked[0, h] = place(f"picked0_{h}", [P, PACK, HALF], F32, PICKED + h * RAW_TILE)
         for r in range(PACK):
-            nc.vector.tensor_tensor(picked[0, 0][:, r, :], windows[0, r][:].indirect(entries(offs_sb, 0, HALF)), gate_sb[0][:], MULT)
+            nc.vector.tensor_copy(picked[0, 0][:, r, :], windows[0, r][:].indirect(entries(offs_sb, 0, HALF)))
             nc.scalar.activation(picked[0, 1][:, r, :], windows[0, r][:].indirect(entries(offs_sb, HALF, S)), COPY)
 
         def gather_pass(c, at):
@@ -205,65 +220,71 @@ def tile_moe_bdx_lin_none_kernel(tc, dyT, w, gate, offs, pos1, pos2, out):
         on_v, on_s = nc.vector.tensor_copy, nc.scalar.copy
         ALL = range(4)
 
-        weave(on_v, "w0", raw[0][:], RING)
-        weave(on_v, "g0_0", picked[0, 0][:], LATE)
-        quantise("w0", "fresh")
+        def weave_part(copy, name, i, f):
+            copy(
+                woven[name][:, f * PACK * FRONT : (f + 1) * PACK * FRONT].rearrange("p (x i r) -> p x r i", i=2, r=PACK),
+                raw[i][:, :, f * FRONT : (f + 1) * FRONT].rearrange("p r (x i) -> p x r i", i=2),
+            )
+
+        weave_gated(0, 0, picked[0, 0][:], LATE)
+        weave(on_g, "w0", raw[0][:], RING)
         weave_gated(0, 1, picked[0, 1][:], LATE + WIDE)
         gather_pass(2, PICKED)
         quantise("g0_0", "fresh")
-        multiply(0, "w0", ALL)
-        weave(on_v, "w1", raw[1][:], RING + WIDE)
         quantise("g0_1", "fresh")
-        weave(on_v, "w2", raw[2][:], RING + 2 * WIDE)
+        weave(on_v, "w1", raw[1][:], RING + WIDE)
+        quantise("w0", "fresh")
+        multiply(0, "w0", ALL)
+        weave(on_v, "w2", raw[2][:], RING + 2 * WIDE + PIECE)
         quantise("w1", "fresh")
-        weave_gated(1, 0, picked[1, 0], raw_place(2))
         quantise("w2", "fresh")
+        weave_gated(1, 0, picked[1, 0], raw_place(2))
+        weave(on_g, "w3", raw[3][:], RING + 2 * WIDE - PIECE + WIDE // 2)
+        woven["w4"] = place("woven_w4", [P, PACK * K], BF16, RING + 3 * WIDE)[:]
+        weave_part(on_g, "w4", 4, 0)
         weave_gated(1, 1, picked[1, 1], raw_place(2) + WIDE)
         quantise("g1_0", "fresh")
         multiply(1, "w1", ALL)
-        weave(on_v, "w3", raw[3][:], RING)
+        weave_part(on_v, "w4", 4, 1)
         quantise("g1_1", "fresh")
-        weave(on_v, "w4", raw[4][:], RING + WIDE)
         quantise("w3", "fresh")
         multiply(3, "w3", ALL)
-        weave_gated(2, 0, picked[2, 0], raw_place(4))
+        weave(on_v, "w5", raw[5][:], RING)
         quantise("w4", "fresh")
         multiply(4, "w4", ALL)
-        for i in range(5, 8):
-            weave(on_s, f"w{i}", raw[i][:], LATE + (i - 5) * WIDE)
-        for f in range(2):
-            weave(on_s, f"w8_{f}", raw[8][:, :, f * FRONT : (f + 1) * FRONT], LATE + 3 * WIDE + f * PIECE)
-        weave_gated(2, 1, picked[2, 1], raw_place(4) + WIDE)
-        quantise("g2_0")
+        quantise("w5")
+        weave_gated(2, 0, picked[2, 0], raw_place(5))
+        weave(on_s, "w6", raw[6][:], LATE)
+        weave(on_g, "w7", raw[7][:], RING)
+        weave(on_s, "w8", raw[8][:], LATE + WIDE)
+        weave(on_s, "w9_0", raw[9][:, :, 0:FRONT], LATE + 2 * WIDE)
+        weave(on_s, "w10_0", raw_half[10, 0][:], LATE + 3 * WIDE)
+        weave(on_s, "w9_1", raw[9][:, :, FRONT:K], LATE + 2 * WIDE + PIECE)
+        weave_gated(2, 1, picked[2, 1], raw_place(5) + WIDE)
+        quantise("g2_0", at=raw_place(8))
         multiply(2, "w2", ALL)
-        quantise("w6")
-        multiply(6, "w6", ALL)
-        quantise("g2_1")
-        quantise("w5", at=raw_place(7))
         multiply(5, "w5", ALL)
+        quantise("w6")
+        quantise("g2_1")
+        multiply(6, "w6", ALL)
         quantise("w7")
         multiply(7, "w7", ALL)
+        quantise("w8")
+        multiply(8, "w8", ALL)
         for kt in ALL:
             empty(kt, 0)
 
-        weave(on_v, "w9_0", raw[9][:, :, 0:FRONT], RING + 2 * WIDE)
-        quantise("w8_0")
-        multiply(8, "w8_0", (0, 1))
-        weave(on_v, "w10_0", raw_half[10, 0][:], RING + 2 * WIDE + PIECE)
         quantise("w9_0")
         multiply(9, "w9_0", (0, 1))
-        weave(on_v, "w11_0", raw_half[11, 0][:], RING)
+        weave(on_v, "w11_0", raw_half[11, 0][:], RING + WIDE + PIECE)
         quantise("w10_0")
         multiply(10, "w10_0", (0, 1))
-        weave(on_v, "w9_1", raw[9][:, :, FRONT:K], half_place(11, 0))
         quantise("w11_0")
         multiply(11, "w11_0", (0, 1))
-        weave(on_v, "w10_1", raw_half[10, 1][:], half_place(11, 0) + PIECE)
-        quantise("w8_1")
-        multiply(8, "w8_1", (2, 3))
-        quantise("w9_1")
+        weave(on_v, "w10_1", raw_half[10, 1][:], RING + WIDE)
+        quantise("w9_1", at=half_place(11, 0))
         multiply(9, "w9_1", (2, 3))
-        weave(on_v, "w11_1", raw_half[11, 1][:], RING + PIECE)
+        weave(on_v, "w11_1", raw_half[11, 1][:], RING + 2 * WIDE)
         quantise("w10_1")
         multiply(10, "w10_1", (2, 3))
         quantise("w11_1")
@@ -271,11 +292,11 @@ def tile_moe_bdx_lin_none_kernel(tc, dyT, w, gate, offs, pos1, pos2, out):
 
         for kt in range(2):
             empty(kt, 1)
+        for kt in range(2, 4):
+            empty(kt, 1, on_v)
         for kt in range(2):
             gather_first(kt, 0, T)
             gather_second_and_store(kt, 0, T, half_place(11, 1) + kt * PIECE)
-        for kt in range(2, 4):
-            empty(kt, 1)
         gather_first(2, 0, T)
         gather_second_and_store(2, 0, T, raw_place(5))
         for lo in (0, T // 2):

@@ -56,7 +56,7 @@ def tile_moe_bdx_lin_none_kernel(tc, dyT, w, gate, offs, pos1, pos2, out):
             return RAW + i * RAW_TILE
 
         def half_place(i, f):
-            return raw_place(10) + (2 * f + i - 10) * WIDE
+            return raw_place(9) + (3 * f + i - 9) * WIDE
 
         offs_sb = held.tile([P, S // PER_COL], U16, name="offs_sb")
         pos1_sb = held.tile([P, T // PER_COL], U16, name="pos1_sb")
@@ -77,8 +77,8 @@ def tile_moe_bdx_lin_none_kernel(tc, dyT, w, gate, offs, pos1, pos2, out):
                 else:
                     nc.vector.memset(windows[c, r][:, T:], 0.0)
 
-        raw = {i: place(f"raw{i}", [P, PACK, K], F32, raw_place(i)) for i in range(10)}
-        raw_half = {(i, f): place(f"raw{i}_{f}", [P, PACK, FRONT], F32, half_place(i, f)) for f in range(2) for i in (10, 11)}
+        raw = {i: place(f"raw{i}", [P, PACK, K], F32, raw_place(i)) for i in range(9)}
+        raw_half = {(i, f): place(f"raw{i}_{f}", [P, PACK, FRONT], F32, half_place(i, f))[:] for f in range(2) for i in (9, 10, 11)}
         picked = {}
         spread = [psum.tile([P, HALF], F32, name=f"bank{2 + h}_1") for h in range(2)]
         banks = {}
@@ -95,7 +95,7 @@ def tile_moe_bdx_lin_none_kernel(tc, dyT, w, gate, offs, pos1, pos2, out):
             nc.sync.dma_start(raw[i][:], weight_rows(i))
 
         def load_half(i, f):
-            nc.sync.dma_start(raw_half[i, f][:], weight_rows(i)[:, :, f * FRONT : (f + 1) * FRONT])
+            nc.sync.dma_start(raw_half[i, f], weight_rows(i)[:, :, f * FRONT : (f + 1) * FRONT])
 
         def on_g(dst, src):
             nc.gpsimd.tensor_scalar(dst.rearrange("p x r i -> p x i r"), src.rearrange("p x r i -> p x i r"), 1.0, 0.0, MULT, ADD)
@@ -106,46 +106,47 @@ def tile_moe_bdx_lin_none_kernel(tc, dyT, w, gate, offs, pos1, pos2, out):
         def entries(lst, lo, hi):
             return lst[:, lo // PER_COL : hi // PER_COL]
 
-        def weave(copy, name, src, at):
-            woven[name] = place(f"woven_{name}", [P, PACK * src.shape[2]], BF16, at)[:]
-            copy(
-                woven[name].rearrange("p (x i r) -> p x r i", i=2, r=PACK),
-                src.rearrange("p r (x i) -> p x r i", i=2),
-            )
+        def new_woven(name, words, at):
+            woven[name] = place(f"woven_{name}", [P, PACK * words], BF16, at)[:]
 
-        def weave_gated(c, h, src, at):
-            name = f"g{c}_{h}"
-            woven[name] = place(f"woven_{name}", [P, PACK * HALF], BF16, at)[:]
+        def part(name, lo, words):
+            return woven[name][:, PACK * lo : PACK * (lo + words)].rearrange("p (x i r) -> p x r i", i=2, r=PACK)
+
+        def pairs(src):
+            return src.rearrange("p r (x i) -> p x r i", i=2)
+
+        def weave(copy, name, lo, src):
+            copy(part(name, lo, src.shape[2]), pairs(src))
+
+        def weave_gated(c, h):
             weights = spread[h][:].rearrange("p (x i) -> p x i", i=2).unsqueeze(2).to_broadcast([P, HALF // 2, PACK, 2])
-            nc.vector.tensor_tensor(
-                woven[name].rearrange("p (x i r) -> p x r i", i=2, r=PACK),
-                src.rearrange("p r (x i) -> p x r i", i=2),
-                weights,
-                MULT,
-            )
+            nc.vector.tensor_tensor(part(f"g{c}", h * HALF, HALF), pairs(picked[c, h]), weights, MULT)
 
         def quantise(name, kind="windows", at=None):
             words = woven[name].shape[1] // PACK
             if at is None:
-                at = {"fresh": CODES, "windows": WINDOWS}[kind] + count[kind] * UNIT
-                count[kind] = count[kind] + 1
+                at = {"fresh": CODES, "windows": WINDOWS}[kind] + count[kind]
+                count[kind] = count[kind] + 5 * words
             codes = place(f"codes_{name}", [P, words], U32, at)
-            scales = place(f"scales_{name}", [P, words], U8, at + PIECE)
+            scales = place(f"scales_{name}", [P, words], U8, at + 4 * words)
             nc.vector.quantize_mx(out=codes[:].bitcast(FP8X4), scales=scales[:], in_=woven[name])
             mx[name] = codes, scales
 
-        def multiply(i, name, kts):
+        def multiply(i, name, lo, kts):
             e, c = divmod(i, NPASS)
             h, u = divmod(e, 2)
-            slots = slice(u * C, (u + 1) * C)
+            slots = slice(e * C, (e + 1) * C)
             w_codes, w_scales = mx[name]
-            g_codes, g_scales = mx[f"g{c}_{h}"]
+            g_codes, g_scales = mx[f"g{c}"]
+            if c == NPASS - 1:
+                g_codes, g_scales = mx[f"g{c}_{h}"]
+                slots = slice(u * C, (u + 1) * C)
             for at, kt in enumerate(kts):
-                cols = slice(at * P, (at + 1) * P)
+                cols = slice(lo + at * P, lo + (at + 1) * P)
                 if (kt, h) not in banks:
                     banks[kt, h] = psum.tile([P, HALF], F32, name=f"bank{kt}_{h}")
                 nc.tensor.matmul_mx(
-                    out=banks[kt, h][:, slots],
+                    out=banks[kt, h][:, u * C : (u + 1) * C],
                     lhsT=w_codes[:, cols].bitcast(FP8X4),
                     lhsT_scale=w_scales[:, cols],
                     rhs=g_codes[:, slots].bitcast(FP8X4),
@@ -190,21 +191,21 @@ def tile_moe_bdx_lin_none_kernel(tc, dyT, w, gate, offs, pos1, pos2, out):
         load_whole(4)
         load_window(2, 2)
         load_window(2, 3)
-        for i in range(5, 10):
+        for i in range(5, 9):
             load_whole(i)
-        load_half(10, 0)
-        load_half(11, 0)
+        for i in range(9, 12):
+            load_half(i, 0)
         nc.sync.dma_start(pos1_sb[:], pos1)
         nc.sync.dma_start(pos2_sb[:], pos2)
-        load_half(10, 1)
-        load_half(11, 1)
+        for i in range(9, 12):
+            load_half(i, 1)
 
         for h in range(2):
             for j in range(PACK):
                 nc.tensor.transpose(spread[h][:, j::PACK], gate_sb[:, h, j : j + 1].to_broadcast([P, P]), identity[:])
 
         for h in range(2):
-            picked[0, h] = place(f"picked0_{h}", [P, PACK, HALF], F32, PICKED + h * RAW_TILE)
+            picked[0, h] = place(f"picked0_{h}", [P, PACK, HALF], F32, PICKED + h * RAW_TILE)[:]
         for r in range(PACK):
             nc.vector.tensor_copy(picked[0, 0][:, r, :], windows[0, r][:].indirect(entries(offs_sb, 0, HALF)))
             nc.scalar.activation(picked[0, 1][:, r, :], windows[0, r][:].indirect(entries(offs_sb, HALF, S)), COPY)
@@ -212,7 +213,9 @@ def tile_moe_bdx_lin_none_kernel(tc, dyT, w, gate, offs, pos1, pos2, out):
         def gather_pass(c, at):
             whole = place(f"picked{c}", [P, PACK, S], F32, at)
             for r in range(PACK):
-                nc.scalar.activation(whole[:, r, :], windows[c, r][:].indirect(offs_sb[:]), COPY)
+                cuts = (0, HALF, S) if (c, r) == (NPASS - 1, PACK - 1) else (0, S)
+                for lo, hi in zip(cuts, cuts[1:]):
+                    nc.scalar.activation(whole[:, r, lo:hi], windows[c, r][:].indirect(entries(offs_sb, lo, hi)), COPY)
             for h in range(2):
                 picked[c, h] = whole[:, :, h * HALF : (h + 1) * HALF]
 
@@ -220,83 +223,100 @@ def tile_moe_bdx_lin_none_kernel(tc, dyT, w, gate, offs, pos1, pos2, out):
         on_v, on_s = nc.vector.tensor_copy, nc.scalar.copy
         ALL = range(4)
 
-        def weave_part(copy, name, i, f):
-            copy(
-                woven[name][:, f * PACK * FRONT : (f + 1) * PACK * FRONT].rearrange("p (x i r) -> p x r i", i=2, r=PACK),
-                raw[i][:, :, f * FRONT : (f + 1) * FRONT].rearrange("p r (x i) -> p x r i", i=2),
-            )
+        def front(i):
+            return raw[i][:, :, 0:FRONT]
 
-        weave_gated(0, 0, picked[0, 0][:], LATE)
-        weave(on_g, "w0", raw[0][:], RING)
-        weave_gated(0, 1, picked[0, 1][:], LATE + WIDE)
+        def back(i):
+            return raw[i][:, :, FRONT:K]
+
+        new_woven("g0", S, LATE)
+        new_woven("w01", 2 * K, RING)
+        weave_gated(0, 0)
+        weave(on_g, "w01", 0, raw[0][:])
+        weave(on_g, "w01", K, front(1))
+        weave_gated(0, 1)
         gather_pass(2, PICKED)
-        quantise("g0_0", "fresh")
-        quantise("g0_1", "fresh")
-        weave(on_v, "w1", raw[1][:], RING + WIDE)
-        quantise("w0", "fresh")
-        multiply(0, "w0", ALL)
-        weave(on_v, "w2", raw[2][:], RING + 2 * WIDE + PIECE)
-        quantise("w1", "fresh")
+        weave(on_v, "w01", K + FRONT, back(1))
+        quantise("g0", "fresh")
+        new_woven("w2", K, RING + 2 * WIDE)
+        weave(on_v, "w2", 0, raw[2][:])
+        quantise("w01", "fresh")
+        multiply(0, "w01", 0, ALL)
         quantise("w2", "fresh")
-        weave_gated(1, 0, picked[1, 0], raw_place(2))
-        weave(on_g, "w3", raw[3][:], RING + 2 * WIDE - PIECE + WIDE // 2)
-        woven["w4"] = place("woven_w4", [P, PACK * K], BF16, RING + 3 * WIDE)[:]
-        weave_part(on_g, "w4", 4, 0)
-        weave_gated(1, 1, picked[1, 1], raw_place(2) + WIDE)
-        quantise("g1_0", "fresh")
-        multiply(1, "w1", ALL)
-        weave_part(on_v, "w4", 4, 1)
-        quantise("g1_1", "fresh")
-        quantise("w3", "fresh")
-        multiply(3, "w3", ALL)
-        weave(on_v, "w5", raw[5][:], RING)
-        quantise("w4", "fresh")
-        multiply(4, "w4", ALL)
-        quantise("w5")
-        weave_gated(2, 0, picked[2, 0], raw_place(5))
-        weave(on_s, "w6", raw[6][:], LATE)
-        weave(on_g, "w7", raw[7][:], RING)
-        weave(on_s, "w8", raw[8][:], LATE + WIDE)
-        weave(on_s, "w9_0", raw[9][:, :, 0:FRONT], LATE + 2 * WIDE)
-        weave(on_s, "w10_0", raw_half[10, 0][:], LATE + 3 * WIDE)
-        weave(on_s, "w9_1", raw[9][:, :, FRONT:K], LATE + 2 * WIDE + PIECE)
-        weave_gated(2, 1, picked[2, 1], raw_place(5) + WIDE)
-        quantise("g2_0", at=raw_place(8))
-        multiply(2, "w2", ALL)
-        multiply(5, "w5", ALL)
-        quantise("w6")
-        quantise("g2_1")
-        multiply(6, "w6", ALL)
+
+        new_woven("g1", S, raw_place(2))
+        new_woven("w34", 2 * K, RING + 2 * WIDE)
+        weave_gated(1, 0)
+        weave(on_g, "w34", 0, raw[3][:])
+        weave(on_g, "w34", K, front(4))
+        weave_gated(1, 1)
+        weave(on_v, "w34", K + FRONT, back(4))
+        quantise("g1", "fresh")
+        multiply(1, "w01", K, ALL)
+        quantise("w34", "fresh")
+        multiply(3, "w34", 0, ALL)
+        multiply(4, "w34", K, ALL)
+
+        new_woven("g2", S, raw_place(4))
+        new_woven("w56", 2 * K, RING + 2 * WIDE)
+        weave_gated(2, 0)
+        weave(on_g, "w56", 0, raw[5][:])
+        weave(on_g, "w56", K, front(6))
+        weave(on_s, "w56", K + FRONT, back(6))
+        for i in (7, 8):
+            new_woven(f"w{i}", K, RING + (i - 7) * WIDE)
+            weave(on_s, f"w{i}", 0, raw[i][:])
+        def weave_last(copy, i, f):
+            tiles = woven[f"last{f}"].rearrange("p (t u x i r) -> p t u x r i", t=2, u=NPASS, i=2, r=PACK)
+            copy(tiles[:, :, i - 9, :, :, :], raw_half[i, f].rearrange("p r (t x i) -> p t x r i", t=2, i=2))
+
+        def finish(kt):
+            f, t = divmod(kt, 2)
+            words = NPASS * P
+            woven[f"row{kt}"] = woven[f"last{f}"][:, t * PACK * words : (t + 1) * PACK * words]
+            quantise(f"row{kt}")
+            for u in range(NPASS):
+                multiply(9 + u, f"row{kt}", u * P, (kt,))
+
+        for f in range(2):
+            new_woven(f"last{f}", NPASS * FRONT, LATE + f * 3 * PIECE)
+        for i in (9, 10):
+            weave_last(on_s, i, 0)
+        weave_gated(2, 1)
+        quantise("w56")
+        multiply(6, "w56", K, ALL)
+        for h in range(2):
+            woven[f"g2_{h}"] = woven["g2"][:, h * PACK * HALF : (h + 1) * PACK * HALF]
+        mx["g2"] = mx["g1"]
+        quantise("g2_0", at=raw_place(7))
+        for kt in ALL:
+            multiply(2, "w2", kt * P, (kt,))
+            multiply(5, "w56", kt * P, (kt,))
         quantise("w7")
-        multiply(7, "w7", ALL)
+        multiply(7, "w7", 0, ALL)
+        quantise("g2_1", at=raw_place(7) + WIDE)
         quantise("w8")
-        multiply(8, "w8", ALL)
+        multiply(8, "w8", 0, ALL)
         for kt in ALL:
             empty(kt, 0)
 
-        quantise("w9_0")
-        multiply(9, "w9_0", (0, 1))
-        weave(on_v, "w11_0", raw_half[11, 0][:], RING + WIDE + PIECE)
-        quantise("w10_0")
-        multiply(10, "w10_0", (0, 1))
-        quantise("w11_0")
-        multiply(11, "w11_0", (0, 1))
-        weave(on_v, "w10_1", raw_half[10, 1][:], RING + WIDE)
-        quantise("w9_1", at=half_place(11, 0))
-        multiply(9, "w9_1", (2, 3))
-        weave(on_v, "w11_1", raw_half[11, 1][:], RING + 2 * WIDE)
-        quantise("w10_1")
-        multiply(10, "w10_1", (2, 3))
-        quantise("w11_1")
-        multiply(11, "w11_1", (2, 3))
+        weave_last(on_v, 11, 0)
+        finish(0)
+        weave_last(on_v, 9, 1)
+        finish(1)
+        for i in (10, 11):
+            weave_last(on_v, i, 1)
+        finish(2)
+        finish(3)
 
-        for kt in range(2):
-            empty(kt, 1)
-        for kt in range(2, 4):
-            empty(kt, 1, on_v)
-        for kt in range(2):
-            gather_first(kt, 0, T)
-            gather_second_and_store(kt, 0, T, half_place(11, 1) + kt * PIECE)
+        empty(0, 1)
+        gather_first(0, 0, T)
+        empty(1, 1)
+        gather_first(1, 0, T)
+        gather_second_and_store(0, 0, T, half_place(11, 1))
+        empty(2, 1)
+        empty(3, 1, on_v)
+        gather_second_and_store(1, 0, T, half_place(11, 1) + PIECE)
         gather_first(2, 0, T)
         gather_second_and_store(2, 0, T, raw_place(5))
         for lo in (0, T // 2):

@@ -13,6 +13,8 @@ HALF = S // 2
 FRONT = K // 2
 PER_COL = 16
 TAIL = 8
+SHARE = {1: 384, 4: 384, 6: 320}
+LAST_CUT = T - P
 
 KIB = 1024
 RAW_TILE = 8 * KIB
@@ -213,8 +215,8 @@ def tile_moe_bdx_lin_none_kernel(tc, dyT, w, gate, offs, pos1, pos2, out):
         def gather_pass(c, at):
             whole = place(f"picked{c}", [P, PACK, S], F32, at)
             for r in range(PACK):
-                cuts = (0, HALF, S) if (c, r) == (NPASS - 1, PACK - 1) else (0, S)
-                for lo, hi in zip(cuts, cuts[1:]):
+                cuts = ((0, HALF), (HALF + C, S)) if (c, r) == (NPASS - 1, PACK - 1) else ((0, S),)
+                for lo, hi in cuts:
                     nc.scalar.activation(whole[:, r, lo:hi], windows[c, r][:].indirect(entries(offs_sb, lo, hi)), COPY)
             for h in range(2):
                 picked[c, h] = whole[:, :, h * HALF : (h + 1) * HALF]
@@ -224,19 +226,19 @@ def tile_moe_bdx_lin_none_kernel(tc, dyT, w, gate, offs, pos1, pos2, out):
         ALL = range(4)
 
         def front(i):
-            return raw[i][:, :, 0:FRONT]
+            return raw[i][:, :, 0 : SHARE[i]]
 
         def back(i):
-            return raw[i][:, :, FRONT:K]
+            return raw[i][:, :, SHARE[i] : K]
 
         new_woven("g0", S, LATE)
         new_woven("w01", 2 * K, RING)
-        weave_gated(0, 0)
+        weave_gated(0, 1)
         weave(on_g, "w01", 0, raw[0][:])
         weave(on_g, "w01", K, front(1))
-        weave_gated(0, 1)
+        weave_gated(0, 0)
         gather_pass(2, PICKED)
-        weave(on_v, "w01", K + FRONT, back(1))
+        weave(on_v, "w01", K + SHARE[1], back(1))
         quantise("g0", "fresh")
         new_woven("w2", K, RING + 2 * WIDE)
         weave(on_v, "w2", 0, raw[2][:])
@@ -250,64 +252,63 @@ def tile_moe_bdx_lin_none_kernel(tc, dyT, w, gate, offs, pos1, pos2, out):
         weave(on_g, "w34", 0, raw[3][:])
         weave(on_g, "w34", K, front(4))
         weave_gated(1, 1)
-        weave(on_v, "w34", K + FRONT, back(4))
+        nc.vector.tensor_copy(picked[2, 1][:, PACK - 1, 0:C], windows[2, PACK - 1][:].indirect(entries(offs_sb, HALF, HALF + C)))
+        weave(on_v, "w34", K + SHARE[4], back(4))
         quantise("g1", "fresh")
         multiply(1, "w01", K, ALL)
         quantise("w34", "fresh")
         multiply(3, "w34", 0, ALL)
         multiply(4, "w34", K, ALL)
 
-        new_woven("g2", S, raw_place(4))
-        new_woven("w56", 2 * K, RING + 2 * WIDE)
-        weave_gated(2, 0)
-        weave(on_g, "w56", 0, raw[5][:])
-        weave(on_g, "w56", K, front(6))
-        weave(on_s, "w56", K + FRONT, back(6))
-        for i in (7, 8):
-            new_woven(f"w{i}", K, RING + (i - 7) * WIDE)
-            weave(on_s, f"w{i}", 0, raw[i][:])
-        def weave_last(copy, i, f):
-            tiles = woven[f"last{f}"].rearrange("p (t u x i r) -> p t u x r i", t=2, u=NPASS, i=2, r=PACK)
-            copy(tiles[:, :, i - 9, :, :, :], raw_half[i, f].rearrange("p r (t x i) -> p t x r i", t=2, i=2))
+        def by_rows(name, u, kts, src):
+            tiles = woven[name].rearrange("p (t u x i r) -> p t u x r i", t=K // P, u=NPASS, i=2, r=PACK)
+            return tiles[:, kts[0] : kts[-1] + 1, u, :, :, :], src.rearrange("p r (t x i) -> p t x r i", t=len(kts), i=2)
 
-        def finish(kt):
-            f, t = divmod(kt, 2)
+        def finish(e, kt, at=None):
             words = NPASS * P
-            woven[f"row{kt}"] = woven[f"last{f}"][:, t * PACK * words : (t + 1) * PACK * words]
-            quantise(f"row{kt}")
+            name = f"e{e}_{kt}"
+            woven[name] = woven[f"e{e}"][:, kt * PACK * words : (kt + 1) * PACK * words]
+            quantise(name, at=at)
             for u in range(NPASS):
-                multiply(9 + u, f"row{kt}", u * P, (kt,))
+                multiply(e * NPASS + u, name, u * P, (kt,))
 
-        for f in range(2):
-            new_woven(f"last{f}", NPASS * FRONT, LATE + f * 3 * PIECE)
+        new_woven("g2", S, raw_place(4))
+        new_woven("w5", K, RING + 3 * WIDE)
+        new_woven("e2", NPASS * K, RING)
+        new_woven("e3", NPASS * K, LATE)
+        weave_gated(2, 0)
+        weave(on_g, "w5", 0, raw[5][:])
+        for kt in range(2):
+            on_g(*[side[:, 0, :, :, :] for side in by_rows("e2", 0, (kt,), raw[6][:, :, kt * P : (kt + 1) * P])])
+        on_s(*by_rows("e2", 0, (2, 3), raw[6][:, :, FRONT:K]))
+        for i in (7, 8):
+            on_s(*by_rows("e2", i - 6, ALL, raw[i][:]))
         for i in (9, 10):
-            weave_last(on_s, i, 0)
+            on_s(*by_rows("e3", i - 9, (0, 1), raw_half[i, 0]))
         weave_gated(2, 1)
-        quantise("w56")
-        multiply(6, "w56", K, ALL)
+        quantise("w5")
         for h in range(2):
             woven[f"g2_{h}"] = woven["g2"][:, h * PACK * HALF : (h + 1) * PACK * HALF]
         mx["g2"] = mx["g1"]
         quantise("g2_0", at=raw_place(7))
         for kt in ALL:
             multiply(2, "w2", kt * P, (kt,))
-            multiply(5, "w56", kt * P, (kt,))
-        quantise("w7")
-        multiply(7, "w7", 0, ALL)
+            multiply(5, "w5", kt * P, (kt,))
         quantise("g2_1", at=raw_place(7) + WIDE)
-        quantise("w8")
-        multiply(8, "w8", 0, ALL)
+        finish(2, 0)
+        finish(2, 1)
         for kt in ALL:
             empty(kt, 0)
 
-        weave_last(on_v, 11, 0)
-        finish(0)
-        weave_last(on_v, 9, 1)
-        finish(1)
-        for i in (10, 11):
-            weave_last(on_v, i, 1)
-        finish(2)
-        finish(3)
+        on_v(*by_rows("e3", 2, (0, 1), raw_half[11, 0]))
+        finish(2, 2, half_place(10, 0))
+        finish(3, 0)
+        finish(2, 3, half_place(10, 0) + PIECE)
+        finish(3, 1)
+        for i in (9, 10, 11):
+            on_v(*by_rows("e3", i - 9, (2, 3), raw_half[i, 1]))
+        finish(3, 2)
+        finish(3, 3)
 
         empty(0, 1)
         gather_first(0, 0, T)
@@ -315,10 +316,10 @@ def tile_moe_bdx_lin_none_kernel(tc, dyT, w, gate, offs, pos1, pos2, out):
         gather_first(1, 0, T)
         gather_second_and_store(0, 0, T, half_place(11, 1))
         empty(2, 1)
-        empty(3, 1, on_v)
         gather_second_and_store(1, 0, T, half_place(11, 1) + PIECE)
+        empty(3, 1, on_v)
         gather_first(2, 0, T)
         gather_second_and_store(2, 0, T, raw_place(5))
-        for lo in (0, T // 2):
-            gather_first(3, lo, lo + T // 2)
-            gather_second_and_store(3, lo, lo + T // 2, raw_place(5) + PIECE)
+        for lo, hi in ((0, LAST_CUT), (LAST_CUT, T)):
+            gather_first(3, lo, hi)
+            gather_second_and_store(3, lo, hi, raw_place(5) + PIECE)

@@ -13,7 +13,7 @@ HALF = S // 2
 FRONT = K // 2
 PER_COL = 16
 TAIL = 8
-SHARE = {1: 384, 4: 384, 6: 320}
+SHARE = {1: 256, 4: 256}
 LAST_CUT = T - P
 
 KIB = 1024

@@ -247,7 +247,7 @@ def tile_moe_bdx_lin_none_kernel(tc, dyT, w, gate, offs, pos1, pos2, out):
         quantise("w2", "fresh")
 
         new_woven("g1", S, raw_place(2))
-        new_woven("w34", 2 * K, RING + 2 * WIDE)
+        new_woven("w34", 2 * K, RING)
         weave_gated(1, 0)
         weave(on_g, "w34", 0, raw[3][:])
         weave(on_g, "w34", K, front(4))
@@ -273,13 +273,19 @@ def tile_moe_bdx_lin_none_kernel(tc, dyT, w, gate, offs, pos1, pos2, out):
                 multiply(e * NPASS + u, name, u * P, (kt,))
 
         new_woven("g2", S, raw_place(4))
-        new_woven("w5", K, RING + 3 * WIDE)
-        new_woven("e2", NPASS * K, RING)
+        new_woven("w5", K, raw_place(2))
+        new_woven("e2", NPASS * K, raw_place(2) + WIDE)
         new_woven("e3", NPASS * K, LATE)
         weave_gated(2, 0)
         weave(on_g, "w5", 0, raw[5][:])
-        for kt in range(2):
-            on_g(*[side[:, 0, :, :, :] for side in by_rows("e2", 0, (kt,), raw[6][:, :, kt * P : (kt + 1) * P])])
+        nc.gpsimd.tensor_scalar(
+            woven["e2"].rearrange("p (t u k r) -> p t u k r", t=K // P, u=NPASS, r=PACK)[:, 0:2, 0, :, :],
+            raw[6][:, :, 0:FRONT].rearrange("p r (t k) -> p t k r", t=2),
+            1.0,
+            0.0,
+            MULT,
+            ADD,
+        )
         on_s(*by_rows("e2", 0, (2, 3), raw[6][:, :, FRONT:K]))
         for i in (7, 8):
             on_s(*by_rows("e2", i - 6, ALL, raw[i][:]))

@@ -82,7 +82,7 @@ def tile_moe_bdx_lin_none_kernel(tc, dyT, w, gate, offs, pos1, pos2, out):
         raw = {i: place(f"raw{i}", [P, PACK, K], F32, raw_place(i)) for i in range(9)}
         raw_half = {(i, f): place(f"raw{i}_{f}", [P, PACK, FRONT], F32, half_place(i, f))[:] for f in range(2) for i in (9, 10, 11)}
         picked = {}
-        spread = [psum.tile([P, HALF], F32, name=f"bank{2 + h}_1") for h in range(2)]
+        spread = [psum.tile([P, HALF], F32, name=f"bank{3 - h}_0") for h in range(2)]
         banks = {}
 
         def load_window(c, r):
@@ -311,8 +311,10 @@ def tile_moe_bdx_lin_none_kernel(tc, dyT, w, gate, offs, pos1, pos2, out):
         finish(3, 0)
         finish(2, 3, half_place(10, 0) + PIECE)
         finish(3, 1)
-        for i in (9, 10, 11):
+        for i in (9, 10):
             on_v(*by_rows("e3", i - 9, (2, 3), raw_half[i, 1]))
+        for kt in (2, 3):
+            on_v(*by_rows("e3", 2, (kt,), raw_half[11, 1][:, :, (kt - 2) * P : (kt - 1) * P]))
         finish(3, 2)
         finish(3, 3)
 

@@ -13,22 +13,20 @@ HALF = S // 2
 FRONT = K // 2
 PER_COL = 16
 TAIL = 8
-SHARE = {1: 256, 4: 256}
 LAST_CUT = T - P
 
 KIB = 1024
-RAW_TILE = 8 * KIB
-WIDE = 4 * KIB
-PIECE = 2 * KIB
-WINDOW_BYTES = 65 * 64
-UNIT = PIECE + 512
+TILE = 8 * KIB
+NARROW = 33 * 64
+BROAD = 65 * 64
 
 WINDOWS = 0
-RAW = WINDOWS + NPASS * PACK * WINDOW_BYTES
-PICKED = RAW + 12 * RAW_TILE
-RING = PICKED + 4 * RAW_TILE
-LATE = RING + 4 * WIDE
-CODES = LATE + 4 * WIDE
+RAW = WINDOWS + PACK * NARROW + 2 * PACK * BROAD
+PARTS = RAW + 6 * TILE
+SPREAD = PARTS + 6 * TILE
+PICKED = SPREAD + 2 * TILE
+WOVEN = PICKED + 4 * TILE
+CODES = WOVEN + 2 * TILE
 
 F32 = mybir.dt.float32
 BF16 = mybir.dt.bfloat16
@@ -54,11 +52,11 @@ def tile_moe_bdx_lin_none_kernel(tc, dyT, w, gate, offs, pos1, pos2, out):
         def place(name, shape, dtype, at):
             return placed.tile(shape, dtype, name=name, offset=at, align_bytes=64)
 
-        def raw_place(i):
-            return RAW + i * RAW_TILE
+        def window_at(c, r):
+            return WINDOWS + (r * NARROW if c == 0 else PACK * NARROW + ((c - 1) * PACK + r) * BROAD)
 
-        def half_place(i, f):
-            return raw_place(9) + (3 * f + i - 9) * WIDE
+        def raw_at(i):
+            return RAW + (i ^ 1) * TILE
 
         offs_sb = held.tile([P, S // PER_COL], U16, name="offs_sb")
         pos1_sb = held.tile([P, T // PER_COL], U16, name="pos1_sb")
@@ -71,7 +69,7 @@ def tile_moe_bdx_lin_none_kernel(tc, dyT, w, gate, offs, pos1, pos2, out):
         for c in range(NPASS):
             for r in range(PACK):
                 width = (HALF if c == 0 else S) + TAIL
-                windows[c, r] = place(f"window{c}_{r}", [P, width], F32, WINDOWS + (c * PACK + r) * WINDOW_BYTES)
+                windows[c, r] = place(f"window{c}_{r}", [P, width], F32, window_at(c, r))
                 if c == NPASS - 1:
                     nc.gpsimd.memset(windows[c, r][:, T:], 0.0)
                 elif (c, r) == (1, PACK - 1):
@@ -79,31 +77,29 @@ def tile_moe_bdx_lin_none_kernel(tc, dyT, w, gate, offs, pos1, pos2, out):
                 else:
                     nc.vector.memset(windows[c, r][:, T:], 0.0)
 
-        raw = {i: place(f"raw{i}", [P, PACK, K], F32, raw_place(i)) for i in range(9)}
-        raw_half = {(i, f): place(f"raw{i}_{f}", [P, PACK, FRONT], F32, half_place(i, f))[:] for f in range(2) for i in (9, 10, 11)}
-        picked = {}
-        spread = [psum.tile([P, HALF], F32, name=f"bank{3 - h}_0") for h in range(2)]
+        raw, raw_place = {}, {}
+        spread = [psum.tile([P, HALF], F32, name=f"bank{3 - h}_1") for h in range(2)]
         banks = {}
 
         def load_window(c, r):
             rows = dyT[c * PASS : (c + 1) * PASS, :].rearrange("(p r) t -> p r t", r=PACK)
             nc.sync.dma_start(windows[c, r][:, 0:T], rows[:, r, :])
 
-        def weight_rows(i):
+        def load(i, lo, hi, at, pitch=None):
             e, c = divmod(i, NPASS)
-            return w[e, c * PASS : (c + 1) * PASS, :].rearrange("(p r) k -> p r k", r=PACK)
-
-        def load_whole(i):
-            nc.sync.dma_start(raw[i][:], weight_rows(i))
-
-        def load_half(i, f):
-            nc.sync.dma_start(raw_half[i, f], weight_rows(i)[:, :, f * FRONT : (f + 1) * FRONT])
+            rows = w[e, c * PASS : (c + 1) * PASS, :].rearrange("(p r) k -> p r k", r=PACK)
+            width = (hi - lo) * P
+            tile = place(f"raw{i}_{lo}", [P, PACK, pitch or width], F32, at)
+            raw[i, lo] = tile[:, :, 0:width]
+            raw_place[i, lo] = at
+            nc.sync.dma_start(raw[i, lo], rows[:, :, lo * P : hi * P])
 
         def on_g(dst, src):
-            nc.gpsimd.tensor_scalar(dst.rearrange("p x r i -> p x i r"), src.rearrange("p x r i -> p x i r"), 1.0, 0.0, MULT, ADD)
+            order = "p t x r i -> p t (x i) r"
+            nc.gpsimd.tensor_scalar(dst.rearrange(order), src.rearrange(order), 1.0, 0.0, MULT, ADD)
 
-        woven, mx = {}, {}
-        count = {"fresh": 0, "windows": 0}
+        on_v, on_s = nc.vector.tensor_copy, nc.scalar.copy
+        woven, mx, picked = {}, {}, {}
 
         def entries(lst, lo, hi):
             return lst[:, lo // PER_COL : hi // PER_COL]
@@ -111,68 +107,79 @@ def tile_moe_bdx_lin_none_kernel(tc, dyT, w, gate, offs, pos1, pos2, out):
         def new_woven(name, words, at):
             woven[name] = place(f"woven_{name}", [P, PACK * words], BF16, at)[:]
 
-        def part(name, lo, words):
-            return woven[name][:, PACK * lo : PACK * (lo + words)].rearrange("p (x i r) -> p x r i", i=2, r=PACK)
-
-        def pairs(src):
-            return src.rearrange("p r (x i) -> p x r i", i=2)
-
-        def weave(copy, name, lo, src):
-            copy(part(name, lo, src.shape[2]), pairs(src))
-
         def weave_gated(c, h):
+            dst = woven[f"g{c}"][:, h * PACK * HALF : (h + 1) * PACK * HALF].rearrange("p (x i r) -> p x r i", i=2, r=PACK)
+            src = picked[c][:, :, h * HALF : (h + 1) * HALF].rearrange("p r (x i) -> p x r i", i=2)
             weights = spread[h][:].rearrange("p (x i) -> p x i", i=2).unsqueeze(2).to_broadcast([P, HALF // 2, PACK, 2])
-            nc.vector.tensor_tensor(part(f"g{c}", h * HALF, HALF), pairs(picked[c, h]), weights, MULT)
+            nc.vector.tensor_tensor(dst, src, weights, MULT)
 
-        def quantise(name, kind="windows", at=None):
-            words = woven[name].shape[1] // PACK
-            if at is None:
-                at = {"fresh": CODES, "windows": WINDOWS}[kind] + count[kind]
-                count[kind] = count[kind] + 5 * words
+        def weave(copy, name, tiles, u, key, lo, hi):
+            dst = woven[name].rearrange("p (t u x i r) -> p t u x r i", t=K // P, u=tiles, i=2, r=PACK)[:, lo:hi, u, :, :, :]
+            src = raw[key][:, :, (lo - key[1]) * P : (hi - key[1]) * P].rearrange("p r (t x i) -> p t x r i", t=hi - lo, i=2)
+            copy(dst, src)
+
+        def quantise(name, values, at, scales_at=None):
+            words = values.shape[1] // PACK
             codes = place(f"codes_{name}", [P, words], U32, at)
-            scales = place(f"scales_{name}", [P, words], U8, at + 4 * words)
-            nc.vector.quantize_mx(out=codes[:].bitcast(FP8X4), scales=scales[:], in_=woven[name])
+            scales = place(f"scales_{name}", [P, words], U8, at + 4 * words if scales_at is None else scales_at)
+            nc.vector.quantize_mx(out=codes[:].bitcast(FP8X4), scales=scales[:], in_=values)
             mx[name] = codes, scales
 
-        def multiply(i, name, lo, kts):
+        def multiply(i, kt, name, lo):
             e, c = divmod(i, NPASS)
             h, u = divmod(e, 2)
-            slots = slice(e * C, (e + 1) * C)
             w_codes, w_scales = mx[name]
-            g_codes, g_scales = mx[f"g{c}"]
             if c == NPASS - 1:
                 g_codes, g_scales = mx[f"g{c}_{h}"]
                 slots = slice(u * C, (u + 1) * C)
-            for at, kt in enumerate(kts):
-                cols = slice(lo + at * P, lo + (at + 1) * P)
-                if (kt, h) not in banks:
-                    banks[kt, h] = psum.tile([P, HALF], F32, name=f"bank{kt}_{h}")
-                nc.tensor.matmul_mx(
-                    out=banks[kt, h][:, u * C : (u + 1) * C],
-                    lhsT=w_codes[:, cols].bitcast(FP8X4),
-                    lhsT_scale=w_scales[:, cols],
-                    rhs=g_codes[:, slots].bitcast(FP8X4),
-                    rhs_scale=g_scales[:, slots],
-                    start=(u == 0 and c == 0),
-                    stop=(u == 1 and c == NPASS - 1),
-                )
+            else:
+                g_codes, g_scales = mx[f"g{c}"]
+                slots = slice(e * C, (e + 1) * C)
+            opens = (kt, h) not in banks
+            if opens:
+                banks[kt, h] = psum.tile([P, HALF], F32, name=f"bank{kt}_{h}")
+            nc.tensor.matmul_mx(
+                out=banks[kt, h][:, u * C : (u + 1) * C],
+                lhsT=w_codes[:, lo : lo + P].bitcast(FP8X4),
+                lhsT_scale=w_scales[:, lo : lo + P],
+                rhs=g_codes[:, slots].bitcast(FP8X4),
+                rhs_scale=g_scales[:, slots],
+                start=opens,
+                stop=(u == 1 and c == NPASS - 1),
+            )
 
-        dx = {}
-        first = {}
+        def multiply_pair(i, name):
+            for kt in range(K // P):
+                multiply(i, kt, name, (2 * kt + i % 2) * P)
+
+        def finish(e, kt, at):
+            words = NPASS * P
+            quantise(f"e{e}_{kt}", woven[f"e{e}"][:, kt * PACK * words : (kt + 1) * PACK * words], at)
+            for u in range(NPASS):
+                multiply(e * NPASS + u, kt, f"e{e}_{kt}", u * P)
+
+        dx, first = {}, {}
 
         def empty(kt, h, copy=nc.scalar.copy):
             if h == 0:
-                dx[kt] = place(f"dx{kt}", [P, S], F32, raw_place(0) + kt * WIDE)
+                dx[kt] = place(f"dx{kt}", [P, S], F32, SPREAD + kt * 4 * KIB)
             copy(dx[kt][:, h * HALF : (h + 1) * HALF], banks[kt, h][:])
 
-        def gather_first(kt, lo, hi):
-            first[kt, lo] = place(f"first{kt}_{lo}", [P, hi - lo], F32, raw_place(3) + kt * PIECE + 4 * lo)
+        def gather_first(kt, lo, hi, at):
+            first[kt, lo] = place(f"first{kt}_{lo}", [P, hi - lo], F32, at + 4 * lo)
             nc.scalar.activation(first[kt, lo][:], dx[kt][:].indirect(entries(pos1_sb, lo, hi)), COPY)
 
         def gather_second_and_store(kt, lo, hi, at):
             total = place(f"total{kt}_{lo}", [P, hi - lo], F32, at + 4 * lo)
             nc.vector.tensor_tensor(total[:], dx[kt][:].indirect(entries(pos2_sb, lo, hi)), first[kt, lo][:], ADD)
             nc.sync.dma_start(out[kt * P : (kt + 1) * P, lo:hi], total[:])
+
+        def gather(on_vector, c, r, lo, hi):
+            src = windows[c, r][:].indirect(entries(offs_sb, lo, hi))
+            if on_vector:
+                nc.vector.tensor_copy(picked[c][:, r, lo:hi], src)
+            else:
+                nc.scalar.activation(picked[c][:, r, lo:hi], src, COPY)
 
         load_window(0, 0)
         nc.sync.dma_start(offs_sb[:], offs)
@@ -181,153 +188,124 @@ def tile_moe_bdx_lin_none_kernel(tc, dyT, w, gate, offs, pos1, pos2, out):
         load_window(0, 2)
         load_window(0, 3)
         load_window(1, 0)
-        load_whole(0)
+        load(0, 0, 4, raw_at(0))
         load_window(1, 1)
-        load_whole(1)
+        load(1, 0, 4, raw_at(1))
         load_window(1, 2)
         load_window(1, 3)
-        load_whole(2)
+        load(2, 0, 4, raw_at(2))
         load_window(2, 0)
-        load_whole(3)
         load_window(2, 1)
-        load_whole(4)
+        load(3, 0, 4, raw_at(3))
         load_window(2, 2)
         load_window(2, 3)
-        for i in range(5, 9):
-            load_whole(i)
-        for i in range(9, 12):
-            load_half(i, 0)
+        load(4, 0, 4, raw_at(4))
+        load(5, 0, 4, raw_at(5))
+        for i in range(6, 12):
+            if i == 11:
+                load(i, 0, 2, SPREAD, pitch=S)
+            else:
+                load(i, 0, 2, PARTS + (i - 6) * TILE // 2)
         nc.sync.dma_start(pos1_sb[:], pos1)
         nc.sync.dma_start(pos2_sb[:], pos2)
-        for i in range(9, 12):
-            load_half(i, 1)
+        for i in range(6, 9):
+            load(i, 2, 4, PARTS + i * TILE // 2)
+        for kt in (2, 3):
+            for i in range(9, 12):
+                load(i, kt, kt + 1, PARTS + 9 * TILE // 2 + (3 * (kt - 2) + i - 9) * TILE // 4)
 
         for h in range(2):
             for j in range(PACK):
                 nc.tensor.transpose(spread[h][:, j::PACK], gate_sb[:, h, j : j + 1].to_broadcast([P, P]), identity[:])
 
-        for h in range(2):
-            picked[0, h] = place(f"picked0_{h}", [P, PACK, HALF], F32, PICKED + h * RAW_TILE)[:]
+        picked[0] = place("picked0", [P, PACK, S], F32, PICKED)[:]
+        picked[1] = place("picked1", [P, PACK, S], F32, PICKED + 2 * TILE)[:]
         for r in range(PACK):
-            nc.vector.tensor_copy(picked[0, 0][:, r, :], windows[0, r][:].indirect(entries(offs_sb, 0, HALF)))
-            nc.scalar.activation(picked[0, 1][:, r, :], windows[0, r][:].indirect(entries(offs_sb, HALF, S)), COPY)
+            gather(True, 0, r, 0, HALF)
+            gather(False, 0, r, HALF, S)
+        gather(False, 1, 0, 0, S)
+        gather(False, 1, 1, 0, S)
+        gather(False, 1, 2, HALF, S)
+        gather(False, 1, 3, 0, S)
 
-        def gather_pass(c, at):
-            whole = place(f"picked{c}", [P, PACK, S], F32, at)
-            for r in range(PACK):
-                cuts = ((0, HALF), (HALF + C, S)) if (c, r) == (NPASS - 1, PACK - 1) else ((0, S),)
-                for lo, hi in cuts:
-                    nc.scalar.activation(whole[:, r, lo:hi], windows[c, r][:].indirect(entries(offs_sb, lo, hi)), COPY)
-            for h in range(2):
-                picked[c, h] = whole[:, :, h * HALF : (h + 1) * HALF]
-
-        gather_pass(1, PICKED + 2 * RAW_TILE)
-        on_v, on_s = nc.vector.tensor_copy, nc.scalar.copy
-        ALL = range(4)
-
-        def front(i):
-            return raw[i][:, :, 0 : SHARE[i]]
-
-        def back(i):
-            return raw[i][:, :, SHARE[i] : K]
-
-        new_woven("g0", S, LATE)
-        new_woven("w01", 2 * K, RING)
+        new_woven("g0", S, WOVEN)
+        new_woven("w01", 2 * K, WOVEN + TILE)
         weave_gated(0, 1)
-        weave(on_g, "w01", 0, raw[0][:])
-        weave(on_g, "w01", K, front(1))
+        weave(on_g, "w01", 2, 0, (0, 0), 0, 4)
+        weave(on_g, "w01", 2, 1, (1, 0), 0, 4)
         weave_gated(0, 0)
-        gather_pass(2, PICKED)
-        weave(on_v, "w01", K + SHARE[1], back(1))
-        quantise("g0", "fresh")
-        new_woven("w2", K, RING + 2 * WIDE)
-        weave(on_v, "w2", 0, raw[2][:])
-        quantise("w01", "fresh")
-        multiply(0, "w01", 0, ALL)
-        quantise("w2", "fresh")
+        gather(True, 1, 2, 0, HALF)
+        picked[2] = place("picked2", [P, PACK, S], F32, PICKED)[:]
+        gather(False, 2, 0, 0, S)
+        gather(False, 2, 1, 0, S)
+        gather(False, 2, 2, HALF, S)
+        gather(False, 2, 3, 0, S)
+        quantise("g0", woven["g0"], raw_at(1), window_at(1, 2))
+        quantise("w01", woven["w01"], CODES)
+        multiply_pair(0, "w01")
 
-        new_woven("g1", S, raw_place(2))
-        new_woven("w34", 2 * K, RING)
+        new_woven("g1", S, raw_at(1) + TILE // 2)
+        new_woven("w23", 2 * K, WOVEN)
         weave_gated(1, 0)
-        weave(on_g, "w34", 0, raw[3][:])
-        weave(on_g, "w34", K, front(4))
+        weave(on_g, "w23", 2, 0, (2, 0), 0, 4)
+        weave(on_g, "w23", 2, 1, (3, 0), 0, 4)
         weave_gated(1, 1)
-        nc.vector.tensor_copy(picked[2, 1][:, PACK - 1, 0:C], windows[2, PACK - 1][:].indirect(entries(offs_sb, HALF, HALF + C)))
-        weave(on_v, "w34", K + SHARE[4], back(4))
-        quantise("g1", "fresh")
-        multiply(1, "w01", K, ALL)
-        quantise("w34", "fresh")
-        multiply(3, "w34", 0, ALL)
-        multiply(4, "w34", K, ALL)
+        gather(True, 2, 2, 0, HALF)
+        quantise("g1", woven["g1"], raw_at(3), window_at(2, 2))
+        multiply_pair(1, "w01")
+        quantise("w23", woven["w23"], CODES + 5 * KIB)
+        multiply_pair(3, "w23")
 
-        def by_rows(name, u, kts, src):
-            tiles = woven[name].rearrange("p (t u x i r) -> p t u x r i", t=K // P, u=NPASS, i=2, r=PACK)
-            return tiles[:, kts[0] : kts[-1] + 1, u, :, :, :], src.rearrange("p r (t x i) -> p t x r i", t=len(kts), i=2)
-
-        def finish(e, kt, at=None):
-            words = NPASS * P
-            name = f"e{e}_{kt}"
-            woven[name] = woven[f"e{e}"][:, kt * PACK * words : (kt + 1) * PACK * words]
-            quantise(name, at=at)
-            for u in range(NPASS):
-                multiply(e * NPASS + u, name, u * P, (kt,))
-
-        new_woven("g2", S, raw_place(4))
-        new_woven("w5", K, raw_place(2))
-        new_woven("e2", NPASS * K, raw_place(2) + WIDE)
-        new_woven("e3", NPASS * K, LATE)
+        new_woven("g2", S, raw_at(3) + TILE // 2)
+        new_woven("w45", 2 * K, raw_at(1) + TILE // 2)
+        new_woven("e2", NPASS * K, WOVEN + TILE)
         weave_gated(2, 0)
-        weave(on_g, "w5", 0, raw[5][:])
-        nc.gpsimd.tensor_scalar(
-            woven["e2"].rearrange("p (t u k r) -> p t u k r", t=K // P, u=NPASS, r=PACK)[:, 0:2, 0, :, :],
-            raw[6][:, :, 0:FRONT].rearrange("p r (t k) -> p t k r", t=2),
-            1.0,
-            0.0,
-            MULT,
-            ADD,
-        )
-        on_s(*by_rows("e2", 0, (2, 3), raw[6][:, :, FRONT:K]))
-        for i in (7, 8):
-            on_s(*by_rows("e2", i - 6, ALL, raw[i][:]))
-        for i in (9, 10):
-            on_s(*by_rows("e3", i - 9, (0, 1), raw_half[i, 0]))
+        weave(on_g, "w45", 2, 0, (4, 0), 0, 4)
+        weave(on_g, "w45", 2, 1, (5, 0), 0, 2)
+        weave(on_s, "w45", 2, 1, (5, 0), 2, 4)
         weave_gated(2, 1)
-        quantise("w5")
-        for h in range(2):
-            woven[f"g2_{h}"] = woven["g2"][:, h * PACK * HALF : (h + 1) * PACK * HALF]
-        mx["g2"] = mx["g1"]
-        quantise("g2_0", at=raw_place(7))
-        for kt in ALL:
-            multiply(2, "w2", kt * P, (kt,))
-            multiply(5, "w5", kt * P, (kt,))
-        quantise("g2_1", at=raw_place(7) + WIDE)
-        finish(2, 0)
-        finish(2, 1)
-        for kt in ALL:
+        new_woven("e3", NPASS * K, PICKED + 2 * TILE)
+        for i in (6, 7, 8):
+            weave(on_s, "e2", NPASS, i - 6, (i, 0), 0, 2)
+        for i in (9, 10, 11):
+            weave(on_s, "e3", NPASS, i - 9, (i, 0), 0, 2)
+        quantise("w45", woven["w45"], CODES + 10 * KIB)
+        multiply_pair(4, "w45")
+        quantise("g2_0", woven["g2"][:, 0 : PACK * HALF], raw_at(5))
+        for kt in range(4):
+            multiply(2, kt, "w23", 2 * kt * P)
+            multiply(5, kt, "w45", (2 * kt + 1) * P)
+        quantise("g2_1", woven["g2"][:, PACK * HALF :], raw_at(5) + TILE // 2)
+        spare = raw_at(4)
+        finish(2, 0, spare)
+        finish(2, 1, spare + 2 * KIB)
+        for kt in range(4):
             empty(kt, 0)
-
-        on_v(*by_rows("e3", 2, (0, 1), raw_half[11, 0]))
-        finish(2, 2, half_place(10, 0))
-        finish(3, 0)
-        finish(2, 3, half_place(10, 0) + PIECE)
-        finish(3, 1)
-        for i in (9, 10):
-            on_v(*by_rows("e3", i - 9, (2, 3), raw_half[i, 1]))
-        for kt in (2, 3):
-            on_v(*by_rows("e3", 2, (kt,), raw_half[11, 1][:, :, (kt - 2) * P : (kt - 1) * P]))
-        finish(3, 2)
-        finish(3, 3)
-
+        weave(on_v, "e2", NPASS, 0, (6, 2), 2, 4)
+        finish(3, 0, spare + 4 * KIB)
+        finish(3, 1, spare + 6 * KIB)
         empty(0, 1)
-        gather_first(0, 0, T)
         empty(1, 1)
-        gather_first(1, 0, T)
-        gather_second_and_store(0, 0, T, half_place(11, 1))
+        for i in (7, 8):
+            weave(on_v, "e2", NPASS, i - 6, (i, 2), 2, 4)
+        weave(on_v, "e3", NPASS, 0, (9, 2), 2, 3)
+        gather_first(0, 0, T, raw_place[6, 0])
+        gather_first(1, 0, T, raw_place[6, 0] + 2 * KIB)
+        finish(2, 2, raw_place[7, 0])
+        weave(on_v, "e3", NPASS, 1, (10, 2), 2, 3)
+        finish(2, 3, raw_place[7, 0] + 2 * KIB)
+        weave(on_v, "e3", NPASS, 2, (11, 2), 2, 3)
+        for i in (9, 10):
+            weave(on_s, "e3", NPASS, i - 9, (i, 3), 3, 4)
+        finish(3, 2, raw_place[8, 0])
+        gather_second_and_store(0, 0, T, raw_place[11, 2])
+        weave(on_v, "e3", NPASS, 2, (11, 3), 3, 4)
+        finish(3, 3, raw_place[8, 0] + 2 * KIB)
+        gather_second_and_store(1, 0, T, raw_place[11, 3] - KIB)
         empty(2, 1)
-        gather_second_and_store(1, 0, T, half_place(11, 1) + PIECE)
-        empty(3, 1, on_v)
-        gather_first(2, 0, T)
-        gather_second_and_store(2, 0, T, raw_place(5))
-        for lo, hi in ((0, LAST_CUT), (LAST_CUT, T)):
-            gather_first(3, lo, hi)
-            gather_second_and_store(3, lo, hi, raw_place(5) + PIECE)
+        gather_first(2, 0, T, raw_place[9, 0])
+        empty(3, 1)
+        gather_second_and_store(2, 0, T, PICKED + 2 * TILE)
+        for lo, hi in ((0, T // 2), (T // 2, T)):
+            gather_first(3, lo, hi, raw_place[10, 0])
+            gather_second_and_store(3, lo, hi, raw_place[10, 0] + 2 * KIB)

@@ -13,7 +13,7 @@ HALF = S // 2
 FRONT = K // 2
 PER_COL = 16
 TAIL = 8
-LAST_CUT = T - P
+LAST_CUT = T // 2
 
 KIB = 1024
 TILE = 8 * KIB
@@ -22,11 +22,11 @@ BROAD = 65 * 64
 
 WINDOWS = 0
 RAW = WINDOWS + PACK * NARROW + 2 * PACK * BROAD
-PARTS = RAW + 6 * TILE
-SPREAD = PARTS + 6 * TILE
-PICKED = SPREAD + 2 * TILE
+WIDE = RAW + 12 * TILE
+PICKED = WIDE + 2 * TILE
 WOVEN = PICKED + 4 * TILE
-CODES = WOVEN + 2 * TILE
+RING = WOVEN + TILE + KIB
+CODES = RING + 2 * TILE
 
 F32 = mybir.dt.float32
 BF16 = mybir.dt.bfloat16
@@ -56,7 +56,7 @@ def tile_moe_bdx_lin_none_kernel(tc, dyT, w, gate, offs, pos1, pos2, out):
             return WINDOWS + (r * NARROW if c == 0 else PACK * NARROW + ((c - 1) * PACK + r) * BROAD)
 
         def raw_at(i):
-            return RAW + (i ^ 1) * TILE
+            return RAW + i * TILE
 
         offs_sb = held.tile([P, S // PER_COL], U16, name="offs_sb")
         pos1_sb = held.tile([P, T // PER_COL], U16, name="pos1_sb")
@@ -95,6 +95,9 @@ def tile_moe_bdx_lin_none_kernel(tc, dyT, w, gate, offs, pos1, pos2, out):
             nc.sync.dma_start(raw[i, lo], rows[:, :, lo * P : hi * P])
 
         def on_g(dst, src):
+            nc.gpsimd.tensor_scalar(dst.rearrange("p x r i -> p x i r"), src.rearrange("p x r i -> p x i r"), 1.0, 0.0, MULT, ADD)
+
+        def on_g_rows(dst, src):
             order = "p t x r i -> p t (x i) r"
             nc.gpsimd.tensor_scalar(dst.rearrange(order), src.rearrange(order), 1.0, 0.0, MULT, ADD)
 
@@ -113,10 +116,14 @@ def tile_moe_bdx_lin_none_kernel(tc, dyT, w, gate, offs, pos1, pos2, out):
             weights = spread[h][:].rearrange("p (x i) -> p x i", i=2).unsqueeze(2).to_broadcast([P, HALF // 2, PACK, 2])
             nc.vector.tensor_tensor(dst, src, weights, MULT)
 
-        def weave(copy, name, tiles, u, key, lo, hi):
-            dst = woven[name].rearrange("p (t u x i r) -> p t u x r i", t=K // P, u=tiles, i=2, r=PACK)[:, lo:hi, u, :, :, :]
+        def weave(copy, name, at, key, lo, hi):
+            dst = woven[name][:, PACK * at : PACK * (at + hi - lo)].rearrange("p (x i r) -> p x r i", i=2, r=PACK)
+            copy(dst, raw[key][:, :, lo:hi].rearrange("p r (x i) -> p x r i", i=2))
+
+        def weave_rows(copy, i, key, lo, hi):
+            dst = woven[f"e{i // NPASS}"].rearrange("p (t u x i r) -> p t u x r i", t=K // P, u=NPASS, i=2, r=PACK)
             src = raw[key][:, :, (lo - key[1]) * P : (hi - key[1]) * P].rearrange("p r (t x i) -> p t x r i", t=hi - lo, i=2)
-            copy(dst, src)
+            copy(dst[:, lo:hi, i % NPASS, :, :, :], src)
 
         def quantise(name, values, at, scales_at=None):
             words = values.shape[1] // PACK
@@ -148,21 +155,21 @@ def tile_moe_bdx_lin_none_kernel(tc, dyT, w, gate, offs, pos1, pos2, out):
                 stop=(u == 1 and c == NPASS - 1),
             )
 
-        def multiply_pair(i, name):
+        def multiply_all(i, name, lo):
             for kt in range(K // P):
-                multiply(i, kt, name, (2 * kt + i % 2) * P)
+                multiply(i, kt, name, lo + kt * P)
 
-        def finish(e, kt, at):
-            words = NPASS * P
-            quantise(f"e{e}_{kt}", woven[f"e{e}"][:, kt * PACK * words : (kt + 1) * PACK * words], at)
-            for u in range(NPASS):
-                multiply(e * NPASS + u, kt, f"e{e}_{kt}", u * P)
+        def finish(e, kt, at, lo=0, hi=NPASS):
+            name = f"e{e}_{kt}_{lo}"
+            quantise(name, woven[f"e{e}"][:, (kt * NPASS + lo) * PASS : (kt * NPASS + hi) * PASS], at)
+            for u in range(lo, hi):
+                multiply(e * NPASS + u, kt, name, (u - lo) * P)
 
         dx, first = {}, {}
 
         def empty(kt, h, copy=nc.scalar.copy):
             if h == 0:
-                dx[kt] = place(f"dx{kt}", [P, S], F32, SPREAD + kt * 4 * KIB)
+                dx[kt] = place(f"dx{kt}", [P, S], F32, WIDE + kt * TILE // 2)
             copy(dx[kt][:, h * HALF : (h + 1) * HALF], banks[kt, h][:])
 
         def gather_first(kt, lo, hi, at):
@@ -195,117 +202,123 @@ def tile_moe_bdx_lin_none_kernel(tc, dyT, w, gate, offs, pos1, pos2, out):
         load_window(1, 3)
         load(2, 0, 4, raw_at(2))
         load_window(2, 0)
-        load_window(2, 1)
         load(3, 0, 4, raw_at(3))
+        load_window(2, 1)
+        load(4, 0, 4, raw_at(4))
         load_window(2, 2)
         load_window(2, 3)
-        load(4, 0, 4, raw_at(4))
-        load(5, 0, 4, raw_at(5))
-        for i in range(6, 12):
-            if i == 11:
-                load(i, 0, 2, SPREAD, pitch=S)
-            else:
-                load(i, 0, 2, PARTS + (i - 6) * TILE // 2)
+        for i in range(5, 9):
+            load(i, 0, 4, raw_at(i))
+        load(9, 0, 2, raw_at(9))
+        load(10, 0, 2, WIDE, pitch=S)
+        load(11, 0, 2, raw_at(11))
         nc.sync.dma_start(pos1_sb[:], pos1)
+        for i in range(9, 12):
+            load(i, 2, 4, raw_at(i) + TILE // 2)
         nc.sync.dma_start(pos2_sb[:], pos2)
-        for i in range(6, 9):
-            load(i, 2, 4, PARTS + i * TILE // 2)
-        for kt in (2, 3):
-            for i in range(9, 12):
-                load(i, kt, kt + 1, PARTS + 9 * TILE // 2 + (3 * (kt - 2) + i - 9) * TILE // 4)
 
         for h in range(2):
             for j in range(PACK):
                 nc.tensor.transpose(spread[h][:, j::PACK], gate_sb[:, h, j : j + 1].to_broadcast([P, P]), identity[:])
 
-        picked[0] = place("picked0", [P, PACK, S], F32, PICKED)[:]
-        picked[1] = place("picked1", [P, PACK, S], F32, PICKED + 2 * TILE)[:]
+        picked[0] = place("picked0", [P, PACK, S], F32, PICKED + 2 * TILE)[:]
+        picked[1] = place("picked1", [P, PACK, S], F32, PICKED)[:]
         for r in range(PACK):
             gather(True, 0, r, 0, HALF)
             gather(False, 0, r, HALF, S)
-        gather(False, 1, 0, 0, S)
-        gather(False, 1, 1, 0, S)
-        gather(False, 1, 2, HALF, S)
-        gather(False, 1, 3, 0, S)
+        for r in range(PACK - 1):
+            gather(False, 1, r, 0, S)
+        gather(False, 1, PACK - 1, 0, HALF)
+        gather(False, 1, PACK - 1, HALF, S)
 
         new_woven("g0", S, WOVEN)
-        new_woven("w01", 2 * K, WOVEN + TILE)
+        new_woven("w01", 2 * K, RING)
+        new_woven("w2", K, RING + TILE)
         weave_gated(0, 1)
-        weave(on_g, "w01", 2, 0, (0, 0), 0, 4)
-        weave(on_g, "w01", 2, 1, (1, 0), 0, 4)
+        weave(on_g, "w01", 0, (0, 0), 0, K)
+        weave(on_g, "w01", K, (1, 0), 0, FRONT)
         weave_gated(0, 0)
-        gather(True, 1, 2, 0, HALF)
-        picked[2] = place("picked2", [P, PACK, S], F32, PICKED)[:]
-        gather(False, 2, 0, 0, S)
-        gather(False, 2, 1, 0, S)
-        gather(False, 2, 2, HALF, S)
-        gather(False, 2, 3, 0, S)
-        quantise("g0", woven["g0"], raw_at(1), window_at(1, 2))
-        quantise("w01", woven["w01"], CODES)
-        multiply_pair(0, "w01")
+        picked[2] = place("picked2", [P, PACK, S], F32, PICKED + 2 * TILE)[:]
+        for r in range(PACK - 1):
+            gather(False, 2, r, 0, S)
+        gather(False, 2, PACK - 1, C, HALF)
+        gather(False, 2, PACK - 1, HALF, S)
+        weave(on_v, "w01", K + FRONT, (1, 0), FRONT, K)
+        quantise("g0", woven["g0"], CODES)
+        weave(on_v, "w2", 0, (2, 0), 0, K)
+        quantise("w01", woven["w01"], CODES + 5 * KIB)
+        multiply_all(0, "w01", 0)
 
         new_woven("g1", S, raw_at(1) + TILE // 2)
-        new_woven("w23", 2 * K, WOVEN)
+        new_woven("w34", 2 * K, RING)
         weave_gated(1, 0)
-        weave(on_g, "w23", 2, 0, (2, 0), 0, 4)
-        weave(on_g, "w23", 2, 1, (3, 0), 0, 4)
+        weave(on_g, "w34", 0, (3, 0), 0, K)
+        weave(on_g, "w34", K, (4, 0), 0, FRONT)
         weave_gated(1, 1)
-        gather(True, 2, 2, 0, HALF)
-        quantise("g1", woven["g1"], raw_at(3), window_at(2, 2))
-        multiply_pair(1, "w01")
-        quantise("w23", woven["w23"], CODES + 5 * KIB)
-        multiply_pair(3, "w23")
+        quantise("w2", woven["w2"], raw_at(3) + 5 * KIB)
+        quantise("g1", woven["g1"], raw_at(3))
+        weave(on_v, "w34", K + FRONT, (4, 0), FRONT, K)
+        gather(True, 2, PACK - 1, 0, C)
+        multiply_all(1, "w01", K)
+        quantise("w34", woven["w34"], CODES + 10 * KIB)
+        multiply_all(3, "w34", 0)
+        multiply_all(4, "w34", K)
 
-        new_woven("g2", S, raw_at(3) + TILE // 2)
-        new_woven("w45", 2 * K, raw_at(1) + TILE // 2)
-        new_woven("e2", NPASS * K, WOVEN + TILE)
+        new_woven("g2", S, raw_at(4))
+        new_woven("w5", K, RING - 3 * KIB)
+        new_woven("e2", NPASS * K, RING + KIB)
+        new_woven("e3", NPASS * K, PICKED)
         weave_gated(2, 0)
-        weave(on_g, "w45", 2, 0, (4, 0), 0, 4)
-        weave(on_g, "w45", 2, 1, (5, 0), 0, 2)
-        weave(on_s, "w45", 2, 1, (5, 0), 2, 4)
+        weave(on_g, "w5", 0, (5, 0), 0, K)
+        weave_rows(on_g_rows, 6, (6, 0), 0, 2)
+        weave_rows(on_s, 6, (6, 0), 2, 4)
+        weave_rows(on_s, 7, (7, 0), 0, 4)
+        weave_rows(on_s, 8, (8, 0), 0, 4)
+        weave_rows(on_s, 10, (10, 0), 0, 2)
         weave_gated(2, 1)
-        new_woven("e3", NPASS * K, PICKED + 2 * TILE)
-        for i in (6, 7, 8):
-            weave(on_s, "e2", NPASS, i - 6, (i, 0), 0, 2)
-        for i in (9, 10, 11):
-            weave(on_s, "e3", NPASS, i - 9, (i, 0), 0, 2)
-        quantise("w45", woven["w45"], CODES + 10 * KIB)
-        multiply_pair(4, "w45")
-        quantise("g2_0", woven["g2"][:, 0 : PACK * HALF], raw_at(5))
+        quantise("w5", woven["w5"], raw_at(5), raw_at(6))
+        quantise("g2_0", woven["g2"][:, 0 : PACK * HALF], raw_at(5) + 2 * KIB, raw_at(6) + 512)
         for kt in range(4):
-            multiply(2, kt, "w23", 2 * kt * P)
-            multiply(5, kt, "w45", (2 * kt + 1) * P)
-        quantise("g2_1", woven["g2"][:, PACK * HALF :], raw_at(5) + TILE // 2)
-        spare = raw_at(4)
-        finish(2, 0, spare)
-        finish(2, 1, spare + 2 * KIB)
+            multiply(2, kt, "w2", kt * P)
+            multiply(5, kt, "w5", kt * P)
+        quantise("g2_1", woven["g2"][:, PACK * HALF :], raw_at(5) + 4 * KIB, raw_at(6) + KIB)
+        ends = WINDOWS
+        weave_rows(on_v, 9, (9, 0), 0, 2)
+        finish(2, 0, ends)
+        finish(2, 1, ends + 2 * KIB)
         for kt in range(4):
             empty(kt, 0)
-        weave(on_v, "e2", NPASS, 0, (6, 2), 2, 4)
-        finish(3, 0, spare + 4 * KIB)
-        finish(3, 1, spare + 6 * KIB)
+        for kt in (0, 1):
+            weave_rows(on_v, 11, (11, 0), kt, kt + 1)
+        finish(3, 0, ends + 4 * KIB)
+        finish(3, 1, ends + 6 * KIB)
+        finish(2, 2, raw_at(11))
+        finish(2, 3, raw_at(11) + 2 * KIB)
         empty(0, 1)
         empty(1, 1)
-        for i in (7, 8):
-            weave(on_v, "e2", NPASS, i - 6, (i, 2), 2, 4)
-        weave(on_v, "e3", NPASS, 0, (9, 2), 2, 3)
-        gather_first(0, 0, T, raw_place[6, 0])
-        gather_first(1, 0, T, raw_place[6, 0] + 2 * KIB)
-        finish(2, 2, raw_place[7, 0])
-        weave(on_v, "e3", NPASS, 1, (10, 2), 2, 3)
-        finish(2, 3, raw_place[7, 0] + 2 * KIB)
-        weave(on_v, "e3", NPASS, 2, (11, 2), 2, 3)
-        for i in (9, 10):
-            weave(on_s, "e3", NPASS, i - 9, (i, 3), 3, 4)
-        finish(3, 2, raw_place[8, 0])
-        gather_second_and_store(0, 0, T, raw_place[11, 2])
-        weave(on_v, "e3", NPASS, 2, (11, 3), 3, 4)
-        finish(3, 3, raw_place[8, 0] + 2 * KIB)
-        gather_second_and_store(1, 0, T, raw_place[11, 3] - KIB)
+        gather_first(0, 0, T, raw_at(2))
+        gather_first(1, 0, T, raw_at(2) + 2 * KIB)
+        weave_rows(on_v, 9, (9, 2), 2, 4)
+        for kt in (2, 3):
+            weave_rows(on_v, 10, (10, 2), kt, kt + 1)
+        finish(3, 2, ends + 8 * KIB, 0, 2)
+        finish(3, 3, ends + 10 * KIB, 0, 2)
+        for kt in (2, 3):
+            weave_rows(on_v, 11, (11, 2), kt, kt + 1)
+        finish(3, 2, ends + 12 * KIB, 2, 3)
+        finish(3, 3, ends + 13 * KIB, 2, 3)
+        gather_second_and_store(0, 0, T, raw_at(11) + TILE // 2)
         empty(2, 1)
-        gather_first(2, 0, T, raw_place[9, 0])
         empty(3, 1)
-        gather_second_and_store(2, 0, T, PICKED + 2 * TILE)
-        for lo, hi in ((0, T // 2), (T // 2, T)):
-            gather_first(3, lo, hi, raw_place[10, 0])
-            gather_second_and_store(3, lo, hi, raw_place[10, 0] + 2 * KIB)
+        gather_second_and_store(1, 0, T, raw_at(11) + TILE // 2 + 2 * KIB)
+        gather_first(2, 0, T, raw_at(2) + 4 * KIB)
+        gather_second_and_store(2, 0, T, raw_at(7))
+        gather_first(3, 0, T, raw_at(2) + 6 * KIB)
+        second = place("second", [P, LAST_CUT], F32, raw_at(10))
+        nc.scalar.activation(second[:], dx[3][:].indirect(entries(pos2_sb, 0, LAST_CUT)), COPY)
+        total = place("total3", [P, T - LAST_CUT], F32, raw_at(7) + 2 * KIB)
+        nc.vector.tensor_tensor(total[:], dx[3][:].indirect(entries(pos2_sb, LAST_CUT, T)), first[3, 0][:, LAST_CUT:T], ADD)
+        nc.sync.dma_start(out[3 * P : 4 * P, LAST_CUT:T], total[:])
+        rest = place("rest", [P, LAST_CUT], F32, raw_at(7) + 4 * KIB)
+        nc.vector.tensor_tensor(rest[:], second[:], first[3, 0][:, 0:LAST_CUT], ADD)
+        nc.sync.dma_start(out[3 * P : 4 * P, 0:LAST_CUT], rest[:])

@@ -15,6 +15,9 @@ PER_COL = 16
 TAIL = 8
 LAST_CUT = T // 2
 
+SHARE = 400
+HELP = 384
+
 KIB = 1024
 TILE = 8 * KIB
 NARROW = 33 * 64
@@ -209,8 +212,8 @@ def tile_moe_bdx_lin_none_kernel(tc, dyT, w, gate, offs, pos1, pos2, out):
         load_window(2, 3)
         for i in range(5, 9):
             load(i, 0, 4, raw_at(i))
-        load(9, 0, 2, raw_at(9))
-        load(10, 0, 2, WIDE, pitch=S)
+        load(9, 0, 2, WIDE, pitch=S)
+        load(10, 0, 2, raw_at(10))
         load(11, 0, 2, raw_at(11))
         nc.sync.dma_start(pos1_sb[:], pos1)
         for i in range(9, 12):
@@ -240,8 +243,8 @@ def tile_moe_bdx_lin_none_kernel(tc, dyT, w, gate, offs, pos1, pos2, out):
         weave_gated(0, 0)
         picked[2] = place("picked2", [P, PACK, S], F32, PICKED + 2 * TILE)[:]
         for r in range(PACK - 1):
-            gather(False, 2, r, 0, S)
-        gather(False, 2, PACK - 1, C, HALF)
+            gather(False, 2, r, HELP if r == 1 else 0, S)
+        gather(False, 2, PACK - 1, 0, HALF)
         gather(False, 2, PACK - 1, HALF, S)
         weave(on_v, "w01", K + FRONT, (1, 0), FRONT, K)
         quantise("g0", woven["g0"], CODES)
@@ -250,23 +253,23 @@ def tile_moe_bdx_lin_none_kernel(tc, dyT, w, gate, offs, pos1, pos2, out):
         multiply_all(0, "w01", 0)
 
         new_woven("g1", S, raw_at(1) + TILE // 2)
-        new_woven("w34", 2 * K, RING)
+        new_woven("w34", 2 * K, WOVEN)
         weave_gated(1, 0)
         weave(on_g, "w34", 0, (3, 0), 0, K)
-        weave(on_g, "w34", K, (4, 0), 0, FRONT)
+        weave(on_g, "w34", K, (4, 0), 0, SHARE)
         weave_gated(1, 1)
+        gather(True, 2, 1, 0, HELP)
+        weave(on_v, "w34", K + SHARE, (4, 0), SHARE, K)
         quantise("w2", woven["w2"], raw_at(3) + 5 * KIB)
-        quantise("g1", woven["g1"], raw_at(3))
-        weave(on_v, "w34", K + FRONT, (4, 0), FRONT, K)
-        gather(True, 2, PACK - 1, 0, C)
+        quantise("g1", woven["g1"], raw_at(3), raw_at(4))
         multiply_all(1, "w01", K)
         quantise("w34", woven["w34"], CODES + 10 * KIB)
         multiply_all(3, "w34", 0)
         multiply_all(4, "w34", K)
 
-        new_woven("g2", S, raw_at(4))
-        new_woven("w5", K, RING - 3 * KIB)
-        new_woven("e2", NPASS * K, RING + KIB)
+        new_woven("g2", S, raw_at(1))
+        new_woven("w5", K, raw_at(2))
+        new_woven("e2", NPASS * K, WOVEN + 4 * KIB)
         new_woven("e3", NPASS * K, PICKED)
         weave_gated(2, 0)
         weave(on_g, "w5", 0, (5, 0), 0, K)
@@ -274,7 +277,7 @@ def tile_moe_bdx_lin_none_kernel(tc, dyT, w, gate, offs, pos1, pos2, out):
         weave_rows(on_s, 6, (6, 0), 2, 4)
         weave_rows(on_s, 7, (7, 0), 0, 4)
         weave_rows(on_s, 8, (8, 0), 0, 4)
-        weave_rows(on_s, 10, (10, 0), 0, 2)
+        weave_rows(on_s, 9, (9, 0), 0, 2)
         weave_gated(2, 1)
         quantise("w5", woven["w5"], raw_at(5), raw_at(6))
         quantise("g2_0", woven["g2"][:, 0 : PACK * HALF], raw_at(5) + 2 * KIB, raw_at(6) + 512)
@@ -283,9 +286,9 @@ def tile_moe_bdx_lin_none_kernel(tc, dyT, w, gate, offs, pos1, pos2, out):
             multiply(5, kt, "w5", kt * P)
         quantise("g2_1", woven["g2"][:, PACK * HALF :], raw_at(5) + 4 * KIB, raw_at(6) + KIB)
         ends = WINDOWS
-        weave_rows(on_v, 9, (9, 0), 0, 2)
         finish(2, 0, ends)
         finish(2, 1, ends + 2 * KIB)
+        weave_rows(on_v, 10, (10, 0), 0, 2)
         for kt in range(4):
             empty(kt, 0)
         for kt in (0, 1):
@@ -298,15 +301,12 @@ def tile_moe_bdx_lin_none_kernel(tc, dyT, w, gate, offs, pos1, pos2, out):
         empty(1, 1)
         gather_first(0, 0, T, raw_at(2))
         gather_first(1, 0, T, raw_at(2) + 2 * KIB)
-        weave_rows(on_v, 9, (9, 2), 2, 4)
-        for kt in (2, 3):
-            weave_rows(on_v, 10, (10, 2), kt, kt + 1)
-        finish(3, 2, ends + 8 * KIB, 0, 2)
-        finish(3, 3, ends + 10 * KIB, 0, 2)
+        for i in (9, 10):
+            weave_rows(on_v, i, (i, 2), 2, 4)
         for kt in (2, 3):
             weave_rows(on_v, 11, (11, 2), kt, kt + 1)
-        finish(3, 2, ends + 12 * KIB, 2, 3)
-        finish(3, 3, ends + 13 * KIB, 2, 3)
+        finish(3, 2, ends + 8 * KIB)
+        finish(3, 3, ends + 10 * KIB)
         gather_second_and_store(0, 0, T, raw_at(11) + TILE // 2)
         empty(2, 1)
         empty(3, 1)

@@ -210,13 +210,14 @@ def tile_moe_bdx_lin_none_kernel(tc, dyT, w, gate, offs, pos1, pos2, out):
         load(4, 0, 4, raw_at(4))
         load_window(2, 2)
         load_window(2, 3)
-        for i in range(5, 9):
+        for i in range(5, 8):
             load(i, 0, 4, raw_at(i))
-        load(9, 0, 2, WIDE, pitch=S)
-        load(10, 0, 2, raw_at(10))
+        load(8, 0, 2, raw_at(8))
+        load(9, 0, 2, raw_at(9))
+        load(10, 0, 2, WIDE, pitch=S)
         load(11, 0, 2, raw_at(11))
         nc.sync.dma_start(pos1_sb[:], pos1)
-        for i in range(9, 12):
+        for i in range(8, 12):
             load(i, 2, 4, raw_at(i) + TILE // 2)
         nc.sync.dma_start(pos2_sb[:], pos2)
 
@@ -276,8 +277,8 @@ def tile_moe_bdx_lin_none_kernel(tc, dyT, w, gate, offs, pos1, pos2, out):
         weave_rows(on_g_rows, 6, (6, 0), 0, 2)
         weave_rows(on_s, 6, (6, 0), 2, 4)
         weave_rows(on_s, 7, (7, 0), 0, 4)
-        weave_rows(on_s, 8, (8, 0), 0, 4)
-        weave_rows(on_s, 9, (9, 0), 0, 2)
+        for i in (8, 9, 10):
+            weave_rows(on_s, i, (i, 0), 0, 2)
         weave_gated(2, 1)
         quantise("w5", woven["w5"], raw_at(5), raw_at(6))
         quantise("g2_0", woven["g2"][:, 0 : PACK * HALF], raw_at(5) + 2 * KIB, raw_at(6) + 512)
@@ -288,25 +289,29 @@ def tile_moe_bdx_lin_none_kernel(tc, dyT, w, gate, offs, pos1, pos2, out):
         ends = WINDOWS
         finish(2, 0, ends)
         finish(2, 1, ends + 2 * KIB)
-        weave_rows(on_v, 10, (10, 0), 0, 2)
         for kt in range(4):
             empty(kt, 0)
         for kt in (0, 1):
             weave_rows(on_v, 11, (11, 0), kt, kt + 1)
         finish(3, 0, ends + 4 * KIB)
         finish(3, 1, ends + 6 * KIB)
+        for kt in (2, 3):
+            weave_rows(on_v, 8, (8, 2), kt, kt + 1)
         finish(2, 2, raw_at(11))
         finish(2, 3, raw_at(11) + 2 * KIB)
         empty(0, 1)
         empty(1, 1)
         gather_first(0, 0, T, raw_at(2))
         gather_first(1, 0, T, raw_at(2) + 2 * KIB)
-        for i in (9, 10):
-            weave_rows(on_v, i, (i, 2), 2, 4)
+        weave_rows(on_v, 9, (9, 2), 2, 4)
+        for kt in (2, 3):
+            weave_rows(on_v, 10, (10, 2), kt, kt + 1)
+        finish(3, 2, ends + 8 * KIB, 0, 2)
+        finish(3, 3, ends + 10 * KIB, 0, 2)
         for kt in (2, 3):
             weave_rows(on_v, 11, (11, 2), kt, kt + 1)
-        finish(3, 2, ends + 8 * KIB)
-        finish(3, 3, ends + 10 * KIB)
+        finish(3, 2, ends + 12 * KIB, 2, 3)
+        finish(3, 3, ends + 13 * KIB, 2, 3)
         gather_second_and_store(0, 0, T, raw_at(11) + TILE // 2)
         empty(2, 1)
         empty(3, 1)

from contextlib import ExitStack

import concourse.mybir as mybir
from concourse.masks import make_identity

K, T, E, C, N = 512, 512, 4, 256, 1536
S = E * C
P = 128
PACK = 4
PASS = P * PACK
NPASS = N // PASS
HALF = S // 2
FRONT = K // 2
PER_COL = 16
TAIL = 8
LAST_CUT = T // 2

SHARE = 400
HELP = 384

KIB = 1024
TILE = 8 * KIB
NARROW = 33 * 64
BROAD = 65 * 64

WINDOWS = 0
RAW = WINDOWS + PACK * NARROW + 2 * PACK * BROAD
WIDE = RAW + 12 * TILE
PICKED = WIDE + 2 * TILE
WOVEN = PICKED + 4 * TILE
RING = WOVEN + TILE + KIB
CODES = RING + 2 * TILE

F32 = mybir.dt.float32
BF16 = mybir.dt.bfloat16
U32 = mybir.dt.uint32
U16 = mybir.dt.uint16
U8 = mybir.dt.uint8
FP8X4 = mybir.dt.float8_e4m3fn_x4
ADD = mybir.AluOpType.add
MULT = mybir.AluOpType.mult
COPY = mybir.ActivationFunctionType.Copy

FLOPS = 2 * K * N * S
BYTES = 4 * (N * T + E * N * K + S + K * T) + 2 * P * (S + 2 * T) // PER_COL


def tile_moe_bdx_lin_none_kernel(tc, dyT, w, gate, offs, pos1, pos2, out):
    nc = tc.nc
    with ExitStack() as ctx:
        held = ctx.enter_context(tc.tile_pool(name="held", bufs=1))
        placed = ctx.enter_context(tc.tile_pool(name="placed", bufs=1))
        psum = ctx.enter_context(tc.psum_pool(name="psum", bufs=1))

        def place(name, shape, dtype, at):
            return placed.tile(shape, dtype, name=name, offset=at, align_bytes=64)

        def window_at(c, r):
            return WINDOWS + (r * NARROW if c == 0 else PACK * NARROW + ((c - 1) * PACK + r) * BROAD)

        def raw_at(i):
            return RAW + i * TILE

        offs_sb = held.tile([P, S // PER_COL], U16, name="offs_sb")
        pos1_sb = held.tile([P, T // PER_COL], U16, name="pos1_sb")
        pos2_sb = held.tile([P, T // PER_COL], U16, name="pos2_sb")
        gate_sb = held.tile([P, 2, PACK], F32, name="gate_sb")
        identity = held.tile([P, P], F32, name="identity")
        make_identity(nc, identity[:])

        windows = {}
        for c in range(NPASS):
            for r in range(PACK):
                width = (HALF if c == 0 else S) + TAIL
                windows[c, r] = place(f"window{c}_{r}", [P, width], F32, window_at(c, r))
                if c == NPASS - 1:
                    nc.gpsimd.memset(windows[c, r][:, T:], 0.0)
                elif (c, r) == (1, PACK - 1):
                    nc.scalar.copy(windows[c, r][:, T:], windows[1, 0][:, T:])
                else:
                    nc.vector.memset(windows[c, r][:, T:], 0.0)

        raw, raw_place = {}, {}
        spread = [psum.tile([P, HALF], F32, name=f"bank{3 - h}_1") for h in range(2)]
        banks = {}

        def load_window(c, r):
            rows = dyT[c * PASS : (c + 1) * PASS, :].rearrange("(p r) t -> p r t", r=PACK)
            nc.sync.dma_start(windows[c, r][:, 0:T], rows[:, r, :])

        def load(i, lo, hi, at, pitch=None):
            e, c = divmod(i, NPASS)
            rows = w[e, c * PASS : (c + 1) * PASS, :].rearrange("(p r) k -> p r k", r=PACK)
            width = (hi - lo) * P
            tile = place(f"raw{i}_{lo}", [P, PACK, pitch or width], F32, at)
            raw[i, lo] = tile[:, :, 0:width]
            raw_place[i, lo] = at
            nc.sync.dma_start(raw[i, lo], rows[:, :, lo * P : hi * P])

        def on_g(dst, src):
            nc.gpsimd.tensor_scalar(dst.rearrange("p x r i -> p x i r"), src.rearrange("p x r i -> p x i r"), 1.0, 0.0, MULT, ADD)

        def on_g_rows(dst, src):
            order = "p t x r i -> p t (x i) r"
            nc.gpsimd.tensor_scalar(dst.rearrange(order), src.rearrange(order), 1.0, 0.0, MULT, ADD)

        on_v, on_s = nc.vector.tensor_copy, nc.scalar.copy
        woven, mx, picked = {}, {}, {}

        def entries(lst, lo, hi):
            return lst[:, lo // PER_COL : hi // PER_COL]

        def new_woven(name, words, at):
            woven[name] = place(f"woven_{name}", [P, PACK * words], BF16, at)[:]

        def weave_gated(c, h):
            dst = woven[f"g{c}"][:, h * PACK * HALF : (h + 1) * PACK * HALF].rearrange("p (x i r) -> p x r i", i=2, r=PACK)
            src = picked[c][:, :, h * HALF : (h + 1) * HALF].rearrange("p r (x i) -> p x r i", i=2)
            weights = spread[h][:].rearrange("p (x i) -> p x i", i=2).unsqueeze(2).to_broadcast([P, HALF // 2, PACK, 2])
            nc.vector.tensor_tensor(dst, src, weights, MULT)

        def weave(copy, name, at, key, lo, hi):
            dst = woven[name][:, PACK * at : PACK * (at + hi - lo)].rearrange("p (x i r) -> p x r i", i=2, r=PACK)
            copy(dst, raw[key][:, :, lo:hi].rearrange("p r (x i) -> p x r i", i=2))

        def weave_rows(copy, i, key, lo, hi):
            dst = woven[f"e{i // NPASS}"].rearrange("p (t u x i r) -> p t u x r i", t=K // P, u=NPASS, i=2, r=PACK)
            src = raw[key][:, :, (lo - key[1]) * P : (hi - key[1]) * P].rearrange("p r (t x i) -> p t x r i", t=hi - lo, i=2)
            copy(dst[:, lo:hi, i % NPASS, :, :, :], src)

        def quantise(name, values, at, scales_at=None):
            words = values.shape[1] // PACK
            codes = place(f"codes_{name}", [P, words], U32, at)
            scales = place(f"scales_{name}", [P, words], U8, at + 4 * words if scales_at is None else scales_at)
            nc.vector.quantize_mx(out=codes[:].bitcast(FP8X4), scales=scales[:], in_=values)
            mx[name] = codes, scales

        def multiply(i, kt, name, lo):
            e, c = divmod(i, NPASS)
            h, u = divmod(e, 2)
            w_codes, w_scales = mx[name]
            if c == NPASS - 1:
                g_codes, g_scales = mx[f"g{c}_{h}"]
                slots = slice(u * C, (u + 1) * C)
            else:
                g_codes, g_scales = mx[f"g{c}"]
                slots = slice(e * C, (e + 1) * C)
            opens = (kt, h) not in banks
            if opens:
                banks[kt, h] = psum.tile([P, HALF], F32, name=f"bank{kt}_{h}")
            nc.tensor.matmul_mx(
                out=banks[kt, h][:, u * C : (u + 1) * C],
                lhsT=w_codes[:, lo : lo + P].bitcast(FP8X4),
                lhsT_scale=w_scales[:, lo : lo + P],
                rhs=g_codes[:, slots].bitcast(FP8X4),
                rhs_scale=g_scales[:, slots],
                start=opens,
                stop=(u == 1 and c == NPASS - 1),
            )

        def multiply_all(i, name, lo):
            for kt in range(K // P):
                multiply(i, kt, name, lo + kt * P)

        def finish(e, kt, at, lo=0, hi=NPASS):
            name = f"e{e}_{kt}_{lo}"
            quantise(name, woven[f"e{e}"][:, (kt * NPASS + lo) * PASS : (kt * NPASS + hi) * PASS], at)
            for u in range(lo, hi):
                multiply(e * NPASS + u, kt, name, (u - lo) * P)

        dx, first = {}, {}

        def empty(kt, h, copy=nc.scalar.copy):
            if h == 0:
                dx[kt] = place(f"dx{kt}", [P, S], F32, WIDE + kt * TILE // 2)
            copy(dx[kt][:, h * HALF : (h + 1) * HALF], banks[kt, h][:])

        def gather_first(kt, lo, hi, at):
            first[kt, lo] = place(f"first{kt}_{lo}", [P, hi - lo], F32, at + 4 * lo)
            nc.scalar.activation(first[kt, lo][:], dx[kt][:].indirect(entries(pos1_sb, lo, hi)), COPY)

        def gather_second_and_store(kt, lo, hi, at):
            total = place(f"total{kt}_{lo}", [P, hi - lo], F32, at + 4 * lo)
            nc.vector.tensor_tensor(total[:], dx[kt][:].indirect(entries(pos2_sb, lo, hi)), first[kt, lo][:], ADD)
            nc.sync.dma_start(out[kt * P : (kt + 1) * P, lo:hi], total[:])

        def gather(on_vector, c, r, lo, hi):
            src = windows[c, r][:].indirect(entries(offs_sb, lo, hi))
            if on_vector:
                nc.vector.tensor_copy(picked[c][:, r, lo:hi], src)
            else:
                nc.scalar.activation(picked[c][:, r, lo:hi], src, COPY)

        load_window(0, 0)
        nc.sync.dma_start(offs_sb[:], offs)
        load_window(0, 1)
        nc.sync.dma_start(gate_sb[:], gate[0, :].rearrange("(h p j) -> p h j", h=2, j=PACK))
        load_window(0, 2)
        load_window(0, 3)
        load_window(1, 0)
        load(0, 0, 4, raw_at(0))
        load_window(1, 1)
        load(1, 0, 4, raw_at(1))
        load_window(1, 2)
        load_window(1, 3)
        load(2, 0, 4, raw_at(2))
        load_window(2, 0)
        load(3, 0, 4, raw_at(3))
        load_window(2, 1)
        load(4, 0, 4, raw_at(4))
        load_window(2, 2)
        load_window(2, 3)
        for i in range(5, 8):
            load(i, 0, 4, raw_at(i))
        load(8, 0, 2, raw_at(8))
        load(9, 0, 2, raw_at(9))
        load(10, 0, 2, WIDE, pitch=S)
        load(11, 0, 2, raw_at(11))
        nc.sync.dma_start(pos1_sb[:], pos1)
        for i in range(8, 12):
            load(i, 2, 4, raw_at(i) + TILE // 2)
        nc.sync.dma_start(pos2_sb[:], pos2)

        for h in range(2):
            for j in range(PACK):
                nc.tensor.transpose(spread[h][:, j::PACK], gate_sb[:, h, j : j + 1].to_broadcast([P, P]), identity[:])

        picked[0] = place("picked0", [P, PACK, S], F32, PICKED + 2 * TILE)[:]
        picked[1] = place("picked1", [P, PACK, S], F32, PICKED)[:]
        for r in range(PACK):
            gather(True, 0, r, 0, HALF)
            gather(False, 0, r, HALF, S)
        for r in range(PACK - 1):
            gather(False, 1, r, 0, S)
        gather(False, 1, PACK - 1, 0, HALF)
        gather(False, 1, PACK - 1, HALF, S)

        new_woven("g0", S, WOVEN)
        new_woven("w01", 2 * K, RING)
        new_woven("w2", K, RING + TILE)
        weave_gated(0, 1)
        weave(on_g, "w01", 0, (0, 0), 0, K)
        weave(on_g, "w01", K, (1, 0), 0, FRONT)
        weave_gated(0, 0)
        picked[2] = place("picked2", [P, PACK, S], F32, PICKED + 2 * TILE)[:]
        for r in range(PACK - 1):
            gather(False, 2, r, HELP if r == 1 else 0, S)
        gather(False, 2, PACK - 1, 0, HALF)
        gather(False, 2, PACK - 1, HALF, S)
        weave(on_v, "w01", K + FRONT, (1, 0), FRONT, K)
        quantise("g0", woven["g0"], CODES)
        weave(on_v, "w2", 0, (2, 0), 0, K)
        quantise("w01", woven["w01"], CODES + 5 * KIB)
        multiply_all(0, "w01", 0)

        new_woven("g1", S, raw_at(1) + TILE // 2)
        new_woven("w34", 2 * K, WOVEN)
        weave_gated(1, 0)
        weave(on_g, "w34", 0, (3, 0), 0, K)
        weave(on_g, "w34", K, (4, 0), 0, SHARE)
        weave_gated(1, 1)
        gather(True, 2, 1, 0, HELP)
        weave(on_v, "w34", K + SHARE, (4, 0), SHARE, K)
        quantise("w2", woven["w2"], raw_at(3) + 5 * KIB)
        quantise("g1", woven["g1"], raw_at(3), raw_at(4))
        multiply_all(1, "w01", K)
        quantise("w34", woven["w34"], CODES + 10 * KIB)
        multiply_all(3, "w34", 0)
        multiply_all(4, "w34", K)

        new_woven("g2", S, raw_at(1))
        new_woven("w5", K, raw_at(2))
        new_woven("e2", NPASS * K, WOVEN + 4 * KIB)
        new_woven("e3", NPASS * K, PICKED)
        weave_gated(2, 0)
        weave(on_g, "w5", 0, (5, 0), 0, K)
        weave_rows(on_g_rows, 6, (6, 0), 0, 2)
        weave_rows(on_s, 6, (6, 0), 2, 4)
        weave_rows(on_s, 7, (7, 0), 0, 4)
        for i in (8, 9, 10):
            weave_rows(on_s, i, (i, 0), 0, 2)
        weave_gated(2, 1)
        quantise("w5", woven["w5"], raw_at(5), raw_at(6))
        quantise("g2_0", woven["g2"][:, 0 : PACK * HALF], raw_at(5) + 2 * KIB, raw_at(6) + 512)
        for kt in range(4):
            multiply(2, kt, "w2", kt * P)
            multiply(5, kt, "w5", kt * P)
        quantise("g2_1", woven["g2"][:, PACK * HALF :], raw_at(5) + 4 * KIB, raw_at(6) + KIB)
        ends = WINDOWS
        finish(2, 0, ends)
        finish(2, 1, ends + 2 * KIB)
        for kt in range(4):
            empty(kt, 0)
        for kt in (0, 1):
            weave_rows(on_v, 11, (11, 0), kt, kt + 1)
        finish(3, 0, ends + 4 * KIB)
        finish(3, 1, ends + 6 * KIB)
        for kt in (2, 3):
            weave_rows(on_v, 8, (8, 2), kt, kt + 1)
        finish(2, 2, raw_at(11))
        finish(2, 3, raw_at(11) + 2 * KIB)
        empty(0, 1)
        empty(1, 1)
        gather_first(0, 0, T, raw_at(2))
        gather_first(1, 0, T, raw_at(2) + 2 * KIB)
        weave_rows(on_v, 9, (9, 2), 2, 4)
        for kt in (2, 3):
            weave_rows(on_v, 10, (10, 2), kt, kt + 1)
        finish(3, 2, ends + 8 * KIB, 0, 2)
        finish(3, 3, ends + 10 * KIB, 0, 2)
        for kt in (2, 3):
            weave_rows(on_v, 11, (11, 2), kt, kt + 1)
        finish(3, 2, ends + 12 * KIB, 2, 3)
        finish(3, 3, ends + 13 * KIB, 2, 3)
        gather_second_and_store(0, 0, T, raw_at(11) + TILE // 2)
        empty(2, 1)
        empty(3, 1)
        gather_second_and_store(1, 0, T, raw_at(11) + TILE // 2 + 2 * KIB)
        gather_first(2, 0, T, raw_at(2) + 4 * KIB)
        gather_second_and_store(2, 0, T, raw_at(7))
        gather_first(3, 0, T, raw_at(2) + 6 * KIB)
        second = place("second", [P, LAST_CUT], F32, raw_at(10))
        nc.scalar.activation(second[:], dx[3][:].indirect(entries(pos2_sb, 0, LAST_CUT)), COPY)
        total = place("total3", [P, T - LAST_CUT], F32, raw_at(7) + 2 * KIB)
        nc.vector.tensor_tensor(total[:], dx[3][:].indirect(entries(pos2_sb, LAST_CUT, T)), first[3, 0][:, LAST_CUT:T], ADD)
        nc.sync.dma_start(out[3 * P : 4 * P, LAST_CUT:T], total[:])
        rest = place("rest", [P, LAST_CUT], F32, raw_at(7) + 4 * KIB)
        nc.vector.tensor_tensor(rest[:], second[:], first[3, 0][:, 0:LAST_CUT], ADD)
        nc.sync.dma_start(out[3 * P : 4 * P, 0:LAST_CUT], rest[:])
